import numpy as np, ml_dtypes
CORES = [16,18,20,22]
N = 4
import mx_ref
BF = ml_dtypes.bfloat16
def gcols(t, e):
    v = np.concatenate([t.reshape(8, 16, -1, 4), np.zeros((8, 16, 1, 4), BF)], axis=2)
    return np.ascontiguousarray(np.stack([v[g][:, e[g]] for g in range(8)])).reshape(128, -1)
def tile(rs):
    return np.stack(rs, axis=2).reshape(128, -1).astype(BF)
def cut(t, i, w=512):
    return t[:, w * i:w * i + w]
def pick(q, e):
    c = np.concatenate([q[0].reshape(128, -1, 4), np.zeros((128, 1, 4), np.uint8)], axis=1); s = np.concatenate([q[1], np.ones((16, 1), np.uint8)], axis=1)
    return (np.ascontiguousarray(c[:, e].reshape(128, -1)), np.ascontiguousarray(s[:, e]))
def join(*qs):
    return (np.concatenate([q[0] for q in qs], axis=1), np.concatenate([q[1] for q in qs], axis=1))
def put(q, e, v):
    c, s = q[0].reshape(128, -1, 4).copy(), q[1].copy(); c[:, e] = v[0].reshape(128, -1, 4); s[:, e] = v[1]
    return (c.reshape(128, -1), s)
def pk(c, s):
    return (np.ascontiguousarray(c), mx_ref.live(s))
def emit(q):
    return q[0], q[1]
def packed(v, rng):
    q = [mx_ref.quantize(np.ascontiguousarray(v[r])) for r in range(N)]
    return np.stack([a for a, b in q]), np.stack([mx_ref.plane(b, rng) for a, b in q])
def values_of_codes():
    e, c = np.zeros((128, 128, 4), np.float32), np.zeros((128, 2, 4), np.uint8)
    e[np.arange(128), np.arange(128), 0] = 1
    c[:127, :, 0] = np.arange(256).reshape(2, 128).T[:127]
    return mx_ref.matmul(mx_ref.quantize(e.reshape(128, 512).astype(BF)), (c.reshape(128, 8), np.full((16, 2), 127, np.uint8))).T.reshape(-1).astype(np.float64)
CODE_VALUE, SCALE_VALUE = values_of_codes(), 2.0 ** (np.arange(256) - 127.0)
def decode(q):
    return (CODE_VALUE[q[0]].reshape(16, 8, -1, 4) * SCALE_VALUE[q[1]][:, None, :, None] + 0.0).reshape(128, -1).astype(np.float32)
def f(rng, *shape):
    return mx_ref.flush((rng.standard_normal(shape, dtype=np.float32) * np.exp2(rng.integers(-2, 3, shape[:-1] + (1,)))).astype(BF))
def wide(rng, *shape, cols=0):
    v = rng.standard_normal(shape, dtype=np.float32) * np.exp2(rng.integers(-12, 13, shape)).astype(np.float32)
    if cols: v *= np.repeat(np.exp2(rng.integers(-cols, cols + 1, shape[:-2] + (1, shape[-1] // 4))) * (rng.random(shape[:-2] + (1, shape[-1] // 4)) > 0.0625), 4, axis=-1).astype(np.float32)
    return mx_ref.flush(v.astype(BF))
C, A, R = 320, 96, 3
STEP = [1, 2, 1]
def parse(b, a):
    word = 64 * b[:, :-3] + 16 * b[:, 1:-2] + 4 * b[:, 2:-1] + b[:, 3:]
    block = 64 * a[:, ::4] + 16 * a[:, 1::4] + 4 * a[:, 2::4] + a[:, 3::4]
    first = np.full((8, 256), -1)
    for m in range(C // 4 - 1, -1, -1): first[np.arange(8), block[:, m]] = m
    found = np.concatenate([np.take_along_axis(first, word, axis=1), np.full((8, 3), -1)], axis=1)
    h = np.zeros((8, C), np.int64)
    go, shift, lits = np.zeros(8, np.int64), np.zeros(8, np.int64), np.zeros(8, np.int64)
    for c in range(C):
        run = (go == c) & (found[:, c] >= 0)
        lit = (go == c) & (found[:, c] < 0)
        shift = np.where(run, 4 * found[:, c] - c, shift)
        h[:, c] = np.where(lit, np.where(lits < A, C + c, c), c + shift)
        lits = lits + lit
        go = np.where(run, c + 4, np.where(lit, c + 1, go))
    return h
def numbers_of(rng):
    return {"x": np.array(f(rng, N, 128, 4 * C)), "u": np.array(f(rng, N, 128, 512)), "v": np.array(f(rng, N, 128, 512))}
def weights(rng, still=[]):
    w = np.array(f(rng, N, 128, 2048)).reshape(N, 8, 16, 4, 8, 16, 4)
    for i in still:
        w[:, :, i] = 0
        w[:, :, :, :, :, i] = 0
    c, p = packed(w.reshape(N, 128, 2048), rng)
    return {"wc": c, "ws": p}
def signs(rng):
    return np.stack([rng.permutation(8) % 2 * 2.0 - 1.0 for r in range(N)])
def planted(rng, z, size, k):
    d = numbers_of(rng)
    x = d["x"].astype(np.float32).reshape(N, 8, 16, C, 4)
    x[:, :, :8] = 0
    for i, b in enumerate((z // 2, z % 2)): x[:, :, i, :, 0] = np.where(b > 0, 1, -rng.integers(0, 2, z.shape)) * size
    u = d["u"].reshape(N, 128, 128, 4)
    for h in range(0, 128, 16):
        u[:, :, h:h + 2] = 0
        for i in range(2): u[:, h + i, h + i, 0] = k
    return {"x": x.reshape(N, 128, 4 * C).astype(BF), "u": u.reshape(N, 128, 512), "v": d["v"], **weights(rng, range(8))}
def setup_inputs(rng):
    return {**numbers_of(rng), **weights(rng)}
def setup_inputs_ties(rng):
    per = rng.permutation([1, 2, 3, 4, 5, 8, 12, 16])
    s = rng.integers(0, 240, (N, 8))
    z = np.zeros((N, 8, C), np.int64)
    for g in range(8):
        pat = rng.integers(0, 4, per[g])
        if per[g] == 1: pat[:] = rng.integers(1, 4)
        if per[g] == 4:
            pat = rng.permutation(4)
            s[1::2, g] = s[::2, g] + rng.integers(1, 4, N // 2)
        z[:, g] = pat[(s[:, g, None] + np.arange(C)) % per[g]]
        if per[g] in (1, 3):
            other = int(rng.choice(np.setdiff1d(np.arange(4), pat)))
            for r in range(0, N, 2): z[r, g, :int(rng.integers(1, 4))] = other
    d = planted(rng, z, 1.0, np.ones(N, np.float32).astype(BF))
    d["x"][rng.integers(N)] = 0
    return d
def setup_inputs_near(rng):
    low = rng.permutation(N) < N // 2
    size = np.exp2(np.where(low[:, None, None], -30.0, rng.integers(-30, 31, (N, 8, C))))
    d = planted(rng, rng.integers(0, 4, (N, 8, C)), size, np.where(low, 2.0 ** -30, 1.0).astype(np.float32).astype(BF))
    x, u = d["x"].reshape(N, 8, 16, C, 4), d["u"].reshape(N, 128, 128, 4)
    for r in range(N):
        if low[r]:
            k = x[r, :, :2, :, 0].astype(np.float32)
            least = (k > 0) & (rng.integers(0, 2, k.shape) > 0)
            x[r, :, :2, :, 0] = np.where(least, 2.25 * 2.0 ** -30, k).astype(np.float32).astype(BF)
            x[r, :, 2:4, :, 0] = np.where(least, -1.625 * 2.0 ** -30, 0.0).astype(np.float32).astype(BF)
            for h in range(0, 128, 16):
                for i in range(2): u[r, h + 2 + i, h + i, 0] = 1.375 * 2.0 ** -30
    return {"x": x.reshape(N, 128, 4 * C), "u": u.reshape(N, 128, 512), "v": d["v"], "wc": d["wc"], "ws": d["ws"]}
def setup_inputs_caps(rng):
    words = (rng.permutation(16)[:8, None] >> np.arange(4)) & 1
    late = rng.permutation(N // 2) % 2
    z = np.zeros((N, 8, C), np.int64)
    for r in range(N):
        if r % 2 == 0: h = int(rng.integers(8))
        n = np.insert(rng.permutation([0, 4, A - 4, A, A + 4, 2 * A, C - 32]), h, C)
        own = 2 + r % 2
        for g in range(8):
            if g == h:
                z[r, g] = own
                if late[r // 2]: z[r, g, r % 2 * (C - 4) + np.arange(4)] = words[0]
                continue
            k = rng.permutation(np.concatenate([np.full(n[g], -1), rng.integers(0, 8, (C - 32 - n[g]) // 4)]))
            mixed = np.concatenate([words[i] if i >= 0 else [own] for i in k])
            blocks = words[rng.permutation(8)].reshape(-1)
            z[r, g] = np.concatenate([mixed, blocks] if rng.integers(2) else [blocks, mixed])
    return planted(rng, z, 1.0, np.ones(N, np.float32).astype(BF))
def setup_inputs_huge(rng):
    d = numbers_of(rng)
    x = 2.0 ** 30 * (0.8 + 0.2 * rng.random((N, 128, C, 4)))
    for r in range(N): x[r][:, rng.permutation(C)[:C // 4 + 1]] = 2.0 ** 30
    c = np.ones((N, C))
    half = int(rng.integers(2))
    for r in range(N):
        if 2 * r // N == half: c[r] = rng.permutation(C) % 2 * 2.0 - 1.0
    x *= c[:, None, :, None]
    u = d["u"].reshape(N, 128, 8, 16, 4)
    h = int(rng.integers(8))
    s = np.stack([signs(rng), signs(rng)], axis=2)
    s = s * s[:, h:h + 1]
    a = 2.0 ** 30 * (1 - 0.1 * rng.random((N, 128, 8, 2, 4))) * s[:, None, :, :, None]
    a[:, :, h] = 2.0 ** 30
    u[:, :, :, :2] = a.astype(np.float32).astype(BF)
    w = np.zeros((N, 128, 4, 128, 4), np.float32)
    i = np.arange(128)
    for b in range(4): w[:, i, b, i, b] = -1
    wc, ws = packed(w.reshape(N, 128, 2048).astype(BF), rng)
    return {"x": x.astype(np.float32).reshape(N, 128, 4 * C).astype(BF), "u": u.reshape(N, 128, 512), "v": d["v"], "wc": wc, "ws": ws}
def setup_inputs_spread(rng):
    d = setup_inputs(rng)
    d["x"] = wide(rng, N, 128, 4 * C, cols=6)
    return d
def check_inputs(d):
    b = []
    for k in ("x", "u", "v"):
        a = np.abs(d[k].astype(np.float32))
        if not (np.isfinite(a).all() and ((a == 0) | (a >= 2.0 ** -30) & (a <= 2.0 ** 30)).all()): b.append("a value of " + k)
    if ((d["wc"] & 0x7F) == 0x7F).any(): b.append("a code of wc that is no number")
    z = np.zeros((128, 4, 4), np.float32)
    z[:, 1] = 2.0 ** -30
    z[:, 2] = 2.0 ** 30
    c, s = emit(mx_ref.quantize(z.reshape(128, 16).astype(BF)))
    for r in range(N):
        p = mx_ref.live(d["ws"][r])
        if not ((p == s[0, 0]) | (p >= s[0, 1]) & (p <= s[0, 2])).all(): b.append("a scale of ws")
    return b
def reference(x, u, v, wc, ws):
    qu = [mx_ref.quantize(u[r]) for r in range(N)]
    lay = [pk(wc[r], ws[r]) for r in range(N)]
    now = [x[r] for r in range(N)]
    for t in range(R):
        sent, z = [], []
        for r in range(N):
            q = mx_ref.quantize(now[r])
            p = mx_ref.matmul(qu[r], q)
            sent.append(q)
            z.append(2 * (p[::16] > 0).astype(np.int64) + (p[1::16] > 0))
        came = decode(join(*sent)).astype(BF)
        made, lists = [], []
        for r in range(N):
            e = r ^ STEP[t]
            h = parse(z[e], z[r])
            c = gcols(np.concatenate([now[r], cut(came, e, 4 * C)], axis=1), h)
            q = mx_ref.quantize(c)
            made.append(tile([mx_ref.matmul(pick(lay[r], np.arange(128 * b, 128 * b + 128)), q) * np.float32(0.015625) + c[:, b::4].astype(np.float32) for b in range(4)]))
            lists.append(h)
        now = made
    y, ot = np.zeros((N, 128, C), np.float32), np.zeros((N, 8, C), np.float32)
    oc, osc = np.zeros((N, 128, 4 * C), np.uint8), np.zeros((N, 16, C), np.uint8)
    for r in range(N):
        q = mx_ref.quantize(now[r])
        y[r] = mx_ref.matmul(mx_ref.quantize(v[r]), q)
        ot[r] = lists[r]
        oc[r], osc[r] = emit(q)
    return {"y": y, "ot": ot, "oc": oc, "osc": osc}

@@ -1,0 +1,360 @@
+from concourse.mybir import dt, AluOpType as A, ActivationFunctionType as F
+
+C, CAP, ROUNDS, STEP = 320, 96, 3, [1, 2, 1]
+HC = C // 2
+TAB, WIN = 344, 664
+BASE = 14212656.0
+A0 = 0.75 + 9 * 2.0 ** -24
+B0 = (11184811 - 9) * 2.0 ** -23
+B1 = 1.0 - 2.0 ** -24
+X4, U8, U16, I32, F32, BF, H16 = "float8_e4m3fn_x4", "uint8", "uint16", "int32", "float32", "bfloat16", "float16"
+
+
+def _scratch():
+    s = {}
+    for t in range(ROUNDS + 1):
+        for n, w, d in [("win", 12 * C if t < ROUNDS else 4 * C, BF), ("qx", C, X4), ("sx", C, U8)]:
+            s["%s%d" % (n, t)] = ("sbuf", [128, w], d)
+    for t in range(ROUNDS):
+        for n, w, d in [("lq", C, X4), ("lsc", C, U8), ("wd", 20, U16), ("lw", 20, U16), ("tb", WIN, F32), ("tm", WIN, F32),
+                        ("gt", 4 * C, BF), ("qg", C, X4), ("sg", C, U8)]:
+            s["%s%d" % (n, t)] = ("sbuf", [128, w], d)
+    for d, names in [
+        (BF, "ut 512 vt 512 ones 516 z0 516 z1 516 dw 672 db 640 dsel 320 dd 400 bits 648 eqm 400 dscan 400 x1 20 g64 1280 rr 1280"),
+        (X4, "uq 128 up 256 vq 128 wq 512 eq 512"), (U8, "usc 128 ups 256 vsc 128 wsc 512 esc 512"),
+        (I32, "i_u 16 i_e 16 i_p 22 e16 16 j22 22"), (U16, "uo 16 jo 22 ofu 8 ix 20 gl 80 ho 20"),
+        (H16, "wscan 648 bscan 640 t2 320 tsel 320"),
+        (F32, "k16 20 k64 8 src_m 80 src_b 80 jf 4 j4 4 kp 4 bk 4 tiny 4 pa 16 pb 16 pc 16 pd 16 pw 16 pe 16 pf 16 pt 16 m0 16 sl 8 "
+              "cf 20 cb 20 ck 20 hv 960 vv 20 wsel 80 wk 8 of 8 al 320 be 320 tf 320 st 324 ssel 320 ll 20 y2 20 ik 20 sh 20 lv 20 "
+              "ha 20 hh 20 hf 320 yo 320"),
+    ]:
+        w = names.split()
+        for i in range(0, len(w), 2):
+            s[w[i]] = ("sbuf", [128, int(w[i + 1])], d)
+    s["ps"] = ("psum", [128, 4096], F32)
+    return s
+
+
+SCRATCH = _scratch()
+POOL = ["s%d" % i for i in range(120)]
+SEMAPHORES = POOL + ["sent"] + ["a%s%d" % (k, t) for k in "cw" for t in range(ROUNDS)]
+
+
+def _sequencer(g, T):
+    Q = {"g": g, "v": g.vector, "a": g.scalar, "p": g.tensor, "s": g.sync}
+    know = {q: {} for q in Q}
+    count, waited, writer, readers = {}, {}, {}, {}
+
+    def wait(q, tok):
+        sem, val, clock = tok
+        if know[q].get(sem, 0) >= val:
+            return
+        Q[q].wait_ge(T.sem[sem], val)
+        waited[sem] = max(waited.get(sem, 0), val)
+        for k, x in list(clock.items()) + [(sem, val)]:
+            if know[q].get(k, 0) < x:
+                know[q][k] = x
+
+    def need(q, r, w):
+        deps = [writer[k] for k in r + w if k in writer]
+        for k in w:
+            deps += readers.get(k, [])
+        for tok in sorted(deps, key=lambda x: -sum(x[2].values())):
+            wait(q, tok)
+
+    def op(q, fn, r=(), w=(), n=1):
+        r, w = list(r), list(w)
+        need(q, r, w)
+        sem = [s for s in POOL if know[q].get(s, 0) == count.get(s, 0)][0]
+        fn(Q[q]).then_inc(T.sem[sem], n)
+        count[sem] = count.get(sem, 0) + n
+        tok = (sem, count[sem], dict(know[q]))
+        for k in r:
+            readers.setdefault(k, []).append(tok)
+        for k in w:
+            writer[k], readers[k] = tok, []
+        return tok
+
+    def arrives(key, sem, val):
+        writer[key] = (sem, val, {})
+
+    def finish(q):
+        for s in POOL:
+            if count.get(s, 0) > waited.get(s, 0):
+                wait(q, (s, count[s], {}))
+    return op, need, arrives, finish
+
+
+def rank_program(g, core, T, topo):
+    rank = T.rank_of(core)
+    if rank is None:
+        return
+    op, need, arrives, finish = _sequencer(g, T)
+    u8, u32 = dt.uint8, dt.uint32
+
+    def ts(out, in0, s1, s2, o0, o1, r, w):
+        if o1 is None:
+            return op("v", lambda e: e.tensor_scalar(out, in0, s1, None, o0), r, w)
+        return op("v", lambda e: e.tensor_scalar(out, in0, s1, s2, o0, o1), r, w)
+
+    def tt(out, a, b, o, r, w):
+        return op("v", lambda e: e.tensor_tensor(out, a, b, o), r, w)
+
+    def cp(out, a, r, w):
+        return op("v", lambda e: e.tensor_copy(out, a), r, w)
+
+    def ms(out, c, w):
+        return op("v", lambda e: e.memset(out, c), (), w)
+
+    def scan(out, d0, d1, init, o0, o1, r, w):
+        return op("v", lambda e: e.tensor_tensor_scan(out, d0, d1, init, o0, o1), r, w)
+
+    def act(out, a, r, w, func=F.Copy, **kw):
+        return op("a", lambda e: e.activation(out, a, func, **kw), r, w)
+
+    def quant(q, s, a, r, w):
+        return op("v", lambda e: e.quantize_mx(q, s, a), r, w)
+
+    def mm(out, lq, ls, rq, rs, r, w):
+        return op("p", lambda e: e.matmul_mx(out, lq, ls, rq, rs, True, True), r, w)
+
+    def dma(q, out, a, r, w):
+        return op(q, lambda e: e.dma_start(out, a), r, w, 16)
+
+    def iota(out, pat, base, cm, w, flt=False):
+        if flt:
+            return op("g", lambda e: e.iota(out, pat, base, cm, allow_small_or_imprecise_dtypes=True), (), w)
+        return op("g", lambda e: e.iota(out, pat, base, cm), (), w)
+
+    def bank(k, n):
+        return T.ps[:, 512 * k:512 * k + n]
+
+    def xk(t, h):
+        return ["x%d.%d.%d" % (t, h, b) for b in range(4)]
+
+    def bits_of(h):
+        act(T.bits[:, 2 * HC * h:2 * HC * h + 2 * HC:2], bank(2 * h, HC), ["tiny"], ["ps%d" % (2 * h), "bit%d" % (2 * h)], func=F.Sign, bias=T.tiny[:, 0:1])
+        ts(T.bits[:, 2 * HC * h + 1:2 * HC * h + 2 * HC:2], bank(2 * h + 1, HC), 0.0, 2.0, A.is_gt, A.add, [], ["ps%d" % (2 * h + 1), "bit%d" % (2 * h + 1)])
+
+    def quant_x(t, h):
+        quant(T["qx%d" % t][:, HC * h:HC * h + HC], T["sx%d" % t][:, HC * h:HC * h + HC], T["win%d" % t][:, 4 * HC * h:4 * HC * h + 4 * HC], xk(t, h), ["qx%d.%d" % (t, h)])
+
+    def by_x(k, q, sc, keys, t, h):
+        mm(bank(k, HC), q, sc, T["qx%d" % t][:, HC * h:HC * h + HC], T["sx%d" % t][:, HC * h:HC * h + HC], keys + ["qx%d.%d" % (t, h)], ["ps%d" % k])
+
+    def fill(t):
+        act(T["tb%d" % t][:, 0:TAB], T.ones[:, 0:TAB], ["ones"], ["tb%d" % t], scale=B0)
+        act(T["tm%d" % t][:, 0:TAB], T.ones[:, 0:TAB], ["ones"], ["tm%d" % t], scale=0.0)
+
+    dma("a", T.ut[:], T.u[:], [], ["ut"])
+    dma("s", T.win0[:, 0:4 * C], T.x[:], [], xk(0, 0) + xk(0, 1))
+    dma("s", T.wq[:].bitcast(u8), T.wc[:], [], ["wq"])
+    dma("s", T.wsc[:], T.ws[:], [], ["wsc"])
+    dma("s", T.vt[:], T.v[:], [], ["vt"])
+
+    iota(T.i_p[:], [[0, 22]], 0, 1, ["i_p"])
+    iota(T.i_e[:], [[1, 16]], 128, -1, ["i_e"])
+    iota(T.i_u[:], [[1, 2], [16, 8]], 0, 0, ["i_u"])
+    iota(T.k16[:], [[16, 20]], 0, 0, ["k16"], True)
+    iota(T.k64[:], [[64, 8]], TAB - 1, 0, ["k64"], True)
+    iota(T.src_m[:], [[4, 80]], 2 * C, 0, ["sm0"], True)
+    ms(T.ones[:], 1.0, ["ones"])
+    ms(T.dw[:, 1:672:2], 1.0, ["dw1"])
+    ms(T.bits[:, 640:648], 1.0, ["bitp"])
+    ms(T.tiny[:], -2.0 ** -120, ["tiny"])
+    ms(T.dd[:], 1.0, ["dd"])
+    for k in range(2):
+        op("g", lambda e, k=k: e.affine_select(T["z%d" % k][:], T.ones[:], [[-1, 516]], A.is_equal, 0.0, 2 + k, 4), ["ones"], ["z%d" % k])
+    ts(T.j22[:], T.i_p[:], 15, None, A.bitwise_and, None, ["i_p"], ["j22"])
+    ts(T.e16[:], T.i_e[:], 15, None, A.bitwise_and, None, ["i_e"], ["e16"])
+    cp(T.uo[:], T.i_u[:], ["i_u"], ["uo"])
+    cp(T.jo[:], T.j22[:], ["j22"], ["jo"])
+    ts(T.pa[:], T.e16[:], 4.0, 124.0, A.is_equal, A.mult, ["e16"], ["pa"])
+    ts(T.pb[:], T.e16[:], 1.0, 4.0, A.min, A.mult, ["e16"], ["pb"])
+    ts(T.pc[:], T.e16[:], 4.0, -3.0, A.is_gt, A.mult, ["e16"], ["pc"])
+    ts(T.pe[:], T.e16[:], 0.0, -4096.0, A.is_equal, A.mult, ["e16"], ["pe"])
+    ts(T.pf[:], T.e16[:], 1.0, 1024.0, A.is_equal, A.mult, ["e16"], ["pf"])
+    tt(T.pd[:], T.pa[:], T.pb[:], A.add, ["pa", "pb"], ["pd"])
+    cp(T.jf[:], T.j22[:, 0:4], ["j22"], ["jf"])
+    tt(T.pt[:], T.pe[:], T.pf[:], A.add, ["pe", "pf"], ["pt"])
+    tt(T.pw[:], T.pd[:], T.pc[:], A.add, ["pd", "pc"], ["pw"])
+    fill(0)
+    act(T.dw[:, 0:672:2], T.pw[:].indirect(T.jo[:, 0:21]), ["pw", "jo"], ["dw0"])
+    ts(T.m0[:], T.e16[:], 0.0, None, A.is_equal, None, ["e16"], ["m0"])
+    ts(T.j4[:], T.jf[:], 4.0, None, A.mult, None, ["jf"], ["j4"])
+    ts(T.kp[:], T.jf[:], 15.0, 1024.0, A.is_lt, A.mult, ["jf"], ["kp"])
+    ts(T.cf[:], T.k16[:], T.jf[:, 0:1], None, A.add, None, ["k16", "jf"], ["cf"])
+    ms(T.db[:, 1:640:2], 1.0, ["db0"])
+    ms(T.db[:, 0:640:8], 0.0, ["db1"])
+    for i in range(3):
+        ms(T.db[:, 2 + 2 * i:640:8], 4.0, ["db%d" % (i + 2)])
+    ts(T.sl[:], T.k64[:], T.j4[:, 0:1], None, A.add, None, ["k64", "j4"], ["sl"])
+    ts(T.bk[:], T.kp[:], BASE, None, A.add, None, ["kp"], ["bk"])
+    ts(T.ck[:], T.cf[:], 576.0, T.kp[:, 0:1], A.add, A.subtract, ["cf", "kp"], ["ck"])
+    ms(T.src_b[:], B1, ["src_b"])
+    ms(T.st[:, 0:1], BASE, ["st0"])
+
+    quant(T.uq[:], T.usc[:], T.ut[:], ["ut"], ["uq"])
+    cp(T.up[:].bitcast(u32), T.uq[:].bitcast(u32).indirect(T.uo[:]), ["uq", "uo"], ["up"])
+    act(T.ups[:], T.usc[:].indirect(T.uo[:]), ["uq", "uo"], ["ups"])
+    ts(T.dw[:, 642:648:2], T.dw[:, 642:648:2], 4.0, None, A.min, None, ["dw0"], ["dw0"])
+    ts(T.cb[:], T.cf[:], -1.0, T.bk[:, 0:1], A.mult, A.add, ["cf", "bk"], ["cb"])
+
+    sent = [0]
+    for h in range(2):
+        quant_x(0, h)
+    for t in range(ROUNDS):
+        win, nxt = T["win%d" % t], T["win%d" % (t + 1)]
+        qx, sx, lq, lsc, wd, lw = [T["%s%d" % (n, t)] for n in ("qx", "sx", "lq", "lsc", "wd", "lw")]
+        tb, tm, gt, qg, sg = [T["%s%d" % (n, t)] for n in ("tb", "tm", "gt", "qg", "sg")]
+        peer = T.cores[rank ^ STEP[t]]
+        rid, pid = topo.addr(peer)[0:2]
+        eng = topo.engines(core, peer)
+        half = len(eng) // 2
+        lo, hi = sum(1 << e for e in eng[:half]), sum(1 << e for e in eng[half:])
+
+        def send(out, src, sem, mask, r):
+            need("g", r, [])
+            g.remote_dma(out, src, T.sem[sem], T.sem.sent, pid, rid, mask)
+            sent[0] += half
+        arrives("lq%d" % t, "ac%d" % t, 2 * half)
+        arrives("lw%d" % t, "aw%d" % t, half)
+        K = lambda n: "%s%d" % (n, t)
+        qk = ["qx%d.%d" % (t, h) for h in range(2)]
+
+        send(lq[:].bitcast(u8), qx[:].bitcast(u8), K("ac"), lo, qk)
+        for h in range(2):
+            for i in range(2):
+                by_x(2 * h + i, T.up[:, 128 * i:128 * i + 128], T.ups[:, 128 * i:128 * i + 128], ["up", "ups"], t, h)
+        if t == 0:
+            for b in range(4):
+                o = 2 - b // 2 * 2
+                if b == 2:
+                    bits_of(0)
+                quant(T.eq[:, 128 * b:128 * b + 128], T.esc[:, 128 * b:128 * b + 128], T["z%d" % (b % 2)][:, o:o + 512], ["z%d" % (b % 2)], ["eq%d" % b])
+        else:
+            bits_of(0)
+        bits_of(1)
+        bk_ = ["bit%d" % i for i in range(4)]
+        scan(T.wscan[:], T.dw[:, 0:648], T.bits[:], 0.0, A.mult, A.add, ["dw0", "dw1", "bitp"] + bk_, ["wscan"])
+        tt(T.vv[:], T.wscan[:, 31:648:32], T.wscan[:, 39:648:32], A.max, ["wscan"], ["vv"])
+        ts(wd[:], T.vv[:], 16.0, 2.0 ** -7, A.subtract, A.mult, ["vv"], [K("wd")])
+        send(lw[:], wd[:], K("aw"), hi, [K("wd")])
+        send(lsc[:], sx[:], K("ac"), lo, qk)
+        if t == 0:
+            act(T.dsel[:], T.pt[:].indirect(T.jo[:, 0:20]), ["pt", "jo"], ["dsel"])
+            for k in range(5):
+                act(T.dd[:, 96 * k:96 * k + 16], T.m0[:], ["m0", "sl", "dd"], ["dd%d" % k], func=F.Identity, scale=T.sl[:, k:k + 1], bias=1.0)
+            iota(T.hv[:, 0:2 * C], [[1, 2 * C]], 0, 0, ["hv0"], True)
+            iota(T.hv[:, 2 * C:3 * C], [[1, C]], 0, 0, ["hv1"], True)
+        act(win[:, 8 * C:12 * C], win[:, 0:4 * C], xk(t, 0) + xk(t, 1), [K("xc")])
+        if t + 1 < ROUNDS:
+            fill(t + 1)
+
+        scan(T.bscan[:], T.db[:], T.bits[:, 0:640], 0.0, A.mult, A.add, ["db%d" % i for i in range(5)] + bk_, ["bscan"])
+        scan(T.wsel[:], T.dsel[:, 0:80], T.bscan[:, 7:640:8], 0.0, A.add, A.max, ["dsel", "bscan"], ["wsel"])
+        ts(T.wk[:, 0:5], T.wsel[:, 15:80:16], T.kp[:, 0:1], None, A.subtract, None, ["wsel", "kp"], ["wk"])
+        if t == 0:
+            ms(T.dd[:, 0:400:80], 0.0, ["dd"] + ["dd%d" % k for k in range(5)])
+        for k in range(5):
+            ts(T.eqm[:, 80 * k:80 * k + 80], T.bscan[:, 7:640:8], T.wk[:, k:k + 1], None, A.is_equal, None, ["bscan", "wk"], ["eqm%d" % k])
+        scan(T.dscan[:], T.dd[:], T.eqm[:], 0.0, A.mult, A.max, ["dd"] + ["eqm%d" % k for k in range(5)], ["dscan"])
+        tt(T.of[:, 0:5], T.dscan[:, 79:400:80], T.wk[:, 0:5], A.max, ["dscan", "wk"], ["of"])
+        cp(T.ofu[:, 0:5], T.of[:, 0:5], ["of"], ["ofu"])
+        cp(tb[:].indirect(T.ofu[:, 0:5]), T.src_b[:], ["ofu", "src_b"], [K("tb")])
+        cp(tm[:].indirect(T.ofu[:, 0:5]), T.src_m[:], ["ofu", "sm0"], [K("tm")])
+
+        for b in range(4):
+            mm(bank(4 + b, C), T.eq[:, 128 * b:128 * b + 128], T.esc[:, 128 * b:128 * b + 128], lq[:], lsc[:], ["eq%d" % b, K("lq")], ["ps%d" % (4 + b)])
+
+        def evac(b, fn):
+            fn(win[:, 4 * C + b:8 * C:4], bank(4 + b, C), [], ["ps%d" % (4 + b), "d%d.%d" % (t, b)])
+
+        act(T.be[:], tb[:, 0:TAB].indirect(lw[:]), [K("tb"), K("lw")], ["be"])
+        ts(T.al[:], tb[:, 0:TAB].indirect(lw[:]), 1.0, A0, A.is_lt, A.max, [K("tb"), K("lw")], ["al"])
+        act(T.tf[:], tm[:, 0:TAB].indirect(lw[:]), [K("tm"), K("lw")], ["tf"])
+        evac(0, act)
+        scan(T.st[:, 1:C + 1], T.al[:], T.be[:], BASE, A.mult, A.mult, ["al", "be"], ["st"])
+        scan(T.ssel[:], T.dsel[:], T.st[:, 0:C], 0.0, A.add, A.max, ["dsel", "st", "st0"], ["ssel"])
+        sv = T.ssel[:, 15:C:16]
+        ts(T.x1[:], sv, T.bk[:, 0:1], 574.5, A.subtract, A.subtract, ["ssel", "bk"], ["x1"])
+        tt(T.ll[:], sv, T.cb[:], A.subtract, ["ssel", "cb"], ["ll"])
+        tt(T.y2[:], T.ll[:], T.x1[:], A.subtract, ["ll", "x1"], ["y2"])
+        ts(T.ix[:], T.y2[:], 576.0, None, A.subtract, None, ["y2"], ["ix"])
+        act(T.t2[:], T.tf[:].indirect(T.ix[:]), ["tf", "ix"], ["t2"])
+        evac(2, act)
+        evac(3, act)
+        ts(T.sh[:], T.ll[:], CAP - 0.5, float(C), A.is_lt, A.mult, ["ll"], ["sh"])
+        tt(T.ik[:], T.ck[:], T.y2[:], A.subtract, ["ck", "y2"], ["ik"])
+        evac(1, cp)
+        tt(T.lv[:], T.sh[:], T.cf[:], A.add, ["sh", "cf"], ["lv"])
+        scan(T.tsel[:], T.dsel[:], T.t2[:], 0.0, A.add, A.max, ["dsel", "t2"], ["tsel"])
+        tt(T.ha[:], T.tsel[:, 15:C:16], T.ik[:], A.add, ["tsel", "ik"], ["ha"])
+        tt(T.hh[:], T.ha[:], T.lv[:], A.max, ["ha", "lv"], ["hh"])
+        for b in (2, 0, 3, 1):
+            ts(T.gl[:, 20 * b:20 * b + 20], T.hh[:], 4.0, float(b), A.mult, A.add, ["hh"], ["gl%d" % b])
+        if t == ROUNDS - 1:
+            cp(T.ho[:], T.hh[:], ["hh"], ["ho"])
+
+        src = xk(t, 0) + xk(t, 1) + [K("xc")] + ["d%d.%d" % (t, b) for b in range(4)]
+        gk = [["g%d.%d.%d" % (t, h, b) for b in range(4)] for h in range(2)]
+
+        def part(buf, h, b=None):
+            return buf[:, 4 * HC * h:4 * HC * h + 4 * HC] if b is None else buf[:, 4 * HC * h + b:4 * HC * h + 4 * HC:4]
+
+        def gather(h, b, fn):
+            fn(part(gt, h, b), win[:].indirect(T.gl[:, 20 * b + 10 * h:20 * b + 10 * h + 10]), src + ["gl%d" % b], [gk[h][b]])
+
+        def layer(h):
+            quant(qg[:, HC * h:HC * h + HC], sg[:, HC * h:HC * h + HC], part(gt, h), gk[h], ["qg%d.%d" % (t, h)])
+            for b in range(4):
+                mm(bank(4 * h + b, HC), T.wq[:, 128 * b:128 * b + 128], T.wsc[:, 128 * b:128 * b + 128], qg[:, HC * h:HC * h + HC], sg[:, HC * h:HC * h + HC],
+                   ["wq", "wsc", "qg%d.%d" % (t, h)], ["ps%d" % (4 * h + b)])
+
+        def add(h, b):
+            tt(part(T.rr, h, b), bank(4 * h + b, HC), part(T.g64, h, b), A.add, ["g64.%d" % h], ["ps%d" % (4 * h + b), "r%d.%d" % (h, b)])
+
+        def scale(h, b, q):
+            if q == "a":
+                act(part(nxt, h, b), part(T.rr, h, b), ["r%d.%d" % (h, b)], [xk(t + 1, h)[b]], scale=2.0 ** -6)
+            else:
+                ts(part(nxt, h, b), part(T.rr, h, b), 2.0 ** -6, None, A.mult, None, ["r%d.%d" % (h, b)], [xk(t + 1, h)[b]])
+        for h in range(2):
+            gather(h, 2, act)
+            gather(h, 3, act)
+        gather(0, 0, cp)
+        gather(0, 1, cp)
+        layer(0)
+        gather(1, 0, cp)
+        gather(1, 1, cp)
+        act(part(T.g64, 0), part(gt, 0), gk[0], ["g64.0"], scale=64.0)
+        layer(1)
+        if t == ROUNDS - 1:
+            act(T.hf[:], T.hv[:].indirect(T.ho[:]), ["hv0", "hv1", "ho"], ["hf"])
+            dma("s", T.ot[:], T.hf[0:128:16, :], ["hf"], ["ot"])
+        ts(part(T.g64, 1), part(gt, 1), 64.0, None, A.mult, None, gk[1], ["g64.1"])
+        for b in range(4):
+            add(0, b)
+            scale(0, b, "a")
+        for b in range(4):
+            add(1, b)
+            if b < 3:
+                scale(1, b, "a")
+        quant_x(t + 1, 0)
+        scale(1, 3, "v")
+        quant_x(t + 1, 1)
+        if t == 0:
+            quant(T.vq[:], T.vsc[:], T.vt[:], ["vt"], ["vq"])
+
+    qx, sx = T["qx%d" % ROUNDS], T["sx%d" % ROUNDS]
+    qk = ["qx%d.%d" % (ROUNDS, h) for h in range(2)]
+    for h in range(2):
+        by_x(h, T.vq[:], T.vsc[:], ["vq"], ROUNDS, h)
+    dma("s", T.oc[:], qx[:].bitcast(u8), qk, ["oc"])
+    act(T.yo[:, 0:HC], bank(0, HC), [], ["ps0", "yo0"])
+    cp(T.yo[:, HC:C], bank(1, HC), [], ["ps1", "yo1"])
+    dma("a", T.y[:], T.yo[:], ["yo0", "yo1"], ["y"])
+    for k in range(4):
+        dma("s", T.osc[4 * k:4 * k + 4, :], sx[32 * k:32 * k + 4, :], qk, ["osc%d" % k])
+    g.wait_ge(T.sem.sent, sent[0])
+    finish("s")

@@ -1,7 +1,7 @@
 from concourse.mybir import dt, AluOpType as A, ActivationFunctionType as F
 
 C, CAP, ROUNDS, STEP = 320, 96, 3, [1, 2, 1]
-HC = C // 2
+CUT = [0, 192, C]
 TAB, WIN = 344, 664
 BASE = 14212656.0
 A0 = 0.75 + 9 * 2.0 ** -24
@@ -126,28 +126,36 @@ def rank_program(g, core, T, topo):
             return op("g", lambda e: e.iota(out, pat, base, cm, allow_small_or_imprecise_dtypes=True), (), w)
         return op("g", lambda e: e.iota(out, pat, base, cm), (), w)
 
-    def bank(k, n):
-        return T.ps[:, 512 * k:512 * k + n]
+    def bank(k, h=None):
+        return T.ps[:, 512 * k:512 * k + (C if h is None else CUT[h + 1] - CUT[h])]
+
+    def part(buf, h, w=1, b=None):
+        return buf[:, w * CUT[h]:w * CUT[h + 1]] if b is None else buf[:, w * CUT[h] + b:w * CUT[h + 1]:w]
 
     def xk(t, h):
         return ["x%d.%d.%d" % (t, h, b) for b in range(4)]
 
     def bits_of(h):
-        act(T.bits[:, 2 * HC * h:2 * HC * h + 2 * HC:2], bank(2 * h, HC), ["tiny"], ["ps%d" % (2 * h), "bit%d" % (2 * h)], func=F.Sign, bias=T.tiny[:, 0:1])
-        ts(T.bits[:, 2 * HC * h + 1:2 * HC * h + 2 * HC:2], bank(2 * h + 1, HC), 0.0, 2.0, A.is_gt, A.add, [], ["ps%d" % (2 * h + 1), "bit%d" % (2 * h + 1)])
+        act(part(T.bits, h, 2, 0), bank(2 * h, h), ["tiny"], ["ps%d" % (2 * h), "bit%d" % (2 * h)], func=F.Sign, bias=T.tiny[:, 0:1])
+        ts(part(T.bits, h, 2, 1), bank(2 * h + 1, h), 0.0, 2.0, A.is_gt, A.add, [], ["ps%d" % (2 * h + 1), "bit%d" % (2 * h + 1)])
 
     def quant_x(t, h):
-        quant(T["qx%d" % t][:, HC * h:HC * h + HC], T["sx%d" % t][:, HC * h:HC * h + HC], T["win%d" % t][:, 4 * HC * h:4 * HC * h + 4 * HC], xk(t, h), ["qx%d.%d" % (t, h)])
+        quant(part(T["qx%d" % t], h), part(T["sx%d" % t], h), part(T["win%d" % t], h, 4), xk(t, h), ["qx%d.%d" % (t, h)])
+
+    def quant_e(b):
+        o = 2 - b // 2 * 2
+        quant(T.eq[:, 128 * b:128 * b + 128], T.esc[:, 128 * b:128 * b + 128], T["z%d" % (b % 2)][:, o:o + 512], ["z%d" % (b % 2)], ["eq%d" % b])
 
     def by_x(k, q, sc, keys, t, h):
-        mm(bank(k, HC), q, sc, T["qx%d" % t][:, HC * h:HC * h + HC], T["sx%d" % t][:, HC * h:HC * h + HC], keys + ["qx%d.%d" % (t, h)], ["ps%d" % k])
+        mm(bank(k, h), q, sc, part(T["qx%d" % t], h), part(T["sx%d" % t], h), keys + ["qx%d.%d" % (t, h)], ["ps%d" % k])
 
     def fill(t):
         act(T["tb%d" % t][:, 0:TAB], T.ones[:, 0:TAB], ["ones"], ["tb%d" % t], scale=B0)
         act(T["tm%d" % t][:, 0:TAB], T.ones[:, 0:TAB], ["ones"], ["tm%d" % t], scale=0.0)
 
     dma("a", T.ut[:], T.u[:], [], ["ut"])
-    dma("s", T.win0[:, 0:4 * C], T.x[:], [], xk(0, 0) + xk(0, 1))
+    for h in range(2):
+        dma("s", part(T.win0, h, 4), part(T.x, h, 4), [], xk(0, h))
     dma("s", T.wq[:].bitcast(u8), T.wc[:], [], ["wq"])
     dma("s", T.wsc[:], T.ws[:], [], ["wsc"])
     dma("s", T.vt[:], T.v[:], [], ["vt"])
@@ -163,8 +171,7 @@ def rank_program(g, core, T, topo):
     ms(T.bits[:, 640:648], 1.0, ["bitp"])
     ms(T.tiny[:], -2.0 ** -120, ["tiny"])
     ms(T.dd[:], 1.0, ["dd"])
-    for k in range(2):
-        op("g", lambda e, k=k: e.affine_select(T["z%d" % k][:], T.ones[:], [[-1, 516]], A.is_equal, 0.0, 2 + k, 4), ["ones"], ["z%d" % k])
+    op("g", lambda e: e.affine_select(T.z1[:], T.ones[:], [[-1, 516]], A.is_equal, 0.0, 3, 4), ["ones"], ["z1"])
     ts(T.j22[:], T.i_p[:], 15, None, A.bitwise_and, None, ["i_p"], ["j22"])
     ts(T.e16[:], T.i_e[:], 15, None, A.bitwise_and, None, ["i_e"], ["e16"])
     cp(T.uo[:], T.i_u[:], ["i_u"], ["uo"])
@@ -183,68 +190,58 @@ def rank_program(g, core, T, topo):
     ts(T.m0[:], T.e16[:], 0.0, None, A.is_equal, None, ["e16"], ["m0"])
     ts(T.j4[:], T.jf[:], 4.0, None, A.mult, None, ["jf"], ["j4"])
     ts(T.kp[:], T.jf[:], 15.0, 1024.0, A.is_lt, A.mult, ["jf"], ["kp"])
-    ts(T.cf[:], T.k16[:], T.jf[:, 0:1], None, A.add, None, ["k16", "jf"], ["cf"])
+    ms(T.src_b[:], B1, ["src_b"])
+    ts(T.sl[:], T.k64[:], T.j4[:, 0:1], None, A.add, None, ["k64", "j4"], ["sl"])
     ms(T.db[:, 1:640:2], 1.0, ["db0"])
     ms(T.db[:, 0:640:8], 0.0, ["db1"])
     for i in range(3):
         ms(T.db[:, 2 + 2 * i:640:8], 4.0, ["db%d" % (i + 2)])
-    ts(T.sl[:], T.k64[:], T.j4[:, 0:1], None, A.add, None, ["k64", "j4"], ["sl"])
-    ts(T.bk[:], T.kp[:], BASE, None, A.add, None, ["kp"], ["bk"])
-    ts(T.ck[:], T.cf[:], 576.0, T.kp[:, 0:1], A.add, A.subtract, ["cf", "kp"], ["ck"])
-    ms(T.src_b[:], B1, ["src_b"])
-    ms(T.st[:, 0:1], BASE, ["st0"])
 
     quant(T.uq[:], T.usc[:], T.ut[:], ["ut"], ["uq"])
-    cp(T.up[:].bitcast(u32), T.uq[:].bitcast(u32).indirect(T.uo[:]), ["uq", "uo"], ["up"])
     act(T.ups[:], T.usc[:].indirect(T.uo[:]), ["uq", "uo"], ["ups"])
-    ts(T.dw[:, 642:648:2], T.dw[:, 642:648:2], 4.0, None, A.min, None, ["dw0"], ["dw0"])
-    ts(T.cb[:], T.cf[:], -1.0, T.bk[:, 0:1], A.mult, A.add, ["cf", "bk"], ["cb"])
-
-    sent = [0]
     for h in range(2):
         quant_x(0, h)
+    cp(T.up[:].bitcast(u32), T.uq[:].bitcast(u32).indirect(T.uo[:]), ["uq", "uo"], ["up"])
+    ts(T.dw[:, 642:648:2], T.dw[:, 642:648:2], 4.0, None, A.min, None, ["dw0"], ["dw0"])
+
+    sent = [0]
     for t in range(ROUNDS):
         win, nxt = T["win%d" % t], T["win%d" % (t + 1)]
         qx, sx, lq, lsc, wd, lw = [T["%s%d" % (n, t)] for n in ("qx", "sx", "lq", "lsc", "wd", "lw")]
         tb, tm, gt, qg, sg = [T["%s%d" % (n, t)] for n in ("tb", "tm", "gt", "qg", "sg")]
         peer = T.cores[rank ^ STEP[t]]
         rid, pid = topo.addr(peer)[0:2]
-        eng = topo.engines(core, peer)
-        half = len(eng) // 2
-        lo, hi = sum(1 << e for e in eng[:half]), sum(1 << e for e in eng[half:])
+        mask, ne = topo.mask(core, peer), len(topo.engines(core, peer))
 
-        def send(out, src, sem, mask, r):
+        def send(out, src, sem, r):
             need("g", r, [])
             g.remote_dma(out, src, T.sem[sem], T.sem.sent, pid, rid, mask)
-            sent[0] += half
-        arrives("lq%d" % t, "ac%d" % t, 2 * half)
-        arrives("lw%d" % t, "aw%d" % t, half)
+            sent[0] += ne
+        arrives("lq%d" % t, "ac%d" % t, 2 * ne)
+        arrives("lw%d" % t, "aw%d" % t, ne)
         K = lambda n: "%s%d" % (n, t)
         qk = ["qx%d.%d" % (t, h) for h in range(2)]
 
-        send(lq[:].bitcast(u8), qx[:].bitcast(u8), K("ac"), lo, qk)
+        send(lq[:].bitcast(u8), qx[:].bitcast(u8), K("ac"), qk)
         for h in range(2):
             for i in range(2):
                 by_x(2 * h + i, T.up[:, 128 * i:128 * i + 128], T.ups[:, 128 * i:128 * i + 128], ["up", "ups"], t, h)
         if t == 0:
-            for b in range(4):
-                o = 2 - b // 2 * 2
-                if b == 2:
-                    bits_of(0)
-                quant(T.eq[:, 128 * b:128 * b + 128], T.esc[:, 128 * b:128 * b + 128], T["z%d" % (b % 2)][:, o:o + 512], ["z%d" % (b % 2)], ["eq%d" % b])
-        else:
-            bits_of(0)
+            quant_e(1)
+            quant_e(3)
+        bits_of(0)
         bits_of(1)
         bk_ = ["bit%d" % i for i in range(4)]
         scan(T.wscan[:], T.dw[:, 0:648], T.bits[:], 0.0, A.mult, A.add, ["dw0", "dw1", "bitp"] + bk_, ["wscan"])
         tt(T.vv[:], T.wscan[:, 31:648:32], T.wscan[:, 39:648:32], A.max, ["wscan"], ["vv"])
         ts(wd[:], T.vv[:], 16.0, 2.0 ** -7, A.subtract, A.mult, ["vv"], [K("wd")])
-        send(lw[:], wd[:], K("aw"), hi, [K("wd")])
-        send(lsc[:], sx[:], K("ac"), lo, qk)
+        send(lw[:], wd[:], K("aw"), [K("wd")])
+        send(lsc[:], sx[:], K("ac"), qk)
         if t == 0:
             act(T.dsel[:], T.pt[:].indirect(T.jo[:, 0:20]), ["pt", "jo"], ["dsel"])
             for k in range(5):
                 act(T.dd[:, 96 * k:96 * k + 16], T.m0[:], ["m0", "sl", "dd"], ["dd%d" % k], func=F.Identity, scale=T.sl[:, k:k + 1], bias=1.0)
+            act(T.z0[:, 0:514], T.z1[:, 1:515], ["z1"], ["z0"])
             iota(T.hv[:, 0:2 * C], [[1, 2 * C]], 0, 0, ["hv0"], True)
             iota(T.hv[:, 2 * C:3 * C], [[1, C]], 0, 0, ["hv1"], True)
         act(win[:, 8 * C:12 * C], win[:, 0:4 * C], xk(t, 0) + xk(t, 1), [K("xc")])
@@ -253,86 +250,85 @@ def rank_program(g, core, T, topo):
 
         scan(T.bscan[:], T.db[:], T.bits[:, 0:640], 0.0, A.mult, A.add, ["db%d" % i for i in range(5)] + bk_, ["bscan"])
         scan(T.wsel[:], T.dsel[:, 0:80], T.bscan[:, 7:640:8], 0.0, A.add, A.max, ["dsel", "bscan"], ["wsel"])
-        ts(T.wk[:, 0:5], T.wsel[:, 15:80:16], T.kp[:, 0:1], None, A.subtract, None, ["wsel", "kp"], ["wk"])
         if t == 0:
             ms(T.dd[:, 0:400:80], 0.0, ["dd"] + ["dd%d" % k for k in range(5)])
         for k in range(5):
-            ts(T.eqm[:, 80 * k:80 * k + 80], T.bscan[:, 7:640:8], T.wk[:, k:k + 1], None, A.is_equal, None, ["bscan", "wk"], ["eqm%d" % k])
+            ts(T.eqm[:, 80 * k:80 * k + 80], T.bscan[:, 7:640:8], T.kp[:, 0:1], T.wsel[:, 16 * k + 15:16 * k + 16], A.add, A.is_equal,
+               ["bscan", "wsel", "kp"], ["eqm%d" % k])
+        ts(T.wk[:, 0:5], T.wsel[:, 15:80:16], T.kp[:, 0:1], None, A.subtract, None, ["wsel", "kp"], ["wk"])
         scan(T.dscan[:], T.dd[:], T.eqm[:], 0.0, A.mult, A.max, ["dd"] + ["eqm%d" % k for k in range(5)], ["dscan"])
+        if t == 0:
+            ts(T.cf[:], T.k16[:], T.jf[:, 0:1], None, A.add, None, ["k16", "jf"], ["cf"])
         tt(T.of[:, 0:5], T.dscan[:, 79:400:80], T.wk[:, 0:5], A.max, ["dscan", "wk"], ["of"])
+        if t == 0:
+            ts(T.bk[:], T.kp[:], BASE, None, A.add, None, ["kp"], ["bk"])
         cp(T.ofu[:, 0:5], T.of[:, 0:5], ["of"], ["ofu"])
+        if t == 0:
+            ms(T.st[:, 0:1], BASE, ["st0"])
         cp(tb[:].indirect(T.ofu[:, 0:5]), T.src_b[:], ["ofu", "src_b"], [K("tb")])
         cp(tm[:].indirect(T.ofu[:, 0:5]), T.src_m[:], ["ofu", "sm0"], [K("tm")])
-
-        for b in range(4):
-            mm(bank(4 + b, C), T.eq[:, 128 * b:128 * b + 128], T.esc[:, 128 * b:128 * b + 128], lq[:], lsc[:], ["eq%d" % b, K("lq")], ["ps%d" % (4 + b)])
-
-        def evac(b, fn):
-            fn(win[:, 4 * C + b:8 * C:4], bank(4 + b, C), [], ["ps%d" % (4 + b), "d%d.%d" % (t, b)])
+        if t == 0:
+            quant_e(0)
+            quant_e(2)
+            ts(T.ck[:], T.cf[:], 576.0, T.kp[:, 0:1], A.add, A.subtract, ["cf", "kp"], ["ck"])
+            ts(T.cb[:], T.cf[:], -1.0, T.bk[:, 0:1], A.mult, A.add, ["cf", "bk"], ["cb"])
 
         act(T.be[:], tb[:, 0:TAB].indirect(lw[:]), [K("tb"), K("lw")], ["be"])
         ts(T.al[:], tb[:, 0:TAB].indirect(lw[:]), 1.0, A0, A.is_lt, A.max, [K("tb"), K("lw")], ["al"])
         act(T.tf[:], tm[:, 0:TAB].indirect(lw[:]), [K("tm"), K("lw")], ["tf"])
-        evac(0, act)
+        for b in range(4):
+            mm(bank(4 + b), T.eq[:, 128 * b:128 * b + 128], T.esc[:, 128 * b:128 * b + 128], lq[:], lsc[:], ["eq%d" % b, K("lq")], ["ps%d" % (4 + b)])
+            act(win[:, 4 * C + b:8 * C:4], bank(4 + b), [], ["ps%d" % (4 + b), "d%d.%d" % (t, b)])
         scan(T.st[:, 1:C + 1], T.al[:], T.be[:], BASE, A.mult, A.mult, ["al", "be"], ["st"])
         scan(T.ssel[:], T.dsel[:], T.st[:, 0:C], 0.0, A.add, A.max, ["dsel", "st", "st0"], ["ssel"])
         sv = T.ssel[:, 15:C:16]
         ts(T.x1[:], sv, T.bk[:, 0:1], 574.5, A.subtract, A.subtract, ["ssel", "bk"], ["x1"])
         tt(T.ll[:], sv, T.cb[:], A.subtract, ["ssel", "cb"], ["ll"])
         tt(T.y2[:], T.ll[:], T.x1[:], A.subtract, ["ll", "x1"], ["y2"])
-        ts(T.ix[:], T.y2[:], 576.0, None, A.subtract, None, ["y2"], ["ix"])
-        act(T.t2[:], T.tf[:].indirect(T.ix[:]), ["tf", "ix"], ["t2"])
-        evac(2, act)
-        evac(3, act)
         ts(T.sh[:], T.ll[:], CAP - 0.5, float(C), A.is_lt, A.mult, ["ll"], ["sh"])
+        ts(T.ix[:], T.y2[:], 576.0, None, A.subtract, None, ["y2"], ["ix"])
         tt(T.ik[:], T.ck[:], T.y2[:], A.subtract, ["ck", "y2"], ["ik"])
-        evac(1, cp)
+        cp(T.t2[:], T.tf[:].indirect(T.ix[:]), ["tf", "ix"], ["t2"])
         tt(T.lv[:], T.sh[:], T.cf[:], A.add, ["sh", "cf"], ["lv"])
         scan(T.tsel[:], T.dsel[:], T.t2[:], 0.0, A.add, A.max, ["dsel", "t2"], ["tsel"])
         tt(T.ha[:], T.tsel[:, 15:C:16], T.ik[:], A.add, ["tsel", "ik"], ["ha"])
         tt(T.hh[:], T.ha[:], T.lv[:], A.max, ["ha", "lv"], ["hh"])
         for b in (2, 0, 3, 1):
             ts(T.gl[:, 20 * b:20 * b + 20], T.hh[:], 4.0, float(b), A.mult, A.add, ["hh"], ["gl%d" % b])
-        if t == ROUNDS - 1:
-            cp(T.ho[:], T.hh[:], ["hh"], ["ho"])
 
         src = xk(t, 0) + xk(t, 1) + [K("xc")] + ["d%d.%d" % (t, b) for b in range(4)]
         gk = [["g%d.%d.%d" % (t, h, b) for b in range(4)] for h in range(2)]
 
-        def part(buf, h, b=None):
-            return buf[:, 4 * HC * h:4 * HC * h + 4 * HC] if b is None else buf[:, 4 * HC * h + b:4 * HC * h + 4 * HC:4]
-
         def gather(h, b, fn):
-            fn(part(gt, h, b), win[:].indirect(T.gl[:, 20 * b + 10 * h:20 * b + 10 * h + 10]), src + ["gl%d" % b], [gk[h][b]])
+            fn(part(gt, h, 4, b), win[:].indirect(T.gl[:, 20 * b + CUT[h] // 16:20 * b + CUT[h + 1] // 16]), src + ["gl%d" % b], [gk[h][b]])
 
         def layer(h):
-            quant(qg[:, HC * h:HC * h + HC], sg[:, HC * h:HC * h + HC], part(gt, h), gk[h], ["qg%d.%d" % (t, h)])
+            quant(part(qg, h), part(sg, h), part(gt, h, 4), gk[h], ["qg%d.%d" % (t, h)])
             for b in range(4):
-                mm(bank(4 * h + b, HC), T.wq[:, 128 * b:128 * b + 128], T.wsc[:, 128 * b:128 * b + 128], qg[:, HC * h:HC * h + HC], sg[:, HC * h:HC * h + HC],
+                mm(bank(4 * h + b, h), T.wq[:, 128 * b:128 * b + 128], T.wsc[:, 128 * b:128 * b + 128], part(qg, h), part(sg, h),
                    ["wq", "wsc", "qg%d.%d" % (t, h)], ["ps%d" % (4 * h + b)])
 
         def add(h, b):
-            tt(part(T.rr, h, b), bank(4 * h + b, HC), part(T.g64, h, b), A.add, ["g64.%d" % h], ["ps%d" % (4 * h + b), "r%d.%d" % (h, b)])
+            tt(part(T.rr, h, 4, b), bank(4 * h + b, h), part(T.g64, h, 4, b), A.add, ["g64.%d" % h], ["ps%d" % (4 * h + b), "r%d.%d" % (h, b)])
 
         def scale(h, b, q):
             if q == "a":
-                act(part(nxt, h, b), part(T.rr, h, b), ["r%d.%d" % (h, b)], [xk(t + 1, h)[b]], scale=2.0 ** -6)
+                act(part(nxt, h, 4, b), part(T.rr, h, 4, b), ["r%d.%d" % (h, b)], [xk(t + 1, h)[b]], scale=2.0 ** -6)
             else:
-                ts(part(nxt, h, b), part(T.rr, h, b), 2.0 ** -6, None, A.mult, None, ["r%d.%d" % (h, b)], [xk(t + 1, h)[b]])
+                ts(part(nxt, h, 4, b), part(T.rr, h, 4, b), 2.0 ** -6, None, A.mult, None, ["r%d.%d" % (h, b)], [xk(t + 1, h)[b]])
         for h in range(2):
             gather(h, 2, act)
             gather(h, 3, act)
         gather(0, 0, cp)
         gather(0, 1, cp)
+        if t == ROUNDS - 1:
+            cp(T.ho[:], T.hh[:], ["hh"], ["ho"])
         layer(0)
         gather(1, 0, cp)
-        gather(1, 1, cp)
-        act(part(T.g64, 0), part(gt, 0), gk[0], ["g64.0"], scale=64.0)
+        gather(1, 1, act)
+        ts(part(T.g64, 0, 4), part(gt, 0, 4), 64.0, None, A.mult, None, gk[0], ["g64.0"])
         layer(1)
-        if t == ROUNDS - 1:
-            act(T.hf[:], T.hv[:].indirect(T.ho[:]), ["hv0", "hv1", "ho"], ["hf"])
-            dma("s", T.ot[:], T.hf[0:128:16, :], ["hf"], ["ot"])
-        ts(part(T.g64, 1), part(gt, 1), 64.0, None, A.mult, None, gk[1], ["g64.1"])
+        act(part(T.g64, 1, 4), part(gt, 1, 4), gk[1], ["g64.1"], scale=64.0)
         for b in range(4):
             add(0, b)
             scale(0, b, "a")
@@ -340,6 +336,8 @@ def rank_program(g, core, T, topo):
             add(1, b)
             if b < 3:
                 scale(1, b, "a")
+        if t == ROUNDS - 1:
+            act(T.hf[:, 0:C // 2], T.hv[:].indirect(T.ho[:, 0:10]), ["hv0", "hv1", "ho"], ["hf0"])
         quant_x(t + 1, 0)
         scale(1, 3, "v")
         quant_x(t + 1, 1)
@@ -350,11 +348,14 @@ def rank_program(g, core, T, topo):
     qk = ["qx%d.%d" % (ROUNDS, h) for h in range(2)]
     for h in range(2):
         by_x(h, T.vq[:], T.vsc[:], ["vq"], ROUNDS, h)
-    dma("s", T.oc[:], qx[:].bitcast(u8), qk, ["oc"])
-    act(T.yo[:, 0:HC], bank(0, HC), [], ["ps0", "yo0"])
-    cp(T.yo[:, HC:C], bank(1, HC), [], ["ps1", "yo1"])
-    dma("a", T.y[:], T.yo[:], ["yo0", "yo1"], ["y"])
+        dma("s", part(T.oc, h, 4), part(qx, h).bitcast(u8), [qk[h]], ["oc%d" % h])
+    cp(T.hf[:, C // 2:C], T.hv[:].indirect(T.ho[:, 10:20]), ["hv0", "hv1", "ho"], ["hf1"])
+    act(part(T.yo, 0), bank(0, 0), [], ["ps0", "yo0"])
+    dma("a", part(T.y, 0), part(T.yo, 0), ["yo0"], ["y0"])
+    cp(part(T.yo, 1), bank(1, 1), [], ["ps1", "yo1"])
     for k in range(4):
-        dma("s", T.osc[4 * k:4 * k + 4, :], sx[32 * k:32 * k + 4, :], qk, ["osc%d" % k])
+        dma("sa"[k // 2], T.osc[4 * k:4 * k + 4, :], sx[32 * k:32 * k + 4, :], qk, ["osc%d" % k])
+    dma("a", T.ot[:], T.hf[0:128:16, :], ["hf0", "hf1"], ["ot"])
+    dma("s", part(T.y, 1), part(T.yo, 1), ["yo1"], ["y1"])
     g.wait_ge(T.sem.sent, sent[0])
     finish("s")

@@ -139,6 +139,10 @@ def rank_program(g, core, T, topo):
         act(part(T.bits, h, 2, 0), bank(2 * h, h), ["tiny"], ["ps%d" % (2 * h), "bit%d" % (2 * h)], func=F.Sign, bias=T.tiny[:, 0:1])
         ts(part(T.bits, h, 2, 1), bank(2 * h + 1, h), 0.0, 2.0, A.is_gt, A.add, [], ["ps%d" % (2 * h + 1), "bit%d" % (2 * h + 1)])
 
+    def blocks_of(h):
+        scan(part(T.bscan, h, 2), part(T.db, h, 2), part(T.bits, h, 2), 0.0, A.mult, A.add,
+             ["db%d" % i for i in range(5)] + ["bit%d" % (2 * h), "bit%d" % (2 * h + 1)], ["bscan%d" % h])
+
     def quant_x(t, h):
         quant(part(T["qx%d" % t], h), part(T["sx%d" % t], h), part(T["win%d" % t], h, 4), xk(t, h), ["qx%d.%d" % (t, h)])
 
@@ -187,6 +191,7 @@ def rank_program(g, core, T, topo):
     tt(T.pw[:], T.pd[:], T.pc[:], A.add, ["pd", "pc"], ["pw"])
     fill(0)
     act(T.dw[:, 0:672:2], T.pw[:].indirect(T.jo[:, 0:21]), ["pw", "jo"], ["dw0"])
+    act(T.dsel[:], T.pt[:].indirect(T.jo[:, 0:20]), ["pt", "jo"], ["dsel"])
     ts(T.m0[:], T.e16[:], 0.0, None, A.is_equal, None, ["e16"], ["m0"])
     ts(T.j4[:], T.jf[:], 4.0, None, A.mult, None, ["jf"], ["j4"])
     ts(T.kp[:], T.jf[:], 15.0, 1024.0, A.is_lt, A.mult, ["jf"], ["kp"])
@@ -223,6 +228,8 @@ def rank_program(g, core, T, topo):
         qk = ["qx%d.%d" % (t, h) for h in range(2)]
 
         send(lq[:].bitcast(u8), qx[:].bitcast(u8), K("ac"), qk)
+        if t > 0:
+            send(lsc[:], sx[:], K("ac"), qk)
         for h in range(2):
             for i in range(2):
                 by_x(2 * h + i, T.up[:, 128 * i:128 * i + 128], T.ups[:, 128 * i:128 * i + 128], ["up", "ups"], t, h)
@@ -231,14 +238,15 @@ def rank_program(g, core, T, topo):
             quant_e(3)
         bits_of(0)
         bits_of(1)
-        bk_ = ["bit%d" % i for i in range(4)]
-        scan(T.wscan[:], T.dw[:, 0:648], T.bits[:], 0.0, A.mult, A.add, ["dw0", "dw1", "bitp"] + bk_, ["wscan"])
+        blocks_of(0)
+        scan(T.wscan[:], T.dw[:, 0:648], T.bits[:], 0.0, A.mult, A.add, ["dw0", "dw1", "bitp"] + ["bit%d" % i for i in range(4)], ["wscan"])
+        blocks_of(1)
         tt(T.vv[:], T.wscan[:, 31:648:32], T.wscan[:, 39:648:32], A.max, ["wscan"], ["vv"])
+        scan(T.wsel[:], T.dsel[:, 0:80], T.bscan[:, 7:640:8], 0.0, A.add, A.max, ["dsel", "bscan0", "bscan1"], ["wsel"])
         ts(wd[:], T.vv[:], 16.0, 2.0 ** -7, A.subtract, A.mult, ["vv"], [K("wd")])
         send(lw[:], wd[:], K("aw"), [K("wd")])
-        send(lsc[:], sx[:], K("ac"), qk)
         if t == 0:
-            act(T.dsel[:], T.pt[:].indirect(T.jo[:, 0:20]), ["pt", "jo"], ["dsel"])
+            send(lsc[:], sx[:], K("ac"), qk)
             for k in range(5):
                 act(T.dd[:, 96 * k:96 * k + 16], T.m0[:], ["m0", "sl", "dd"], ["dd%d" % k], func=F.Identity, scale=T.sl[:, k:k + 1], bias=1.0)
             act(T.z0[:, 0:514], T.z1[:, 1:515], ["z1"], ["z0"])
@@ -248,13 +256,11 @@ def rank_program(g, core, T, topo):
         if t + 1 < ROUNDS:
             fill(t + 1)
 
-        scan(T.bscan[:], T.db[:], T.bits[:, 0:640], 0.0, A.mult, A.add, ["db%d" % i for i in range(5)] + bk_, ["bscan"])
-        scan(T.wsel[:], T.dsel[:, 0:80], T.bscan[:, 7:640:8], 0.0, A.add, A.max, ["dsel", "bscan"], ["wsel"])
         if t == 0:
             ms(T.dd[:, 0:400:80], 0.0, ["dd"] + ["dd%d" % k for k in range(5)])
         for k in range(5):
             ts(T.eqm[:, 80 * k:80 * k + 80], T.bscan[:, 7:640:8], T.kp[:, 0:1], T.wsel[:, 16 * k + 15:16 * k + 16], A.add, A.is_equal,
-               ["bscan", "wsel", "kp"], ["eqm%d" % k])
+               ["bscan0", "bscan1", "wsel", "kp"], ["eqm%d" % k])
         ts(T.wk[:, 0:5], T.wsel[:, 15:80:16], T.kp[:, 0:1], None, A.subtract, None, ["wsel", "kp"], ["wk"])
         scan(T.dscan[:], T.dd[:], T.eqm[:], 0.0, A.mult, A.max, ["dd"] + ["eqm%d" % k for k in range(5)], ["dscan"])
         if t == 0:
@@ -273,24 +279,35 @@ def rank_program(g, core, T, topo):
             ts(T.ck[:], T.cf[:], 576.0, T.kp[:, 0:1], A.add, A.subtract, ["cf", "kp"], ["ck"])
             ts(T.cb[:], T.cf[:], -1.0, T.bk[:, 0:1], A.mult, A.add, ["cf", "bk"], ["cb"])
 
-        act(T.be[:], tb[:, 0:TAB].indirect(lw[:]), [K("tb"), K("lw")], ["be"])
-        ts(T.al[:], tb[:, 0:TAB].indirect(lw[:]), 1.0, A0, A.is_lt, A.max, [K("tb"), K("lw")], ["al"])
+        def evac(b):
+            act(win[:, 4 * C + b:8 * C:4], bank(4 + b), [], ["ps%d" % (4 + b), "d%d.%d" % (t, b)])
+        for h in range(2):
+            o = lw[:, CUT[h] // 16:CUT[h + 1] // 16]
+            act(part(T.be, h), tb[:, 0:TAB].indirect(o), [K("tb"), K("lw")], ["be%d" % h])
+            ts(part(T.al, h), tb[:, 0:TAB].indirect(o), 1.0, A0, A.is_lt, A.max, [K("tb"), K("lw")], ["al%d" % h])
         act(T.tf[:], tm[:, 0:TAB].indirect(lw[:]), [K("tm"), K("lw")], ["tf"])
         for b in range(4):
             mm(bank(4 + b), T.eq[:, 128 * b:128 * b + 128], T.esc[:, 128 * b:128 * b + 128], lq[:], lsc[:], ["eq%d" % b, K("lq")], ["ps%d" % (4 + b)])
-            act(win[:, 4 * C + b:8 * C:4], bank(4 + b), [], ["ps%d" % (4 + b), "d%d.%d" % (t, b)])
-        scan(T.st[:, 1:C + 1], T.al[:], T.be[:], BASE, A.mult, A.mult, ["al", "be"], ["st"])
-        scan(T.ssel[:], T.dsel[:], T.st[:, 0:C], 0.0, A.add, A.max, ["dsel", "st", "st0"], ["ssel"])
+        evac(0)
+        evac(1)
+        m = CUT[1]
+        scan(T.st[:, 1:m + 1], part(T.al, 0), part(T.be, 0), BASE, A.mult, A.mult, ["al0", "be0"], ["sta"])
+        scan(T.st[:, m + 1:C + 1], part(T.al, 1), part(T.be, 1), T.st[:, m:m + 1], A.mult, A.mult, ["al1", "be1", "sta"], ["stb"])
+        scan(part(T.ssel, 0), part(T.dsel, 0), part(T.st, 0), 0.0, A.add, A.max, ["dsel", "sta", "st0"], ["ssela"])
+        scan(part(T.ssel, 1), part(T.dsel, 1), part(T.st, 1), 0.0, A.add, A.max, ["dsel", "sta", "stb"], ["ssel"])
         sv = T.ssel[:, 15:C:16]
-        ts(T.x1[:], sv, T.bk[:, 0:1], 574.5, A.subtract, A.subtract, ["ssel", "bk"], ["x1"])
-        tt(T.ll[:], sv, T.cb[:], A.subtract, ["ssel", "cb"], ["ll"])
+        ts(T.x1[:], sv, T.bk[:, 0:1], 574.5, A.subtract, A.subtract, ["ssel", "ssela", "bk"], ["x1"])
+        tt(T.ll[:], sv, T.cb[:], A.subtract, ["ssel", "ssela", "cb"], ["ll"])
         tt(T.y2[:], T.ll[:], T.x1[:], A.subtract, ["ll", "x1"], ["y2"])
         ts(T.sh[:], T.ll[:], CAP - 0.5, float(C), A.is_lt, A.mult, ["ll"], ["sh"])
         ts(T.ix[:], T.y2[:], 576.0, None, A.subtract, None, ["y2"], ["ix"])
+        act(T.t2[:, 0:C // 2], T.tf[:].indirect(T.ix[:, 0:10]), ["tf", "ix"], ["t2a"])
+        evac(2)
+        evac(3)
         tt(T.ik[:], T.ck[:], T.y2[:], A.subtract, ["ck", "y2"], ["ik"])
-        cp(T.t2[:], T.tf[:].indirect(T.ix[:]), ["tf", "ix"], ["t2"])
+        cp(T.t2[:, C // 2:C], T.tf[:].indirect(T.ix[:, 10:20]), ["tf", "ix"], ["t2b"])
         tt(T.lv[:], T.sh[:], T.cf[:], A.add, ["sh", "cf"], ["lv"])
-        scan(T.tsel[:], T.dsel[:], T.t2[:], 0.0, A.add, A.max, ["dsel", "t2"], ["tsel"])
+        scan(T.tsel[:], T.dsel[:], T.t2[:], 0.0, A.add, A.max, ["dsel", "t2a", "t2b"], ["tsel"])
         tt(T.ha[:], T.tsel[:, 15:C:16], T.ik[:], A.add, ["tsel", "ik"], ["ha"])
         tt(T.hh[:], T.ha[:], T.lv[:], A.max, ["ha", "lv"], ["hh"])
         for b in (2, 0, 3, 1):

@@ -2,31 +2,37 @@ from concourse.mybir import dt, AluOpType as A, ActivationFunctionType as F
 
 C, CAP, ROUNDS, STEP = 320, 96, 3, [1, 2, 1]
 CUT = [0, 192, C]
-TAB, WIN = 344, 664
+WCUT = [0, 176, C]
+KS = [(0, 1, 2), (3, 4)]
+SEG = [CUT[1] // 4 + 1, C // 4 + 1]
+TAB, WIN = 260, 584
+HOLD, LIFT = 1024.0, 1024.0
 BASE = 14212656.0
 A0 = 0.75 + 9 * 2.0 ** -24
 B0 = (11184811 - 9) * 2.0 ** -23
 B1 = 1.0 - 2.0 ** -24
+TINY = 2.0 ** -40
+NONE = (B1 - B0) / TINY
 X4, U8, U16, I32, F32, BF, H16 = "float8_e4m3fn_x4", "uint8", "uint16", "int32", "float32", "bfloat16", "float16"
 
 
 def _scratch():
     s = {}
     for t in range(ROUNDS + 1):
-        for n, w, d in [("win", 12 * C if t < ROUNDS else 4 * C, BF), ("qx", C, X4), ("sx", C, U8)]:
+        for n, w, d in [("xt", 4 * C, BF), ("win", 12 * C, BF), ("qx", C, X4), ("sx", C, U8)]:
             s["%s%d" % (n, t)] = ("sbuf", [128, w], d)
     for t in range(ROUNDS):
-        for n, w, d in [("lq", C, X4), ("lsc", C, U8), ("wd", 20, U16), ("lw", 20, U16), ("tb", WIN, F32), ("tm", WIN, F32),
+        for n, w, d in [("lq", C, X4), ("lsc", C, U8), ("wd", 32, U16), ("lw", 32, U16), ("tm", WIN, F32),
                         ("gt", 4 * C, BF), ("qg", C, X4), ("sg", C, U8)]:
             s["%s%d" % (n, t)] = ("sbuf", [128, w], d)
     for d, names in [
-        (BF, "ut 512 vt 512 ones 516 z0 516 z1 516 dw 672 db 640 dsel 320 dd 400 bits 648 eqm 400 dscan 400 x1 20 g64 1280 rr 1280"),
+        (BF, "ut 512 vt 512 ones 516 z0 516 z1 516 dw 672 db 640 dsel 320 dd 312 bits 648 wscan 648 bscan 640 x1 20 g64 1280"),
         (X4, "uq 128 up 256 vq 128 wq 512 eq 512"), (U8, "usc 128 ups 256 vsc 128 wsc 512 esc 512"),
-        (I32, "i_u 16 i_e 16 i_p 22 e16 16 j22 22"), (U16, "uo 16 jo 22 ofu 8 ix 20 gl 80 ho 20"),
-        (H16, "wscan 648 bscan 640 t2 320 tsel 320"),
-        (F32, "k16 20 k64 8 src_m 80 src_b 80 jf 4 j4 4 kp 4 bk 4 tiny 4 pa 16 pb 16 pc 16 pd 16 pw 16 pe 16 pf 16 pt 16 m0 16 sl 8 "
-              "cf 20 cb 20 ck 20 hv 960 vv 20 wsel 80 wk 8 of 8 al 320 be 320 tf 320 st 324 ssel 320 ll 20 y2 20 ik 20 sh 20 lv 20 "
-              "ha 20 hh 20 hf 320 yo 320"),
+        (I32, "i_u 16 i_e 16 i_p 22 e16 16 j22 22"), (U16, "uo 16 jo 22 ofu 8 ho 20 ix 20 gl 80"),
+        (H16, "eqm 312 dscan 312 t2 320 tsel 320 dts 320"),
+        (F32, "k16 20 src_m 80 jf 8 j4 4 kp 1 kq 4 bk 1 wc0 1 fw 4 fa 4 tiny 4 pa 16 pc 16 pd 16 pw 16 po 16 pe 16 pf 16 pt 16 m0 16 sl 8 "
+              "cf 20 cx 20 ck 20 cl 20 hv 960 vv 20 wsel 80 al 320 be 320 tf 320 st 324 ssel 320 dss 320 y2 20 sh 20 lv 20 "
+              "hh 20 hf 320 yo 320"),
     ]:
         w = names.split()
         for i in range(0, len(w), 2):
@@ -36,8 +42,8 @@ def _scratch():
 
 
 SCRATCH = _scratch()
-POOL = ["s%d" % i for i in range(120)]
-SEMAPHORES = POOL + ["sent"] + ["a%s%d" % (k, t) for k in "cw" for t in range(ROUNDS)]
+POOL = ["s%d" % i for i in range(130)]
+SEMAPHORES = POOL + ["sent"] + [n % t for n in ("ac%d", "aw%d_0", "aw%d_1") for t in range(ROUNDS)]
 
 
 def _sequencer(g, T):
@@ -112,6 +118,9 @@ def rank_program(g, core, T, topo):
     def act(out, a, r, w, func=F.Copy, **kw):
         return op("a", lambda e: e.activation(out, a, func, **kw), r, w)
 
+    def times(q, out, a, c, r, w):
+        return act(out, a, r, w, scale=c) if q == "a" else ts(out, a, c, None, A.mult, None, r, w)
+
     def quant(q, s, a, r, w):
         return op("v", lambda e: e.quantize_mx(q, s, a), r, w)
 
@@ -129,250 +138,310 @@ def rank_program(g, core, T, topo):
     def bank(k, h=None):
         return T.ps[:, 512 * k:512 * k + (C if h is None else CUT[h + 1] - CUT[h])]
 
-    def part(buf, h, w=1, b=None):
-        return buf[:, w * CUT[h]:w * CUT[h + 1]] if b is None else buf[:, w * CUT[h] + b:w * CUT[h + 1]:w]
+    def part(buf, h, w=1, b=None, cut=CUT):
+        return buf[:, w * cut[h]:w * cut[h + 1]] if b is None else buf[:, w * cut[h] + b:w * cut[h + 1]:w]
 
-    def xk(t, h):
-        return ["x%d.%d.%d" % (t, h, b) for b in range(4)]
+    def plane(t, b, third, h=None):
+        lo, hi = (0, C) if h is None else CUT[h:h + 2]
+        if t == 0:
+            return T.win0[:, 4 * (C * third + lo) + b:4 * (C * third + hi):4]
+        o = 3 * C * b + C * third
+        return T["win%d" % t][:, o + lo:o + hi]
 
-    def bits_of(h):
-        act(part(T.bits, h, 2, 0), bank(2 * h, h), ["tiny"], ["ps%d" % (2 * h), "bit%d" % (2 * h)], func=F.Sign, bias=T.tiny[:, 0:1])
-        ts(part(T.bits, h, 2, 1), bank(2 * h + 1, h), 0.0, 2.0, A.is_gt, A.add, [], ["ps%d" % (2 * h + 1), "bit%d" % (2 * h + 1)])
+    def tile_x(t):
+        return T["xt%d" % t] if t else T.win0
 
-    def blocks_of(h):
-        scan(part(T.bscan, h, 2), part(T.db, h, 2), part(T.bits, h, 2), 0.0, A.mult, A.add,
-             ["db%d" % i for i in range(5)] + ["bit%d" % (2 * h), "bit%d" % (2 * h + 1)], ["bscan%d" % h])
+    def keys(n, t, h):
+        return ["%s%d.%d.%d" % (n, t, h, b) for b in range(4)]
+
+    def seg(h):
+        o = h * len(KS[0]) * SEG[0]
+        return o, o + len(KS[h]) * SEG[h]
+
+    sent = [0]
+
+    def send(t, out, src, sem, r):
+        peer = T.cores[rank ^ STEP[t]]
+        rid, pid = topo.addr(peer)[0:2]
+        need("g", r, [])
+        g.remote_dma(out, src, T.sem[sem], T.sem.sent, pid, rid, topo.mask(core, peer))
+        sent[0] += len(topo.engines(core, peer))
 
     def quant_x(t, h):
-        quant(part(T["qx%d" % t], h), part(T["sx%d" % t], h), part(T["win%d" % t], h, 4), xk(t, h), ["qx%d.%d" % (t, h)])
+        qx, sx, k = T["qx%d" % t], T["sx%d" % t], "qx%d.%d" % (t, h)
+        quant(part(qx, h), part(sx, h), part(tile_x(t), h, 4), keys("x", t, h), [k])
+        if t == ROUNDS:
+            return
+        ne = len(topo.engines(core, T.cores[rank ^ STEP[t]]))
+        arrives("lq%d" % t, "ac%d" % t, 3 * ne)
+        arrives("lw%d.%d" % (t, h), "aw%d_%d" % (t, h), ne)
+        send(t, part(T["lq%d" % t], h).bitcast(u8), part(qx, h).bitcast(u8), "ac%d" % t, [k])
+        if h:
+            send(t, T["lsc%d" % t][:], sx[:], "ac%d" % t, [k])
+        for i in range(2):
+            by_x(2 * h + i, T.up[:, 128 * i:128 * i + 128], T.ups[:, 128 * i:128 * i + 128], ["up%d" % i, "ups%d" % i], t, h)
+
+    def signs(h):
+        for i in range(2):
+            act(part(T.bits, h, 2, i), bank(2 * h + i, h), ["tiny"], ["ps%d" % (2 * h + i), "bit%d" % (2 * h + i)], func=F.Sign, bias=T.tiny[:, 0:1])
 
     def quant_e(b):
         o = 2 - b // 2 * 2
         quant(T.eq[:, 128 * b:128 * b + 128], T.esc[:, 128 * b:128 * b + 128], T["z%d" % (b % 2)][:, o:o + 512], ["z%d" % (b % 2)], ["eq%d" % b])
 
-    def by_x(k, q, sc, keys, t, h):
-        mm(bank(k, h), q, sc, part(T["qx%d" % t], h), part(T["sx%d" % t], h), keys + ["qx%d.%d" % (t, h)], ["ps%d" % k])
+    def by_x(k, q, sc, ks, t, h):
+        mm(bank(k, h), q, sc, part(T["qx%d" % t], h), part(T["sx%d" % t], h), ks + ["qx%d.%d" % (t, h)], ["ps%d" % k])
 
     def fill(t):
-        act(T["tb%d" % t][:, 0:TAB], T.ones[:, 0:TAB], ["ones"], ["tb%d" % t], scale=B0)
-        act(T["tm%d" % t][:, 0:TAB], T.ones[:, 0:TAB], ["ones"], ["tm%d" % t], scale=0.0)
+        op("g", lambda e: e.affine_select(T["tm%d" % t][:, 0:TAB], T.ones[:, 0:TAB], [[0, TAB]], A.is_equal, NONE, 1, 0), ["ones"], ["tm%d" % t])
+
+    def words(t, h):
+        a, b, n = 2 * CUT[h], 2 * CUT[h + 1] + 8 * h, (WCUT[h + 1] - WCUT[h]) // 16
+        o, wd = 2 * WCUT[h], T["wd%d" % t][:, 16 * h:16 * h + n]
+        bit = ["bit%d" % (2 * h), "bit%d" % (2 * h + 1)]
+        return [
+            lambda: scan(T.wscan[:, a:b], T.dw[:, a:b], T.bits[:, a:b], T.wscan[:, a - 1:a] if h else 0.0, A.mult, A.add,
+                         ["dw0", "dw1", "bitp", "wscan0"][:3 + h] + bit, ["wscan%d" % h]),
+            lambda: tt(T.vv[:, 0:n], T.wscan[:, o + 31:o + 32 * n:32], T.wscan[:, o + 39:o + 32 * n + 8:32], A.add, ["wscan0", "wscan%d" % h], ["vv"]),
+            lambda: (ts(wd, T.vv[:, 0:n], T.fw[:, 0:1], 128.5, A.mult, A.add, ["vv", "fw"], ["wd%d.%d" % (t, h)]),
+                     send(t, T["lw%d" % t][:, 16 * h:16 * h + n], wd, "aw%d_%d" % (t, h), ["wd%d.%d" % (t, h)])),
+        ]
+
+    def table(t, h):
+        (o, e), n, k0 = seg(h), SEG[h], KS[h][0]
+        a, b = CUT[h] // 4, CUT[h + 1] // 4
+        blocks = ["bscan0", "bscan%d" % h]
+
+        def equal():
+            act(T.eqm[:, o + b:e:n], T.wsel[:, a + 15:b:16], ["wsel%d" % h, "wc0"], ["wk%d" % h], func=F.Identity, scale=0.5, bias=T.wc0[:, 0:1])
+            for k in KS[h]:
+                ts(T.eqm[:, o + n * (k - k0):o + n * (k - k0) + b], T.bscan[:, 7:8 * b:8], T.kp[:, 0:1], T.wsel[:, 16 * k + 15:16 * k + 16],
+                   A.add, A.is_equal, blocks + ["wsel%d" % h, "kp"], ["eqm%d" % k])
+        return [
+            lambda: scan(part(T.bscan, h, 2), part(T.db, h, 2), part(T.bits, h, 2), 0.0, A.mult, A.add,
+                         ["db", "bit%d" % (2 * h), "bit%d" % (2 * h + 1)], ["bscan%d" % h]),
+            lambda: scan(T.wsel[:, a:b], T.bscan[:, 8 * a + 7:8 * b:8], T.dsel[:, a:b], -4 * LIFT, A.max, A.add, ["dsel", "bscan%d" % h], ["wsel%d" % h]),
+            equal,
+            lambda: scan(T.dscan[:, o:e], T.dd[:, o:e], T.eqm[:, o:e], 0.0, A.mult, A.max,
+                         ["dd", "wk%d" % h] + ["eqm%d" % k for k in KS[h]], ["dscan%d" % h]),
+            lambda: cp(T.ofu[:, k0:k0 + len(KS[h])], T.dscan[:, o + b:e:n], ["dscan%d" % h], ["ofu%d" % h]),
+        ]
+
+    def evac(t, b):
+        times("a", plane(t, b, 1), bank(4 + b), 64.0 if t else 1.0, [], ["ps%d" % (4 + b), "d%d.%d" % (t, b)])
+
+    def again(t, b):
+        if t:
+            act(plane(t, b, 2), plane(t, b, 0), [keys("y", t, h)[b] for h in range(2)], ["yc%d.%d" % (t, b)])
 
     dma("a", T.ut[:], T.u[:], [], ["ut"])
     for h in range(2):
-        dma("s", part(T.win0, h, 4), part(T.x, h, 4), [], xk(0, h))
+        dma("s", part(T.win0, h, 4), part(T.x, h, 4), [], keys("x", 0, h) + keys("y", 0, h))
     dma("s", T.wq[:].bitcast(u8), T.wc[:], [], ["wq"])
     dma("s", T.wsc[:], T.ws[:], [], ["wsc"])
-    dma("s", T.vt[:], T.v[:], [], ["vt"])
 
     iota(T.i_p[:], [[0, 22]], 0, 1, ["i_p"])
     iota(T.i_e[:], [[1, 16]], 128, -1, ["i_e"])
     iota(T.i_u[:], [[1, 2], [16, 8]], 0, 0, ["i_u"])
     iota(T.k16[:], [[16, 20]], 0, 0, ["k16"], True)
-    iota(T.k64[:], [[64, 8]], TAB - 1, 0, ["k64"], True)
-    iota(T.src_m[:], [[4, 80]], 2 * C, 0, ["sm0"], True)
     ms(T.ones[:], 1.0, ["ones"])
-    ms(T.dw[:, 1:672:2], 1.0, ["dw1"])
-    ms(T.bits[:, 640:648], 1.0, ["bitp"])
     ms(T.tiny[:], -2.0 ** -120, ["tiny"])
+    ms(T.db[:], 2.0, ["db"])
     ms(T.dd[:], 1.0, ["dd"])
     op("g", lambda e: e.affine_select(T.z1[:], T.ones[:], [[-1, 516]], A.is_equal, 0.0, 3, 4), ["ones"], ["z1"])
+    fill(0)
+    iota(T.src_m[:], [[4, 80]], 2 * C, 0, ["src_m"], True)
     ts(T.j22[:], T.i_p[:], 15, None, A.bitwise_and, None, ["i_p"], ["j22"])
     ts(T.e16[:], T.i_e[:], 15, None, A.bitwise_and, None, ["i_e"], ["e16"])
-    cp(T.uo[:], T.i_u[:], ["i_u"], ["uo"])
+    ms(T.db[:, 0:640:8], 0.0, ["db"])
     cp(T.jo[:], T.j22[:], ["j22"], ["jo"])
-    ts(T.pa[:], T.e16[:], 4.0, 124.0, A.is_equal, A.mult, ["e16"], ["pa"])
-    ts(T.pb[:], T.e16[:], 1.0, 4.0, A.min, A.mult, ["e16"], ["pb"])
-    ts(T.pc[:], T.e16[:], 4.0, -3.0, A.is_gt, A.mult, ["e16"], ["pc"])
-    ts(T.pe[:], T.e16[:], 0.0, -4096.0, A.is_equal, A.mult, ["e16"], ["pe"])
-    ts(T.pf[:], T.e16[:], 1.0, 1024.0, A.is_equal, A.mult, ["e16"], ["pf"])
-    tt(T.pd[:], T.pa[:], T.pb[:], A.add, ["pa", "pb"], ["pd"])
-    cp(T.jf[:], T.j22[:, 0:4], ["j22"], ["jf"])
+    ts(T.po[:], T.e16[:], 3.5, 1.0, A.is_lt, A.add, ["e16"], ["po"])
+    ts(T.pa[:], T.e16[:], 4.0, HOLD - 1, A.is_equal, A.mult, ["e16"], ["pa"])
+    ts(T.pc[:], T.e16[:], 0.0, -2.0, A.is_equal, A.mult, ["e16"], ["pc"])
+    ts(T.pe[:], T.e16[:], 0.0, LIFT, A.is_equal, A.mult, ["e16"], ["pe"])
+    ts(T.pf[:], T.e16[:], 15.0, -2 * LIFT, A.is_equal, A.mult, ["e16"], ["pf"])
+    tt(T.pd[:], T.pa[:], T.pc[:], A.add, ["pa", "pc"], ["pd"])
+    cp(T.jf[:], T.j22[:, 0:8], ["j22"], ["jf"])
     tt(T.pt[:], T.pe[:], T.pf[:], A.add, ["pe", "pf"], ["pt"])
-    tt(T.pw[:], T.pd[:], T.pc[:], A.add, ["pd", "pc"], ["pw"])
-    fill(0)
+    cp(T.uo[:], T.i_u[:], ["i_u"], ["uo"])
+    tt(T.pw[:], T.pd[:], T.po[:], A.add, ["pd", "po"], ["pw"])
+    act(T.dw[:, 1:672:2], T.po[:].indirect(T.jo[:, 0:21]), ["po", "jo"], ["dw1"])
     act(T.dw[:, 0:672:2], T.pw[:].indirect(T.jo[:, 0:21]), ["pw", "jo"], ["dw0"])
     act(T.dsel[:], T.pt[:].indirect(T.jo[:, 0:20]), ["pt", "jo"], ["dsel"])
+    act(T.fa[:], T.jf[:, 0:4], ["jf"], ["fa"], func=F.Square, bias=-7.5)
     ts(T.m0[:], T.e16[:], 0.0, None, A.is_equal, None, ["e16"], ["m0"])
-    ts(T.j4[:], T.jf[:], 4.0, None, A.mult, None, ["jf"], ["j4"])
-    ts(T.kp[:], T.jf[:], 15.0, 1024.0, A.is_lt, A.mult, ["jf"], ["kp"])
-    ms(T.src_b[:], B1, ["src_b"])
-    ts(T.sl[:], T.k64[:], T.j4[:, 0:1], None, A.add, None, ["k64", "j4"], ["sl"])
-    ms(T.db[:, 1:640:2], 1.0, ["db0"])
-    ms(T.db[:, 0:640:8], 0.0, ["db1"])
-    for i in range(3):
-        ms(T.db[:, 2 + 2 * i:640:8], 4.0, ["db%d" % (i + 2)])
+    ts(T.j4[:], T.jf[:, 0:4], 4.0, TAB - 1.0, A.mult, A.add, ["jf"], ["j4"])
+    ts(T.kp[:], T.pt[:, 15:16], LIFT, LIFT, A.add, A.min, ["pt"], ["kp"])
+    ts(T.bits[:, 640:648], T.jf[:], 12.5, -2.0 ** 20, A.is_gt, A.mult, ["jf"], ["bitp"])
+    ts(T.sl[:, 0:5], T.k16[:, 0:5], 4.0, T.j4[:, 0:1], A.mult, A.add, ["k16", "j4"], ["sl"])
+    ts(T.cf[:], T.k16[:], T.jf[:, 0:1], None, A.add, None, ["k16", "jf"], ["cf"])
+    ts(T.bk[:], T.jf[:, 0:1], 14.5, LIFT, A.is_lt, A.mult, ["jf"], ["bk"])
 
     quant(T.uq[:], T.usc[:], T.ut[:], ["ut"], ["uq"])
-    act(T.ups[:], T.usc[:].indirect(T.uo[:]), ["uq", "uo"], ["ups"])
+    ts(T.wc0[:], T.kp[:], -0.5, 128.5, A.mult, A.add, ["kp"], ["wc0"])
+    for i in range(2):
+        o = T.uo[:, 8 * i:8 * i + 8]
+        act(T.ups[:, 128 * i:128 * i + 128], T.usc[:].indirect(o), ["uq", "uo"], ["ups%d" % i])
+        cp(T.up[:, 128 * i:128 * i + 128].bitcast(u32), T.uq[:].bitcast(u32).indirect(o), ["uq", "uo"], ["up%d" % i])
     for h in range(2):
-        quant_x(0, h)
-    cp(T.up[:].bitcast(u32), T.uq[:].bitcast(u32).indirect(T.uo[:]), ["uq", "uo"], ["up"])
-    ts(T.dw[:, 642:648:2], T.dw[:, 642:648:2], 4.0, None, A.min, None, ["dw0"], ["dw0"])
+        for k in KS[h]:
+            o = seg(h)[0] + SEG[h] * (k - KS[h][0]) + 16 * k
+            act(T.dd[:, o:o + 16], T.m0[:], ["m0", "sl", "dd"], ["dd%d" % k], func=F.Identity, scale=T.sl[:, k:k + 1], bias=1.0)
+    quant_x(0, 0)
+    signs(0)
+    ts(T.fw[:], T.fa[:], 16.0, 1.0, A.is_gt, A.add, ["fa"], ["fw"])
+    quant_e(1)
+    quant_x(0, 1)
+    signs(1)
+    ts(T.fw[:], T.fw[:], 0.25 / HOLD, None, A.mult, None, ["fw"], ["fw"])
+    for h in range(2):
+        ms(T.dd[:, seg(h)[0]:seg(h)[1]:SEG[h]], 0.0, ["dd"] + ["dd%d" % k for k in KS[h]])
+    quant_e(3)
+    act(T.z0[:, 0:514], T.z1[:, 1:515], ["z1"], ["z0"])
+    act(T.dss[:], T.dsel[:], ["dsel"], ["dss"])
+    act(T.dts[:], T.dsel[:], ["dsel"], ["dts"])
+    act(T.cx[:], T.cf[:], ["cf"], ["cx"], func=F.Identity, bias=574.5)
+    act(T.cl[:], T.cf[:], ["cf", "kp"], ["cl"], func=F.Identity, bias=T.kp[:, 0:1])
+    act(T.kq[:], T.k16[:, 0:4], ["k16", "kp"], ["kq"], func=F.Identity, scale=-1.0 / 64, bias=T.kp[:, 0:1])
+    once = [
+        lambda: quant_e(0),
+        lambda: quant_e(2),
+        lambda: ts(T.dss[:, 15:C:16], T.cf[:], BASE, T.bk[:, 0:1], A.subtract, A.subtract, ["cf", "bk"], ["dss"]),
+        lambda: ms(T.st[:, 0:1], BASE, ["st0"]),
+        lambda: ts(T.ck[:], T.cf[:], 576.0, T.pt[:, 15:16], A.add, A.add, ["cf", "pt"], ["ck"]),
+        lambda: None,
+        lambda: quant(T.vq[:], T.vsc[:], T.vt[:], ["vt"], ["vq"]),
+    ]
 
-    sent = [0]
+    def gap():
+        if once:
+            once.pop(0)()
+
     for t in range(ROUNDS):
-        win, nxt = T["win%d" % t], T["win%d" % (t + 1)]
-        qx, sx, lq, lsc, wd, lw = [T["%s%d" % (n, t)] for n in ("qx", "sx", "lq", "lsc", "wd", "lw")]
-        tb, tm, gt, qg, sg = [T["%s%d" % (n, t)] for n in ("tb", "tm", "gt", "qg", "sg")]
-        peer = T.cores[rank ^ STEP[t]]
-        rid, pid = topo.addr(peer)[0:2]
-        mask, ne = topo.mask(core, peer), len(topo.engines(core, peer))
-
-        def send(out, src, sem, r):
-            need("g", r, [])
-            g.remote_dma(out, src, T.sem[sem], T.sem.sent, pid, rid, mask)
-            sent[0] += ne
-        arrives("lq%d" % t, "ac%d" % t, 2 * ne)
-        arrives("lw%d" % t, "aw%d" % t, ne)
+        lw, tm, gt, qg, sg = [T["%s%d" % (n, t)] for n in ("lw", "tm", "gt", "qg", "sg")]
         K = lambda n: "%s%d" % (n, t)
-        qk = ["qx%d.%d" % (t, h) for h in range(2)]
 
-        send(lq[:].bitcast(u8), qx[:].bitcast(u8), K("ac"), qk)
-        if t > 0:
-            send(lsc[:], sx[:], K("ac"), qk)
-        for h in range(2):
-            for i in range(2):
-                by_x(2 * h + i, T.up[:, 128 * i:128 * i + 128], T.ups[:, 128 * i:128 * i + 128], ["up", "ups"], t, h)
+        w0, w1, t0, t1 = words(t, 0), words(t, 1), table(t, 0), table(t, 1)
+        again(t, 0)
+        for step in [w0[0], t0[0], w0[1], t0[1], w0[2], w1[0], t1[0], w1[1], t1[1], w1[2], t0[2], t1[2], t0[3], t1[3], t0[4], t1[4], gap]:
+            step()
+        cp(tm[:].indirect(T.ofu[:, 0:5]), T.src_m[:], ["ofu0", "ofu1", "src_m"], [K("tm")])
         if t == 0:
-            quant_e(1)
-            quant_e(3)
-        bits_of(0)
-        bits_of(1)
-        blocks_of(0)
-        scan(T.wscan[:], T.dw[:, 0:648], T.bits[:], 0.0, A.mult, A.add, ["dw0", "dw1", "bitp"] + ["bit%d" % i for i in range(4)], ["wscan"])
-        blocks_of(1)
-        tt(T.vv[:], T.wscan[:, 31:648:32], T.wscan[:, 39:648:32], A.max, ["wscan"], ["vv"])
-        scan(T.wsel[:], T.dsel[:, 0:80], T.bscan[:, 7:640:8], 0.0, A.add, A.max, ["dsel", "bscan0", "bscan1"], ["wsel"])
-        ts(wd[:], T.vv[:], 16.0, 2.0 ** -7, A.subtract, A.mult, ["vv"], [K("wd")])
-        send(lw[:], wd[:], K("aw"), [K("wd")])
-        if t == 0:
-            send(lsc[:], sx[:], K("ac"), qk)
-            for k in range(5):
-                act(T.dd[:, 96 * k:96 * k + 16], T.m0[:], ["m0", "sl", "dd"], ["dd%d" % k], func=F.Identity, scale=T.sl[:, k:k + 1], bias=1.0)
-            act(T.z0[:, 0:514], T.z1[:, 1:515], ["z1"], ["z0"])
-            iota(T.hv[:, 0:2 * C], [[1, 2 * C]], 0, 0, ["hv0"], True)
-            iota(T.hv[:, 2 * C:3 * C], [[1, C]], 0, 0, ["hv1"], True)
-        act(win[:, 8 * C:12 * C], win[:, 0:4 * C], xk(t, 0) + xk(t, 1), [K("xc")])
+            dma("s", T.win0[:, 8 * C:12 * C], T.x[:], ["lw0.1"], ["yc0.%d" % b for b in range(4)])
+            dma("s", T.vt[:], T.v[:], [], ["vt"])
+        for b in range(1, 4):
+            again(t, b)
         if t + 1 < ROUNDS:
             fill(t + 1)
-
-        if t == 0:
-            ms(T.dd[:, 0:400:80], 0.0, ["dd"] + ["dd%d" % k for k in range(5)])
-        for k in range(5):
-            ts(T.eqm[:, 80 * k:80 * k + 80], T.bscan[:, 7:640:8], T.kp[:, 0:1], T.wsel[:, 16 * k + 15:16 * k + 16], A.add, A.is_equal,
-               ["bscan0", "bscan1", "wsel", "kp"], ["eqm%d" % k])
-        ts(T.wk[:, 0:5], T.wsel[:, 15:80:16], T.kp[:, 0:1], None, A.subtract, None, ["wsel", "kp"], ["wk"])
-        scan(T.dscan[:], T.dd[:], T.eqm[:], 0.0, A.mult, A.max, ["dd"] + ["eqm%d" % k for k in range(5)], ["dscan"])
-        if t == 0:
-            ts(T.cf[:], T.k16[:], T.jf[:, 0:1], None, A.add, None, ["k16", "jf"], ["cf"])
-        tt(T.of[:, 0:5], T.dscan[:, 79:400:80], T.wk[:, 0:5], A.max, ["dscan", "wk"], ["of"])
-        if t == 0:
-            ts(T.bk[:], T.kp[:], BASE, None, A.add, None, ["kp"], ["bk"])
-        cp(T.ofu[:, 0:5], T.of[:, 0:5], ["of"], ["ofu"])
-        if t == 0:
-            ms(T.st[:, 0:1], BASE, ["st0"])
-        cp(tb[:].indirect(T.ofu[:, 0:5]), T.src_b[:], ["ofu", "src_b"], [K("tb")])
-        cp(tm[:].indirect(T.ofu[:, 0:5]), T.src_m[:], ["ofu", "sm0"], [K("tm")])
-        if t == 0:
-            quant_e(0)
-            quant_e(2)
-            ts(T.ck[:], T.cf[:], 576.0, T.kp[:, 0:1], A.add, A.subtract, ["cf", "kp"], ["ck"])
-            ts(T.cb[:], T.cf[:], -1.0, T.bk[:, 0:1], A.mult, A.add, ["cf", "bk"], ["cb"])
-
-        def evac(b):
-            act(win[:, 4 * C + b:8 * C:4], bank(4 + b), [], ["ps%d" % (4 + b), "d%d.%d" % (t, b)])
-        for h in range(2):
-            o = lw[:, CUT[h] // 16:CUT[h + 1] // 16]
-            act(part(T.be, h), tb[:, 0:TAB].indirect(o), [K("tb"), K("lw")], ["be%d" % h])
-            ts(part(T.al, h), tb[:, 0:TAB].indirect(o), 1.0, A0, A.is_lt, A.max, [K("tb"), K("lw")], ["al%d" % h])
-        act(T.tf[:], tm[:, 0:TAB].indirect(lw[:]), [K("tm"), K("lw")], ["tf"])
+        if t == 1:
+            iota(T.hv[:, 0:2 * C], [[1, 2 * C]], 0, 0, ["hv0"], True)
+            iota(T.hv[:, 2 * C:3 * C], [[1, C]], 0, 0, ["hv1"], True)
+        gap()
         for b in range(4):
-            mm(bank(4 + b), T.eq[:, 128 * b:128 * b + 128], T.esc[:, 128 * b:128 * b + 128], lq[:], lsc[:], ["eq%d" % b, K("lq")], ["ps%d" % (4 + b)])
-        evac(0)
-        evac(1)
-        m = CUT[1]
-        scan(T.st[:, 1:m + 1], part(T.al, 0), part(T.be, 0), BASE, A.mult, A.mult, ["al0", "be0"], ["sta"])
-        scan(T.st[:, m + 1:C + 1], part(T.al, 1), part(T.be, 1), T.st[:, m:m + 1], A.mult, A.mult, ["al1", "be1", "sta"], ["stb"])
-        scan(part(T.ssel, 0), part(T.dsel, 0), part(T.st, 0), 0.0, A.add, A.max, ["dsel", "sta", "st0"], ["ssela"])
-        scan(part(T.ssel, 1), part(T.dsel, 1), part(T.st, 1), 0.0, A.add, A.max, ["dsel", "sta", "stb"], ["ssel"])
-        sv = T.ssel[:, 15:C:16]
-        ts(T.x1[:], sv, T.bk[:, 0:1], 574.5, A.subtract, A.subtract, ["ssel", "ssela", "bk"], ["x1"])
-        tt(T.ll[:], sv, T.cb[:], A.subtract, ["ssel", "ssela", "cb"], ["ll"])
-        tt(T.y2[:], T.ll[:], T.x1[:], A.subtract, ["ll", "x1"], ["y2"])
-        ts(T.sh[:], T.ll[:], CAP - 0.5, float(C), A.is_lt, A.mult, ["ll"], ["sh"])
+            mm(bank(4 + b), T.eq[:, 128 * b:128 * b + 128], T.esc[:, 128 * b:128 * b + 128], T[K("lq")][:], T[K("lsc")][:], ["eq%d" % b, K("lq")], ["ps%d" % (4 + b)])
+
+        look = [tm[:, 0:TAB].indirect(lw[:, 16 * h:16 * h + (WCUT[h + 1] - WCUT[h]) // 16]) for h in range(2)]
+        lk = [[K("tm"), "lw%d.%d" % (t, h)] for h in range(2)]
+        m = WCUT[1]
+        for h in range(2):
+            act(part(T.be, h, cut=WCUT), look[h], lk[h], ["be%d" % h], func=F.Identity, scale=-TINY, bias=B1)
+            ts(part(T.al, h, cut=WCUT), look[h], 0.0, A0, A.is_gt, A.max, lk[h], ["al%d" % h])
+        for h in range(2):
+            act(part(T.tf, h, cut=WCUT), look[h], lk[h], ["tf%d" % h], func=F.Relu)
+            scan(T.st[:, WCUT[h] + 1:WCUT[h + 1] + 1], part(T.al, h, cut=WCUT), part(T.be, h, cut=WCUT), T.st[:, m:m + 1] if h else BASE,
+                 A.mult, A.mult, ["al%d" % h, "be%d" % h, "st1"][:2 + h], ["st%d" % (h + 1)])
+            if h == 0:
+                gap()
+                gap()
+        for h in range(2):
+            scan(part(T.ssel, h, cut=WCUT), part(T.st, h, cut=WCUT), part(T.dss, h, cut=WCUT), 0.0, A.max, A.add,
+                 ["dss", "st%d" % h, "st%d" % (h + 1)], ["ssel%d" % h])
+        evac(t, 0)
+        evac(t, 1)
+        gap()
+        ll, sk = T.ssel[:, 15:C:16], ["ssel0", "ssel1"]
+        tt(T.x1[:], ll, T.cx[:], A.subtract, sk + ["cx"], ["x1"])
+        ts(T.sh[:], ll, CAP - 0.5, float(C), A.is_lt, A.mult, sk, ["sh"])
+        tt(T.y2[:], ll, T.x1[:], A.subtract, sk + ["x1"], ["y2"])
+        tt(T.lv[:], T.sh[:], T.cl[:], A.add, ["sh", "cl"], ["lv"])
         ts(T.ix[:], T.y2[:], 576.0, None, A.subtract, None, ["y2"], ["ix"])
-        act(T.t2[:, 0:C // 2], T.tf[:].indirect(T.ix[:, 0:10]), ["tf", "ix"], ["t2a"])
-        evac(2)
-        evac(3)
-        tt(T.ik[:], T.ck[:], T.y2[:], A.subtract, ["ck", "y2"], ["ik"])
-        cp(T.t2[:, C // 2:C], T.tf[:].indirect(T.ix[:, 10:20]), ["tf", "ix"], ["t2b"])
-        tt(T.lv[:], T.sh[:], T.cf[:], A.add, ["sh", "cf"], ["lv"])
-        scan(T.tsel[:], T.dsel[:], T.t2[:], 0.0, A.add, A.max, ["dsel", "t2a", "t2b"], ["tsel"])
-        tt(T.ha[:], T.tsel[:, 15:C:16], T.ik[:], A.add, ["tsel", "ik"], ["ha"])
-        tt(T.hh[:], T.ha[:], T.lv[:], A.max, ["ha", "lv"], ["hh"])
-        for b in (2, 0, 3, 1):
-            ts(T.gl[:, 20 * b:20 * b + 20], T.hh[:], 4.0, float(b), A.mult, A.add, ["hh"], ["gl%d" % b])
+        act(T.t2[:, 0:C // 2], T.tf[:].indirect(T.ix[:, 0:10]), ["tf0", "tf1", "ix"], ["t2a"])
+        evac(t, 2)
+        evac(t, 3)
+        tt(T.dts[:, 15:C:16], T.ck[:], T.y2[:], A.subtract, ["ck", "y2"], ["dts"])
+        cp(T.t2[:, C // 2:C], T.tf[:].indirect(T.ix[:, 10:20]), ["tf0", "tf1", "ix"], ["t2b"])
+        gap()
+        scan(T.tsel[:], T.t2[:], T.dts[:], 0.0, A.max, A.add, ["dts", "t2a", "t2b"], ["tsel"])
+        tt(T.hh[:], T.tsel[:, 15:C:16], T.lv[:], A.max, ["tsel", "lv"], ["hh"])
+        if t:
+            ts(T.ho[:], T.hh[:], T.kp[:, 0:1], None, A.subtract, None, ["hh", "kp"], ["ho"])
+        else:
+            for b in (0, 2, 1, 3):
+                ts(T.gl[:, 20 * b:20 * b + 20], T.hh[:], T.kq[:, b:b + 1], 4.0, A.subtract, A.mult, ["hh", "kq"], ["gl%d" % b])
 
-        src = xk(t, 0) + xk(t, 1) + [K("xc")] + ["d%d.%d" % (t, b) for b in range(4)]
-        gk = [["g%d.%d.%d" % (t, h, b) for b in range(4)] for h in range(2)]
-
-        def gather(h, b, fn):
-            fn(part(gt, h, 4, b), win[:].indirect(T.gl[:, 20 * b + CUT[h] // 16:20 * b + CUT[h + 1] // 16]), src + ["gl%d" % b], [gk[h][b]])
+        def gather(h, b, q):
+            lo, hi = CUT[h] // 16, CUT[h + 1] // 16
+            src = lambda i: [keys("y", t, 0)[i], keys("y", t, 1)[i], "d%d.%d" % (t, i), "yc%d.%d" % (t, i)]
+            if t:
+                times(q, part(gt, h, 4, b), T[K("win")][:, 3 * C * b:3 * C * (b + 1)].indirect(T.ho[:, lo:hi]), 2.0 ** -6, src(b) + ["ho"], [keys("g", t, h)[b]])
+            else:
+                times(q, part(gt, h, 4, b), T.win0[:].indirect(T.gl[:, 20 * b + lo:20 * b + hi]), 1.0, sum(map(src, range(4)), ["gl%d" % b]), [keys("g", t, h)[b]])
 
         def layer(h):
-            quant(part(qg, h), part(sg, h), part(gt, h, 4), gk[h], ["qg%d.%d" % (t, h)])
+            quant(part(qg, h), part(sg, h), part(gt, h, 4), keys("g", t, h), ["qg%d.%d" % (t, h)])
             for b in range(4):
                 mm(bank(4 * h + b, h), T.wq[:, 128 * b:128 * b + 128], T.wsc[:, 128 * b:128 * b + 128], part(qg, h), part(sg, h),
                    ["wq", "wsc", "qg%d.%d" % (t, h)], ["ps%d" % (4 * h + b)])
 
+        def lift(h, q):
+            times(q, part(T.g64, h, 4), part(gt, h, 4), 64.0, keys("g", t, h), ["g64.%d" % h])
+
         def add(h, b):
-            tt(part(T.rr, h, 4, b), bank(4 * h + b, h), part(T.g64, h, 4, b), A.add, ["g64.%d" % h], ["ps%d" % (4 * h + b), "r%d.%d" % (h, b)])
+            tt(plane(t + 1, b, 0, h), bank(4 * h + b, h), part(T.g64, h, 4, b), A.add, ["g64.%d" % h], ["ps%d" % (4 * h + b), keys("y", t + 1, h)[b]])
 
         def scale(h, b, q):
-            if q == "a":
-                act(part(nxt, h, 4, b), part(T.rr, h, 4, b), ["r%d.%d" % (h, b)], [xk(t + 1, h)[b]], scale=2.0 ** -6)
-            else:
-                ts(part(nxt, h, 4, b), part(T.rr, h, 4, b), 2.0 ** -6, None, A.mult, None, ["r%d.%d" % (h, b)], [xk(t + 1, h)[b]])
-        for h in range(2):
-            gather(h, 2, act)
-            gather(h, 3, act)
-        gather(0, 0, cp)
-        gather(0, 1, cp)
-        if t == ROUNDS - 1:
-            cp(T.ho[:], T.hh[:], ["hh"], ["ho"])
+            times(q, part(T["xt%d" % (t + 1)], h, 4, b), plane(t + 1, b, 0, h), 2.0 ** -6, [keys("y", t + 1, h)[b]], [keys("x", t + 1, h)[b]])
+        for h, b, q in [(0, 0, "v"), (0, 2, "a"), (0, 1, "v"), (0, 3, "a"), (1, 0, "a"), (1, 1, "a"), (1, 2, "a"), (1, 3, "a")]:
+            gather(h, b, q)
         layer(0)
-        gather(1, 0, cp)
-        gather(1, 1, act)
-        ts(part(T.g64, 0, 4), part(gt, 0, 4), 64.0, None, A.mult, None, gk[0], ["g64.0"])
+        lift(0, "v")
+        add(0, 0)
+        scale(0, 0, "a")
+        add(0, 1)
         layer(1)
-        act(part(T.g64, 1, 4), part(gt, 1, 4), gk[1], ["g64.1"], scale=64.0)
-        for b in range(4):
-            add(0, b)
-            scale(0, b, "a")
-        for b in range(4):
-            add(1, b)
-            if b < 3:
-                scale(1, b, "a")
-        if t == ROUNDS - 1:
-            act(T.hf[:, 0:C // 2], T.hv[:].indirect(T.ho[:, 0:10]), ["hv0", "hv1", "ho"], ["hf0"])
+        lift(1, "a")
+        add(0, 2)
+        scale(0, 2, "a")
+        add(0, 3)
+        scale(0, 1, "v")
+        scale(0, 3, "v")
+        add(1, 0)
+        scale(1, 0, "a")
         quant_x(t + 1, 0)
+        add(1, 1)
+        scale(1, 1, "a")
+        if t + 1 < ROUNDS:
+            signs(0)
+        add(1, 2)
+        add(1, 3)
+        scale(1, 2, "v")
         scale(1, 3, "v")
         quant_x(t + 1, 1)
-        if t == 0:
-            quant(T.vq[:], T.vsc[:], T.vt[:], ["vt"], ["vq"])
+        if t + 1 < ROUNDS:
+            signs(1)
 
     qx, sx = T["qx%d" % ROUNDS], T["sx%d" % ROUNDS]
     qk = ["qx%d.%d" % (ROUNDS, h) for h in range(2)]
     for h in range(2):
         by_x(h, T.vq[:], T.vsc[:], ["vq"], ROUNDS, h)
         dma("s", part(T.oc, h, 4), part(qx, h).bitcast(u8), [qk[h]], ["oc%d" % h])
-    cp(T.hf[:, C // 2:C], T.hv[:].indirect(T.ho[:, 10:20]), ["hv0", "hv1", "ho"], ["hf1"])
     act(part(T.yo, 0), bank(0, 0), [], ["ps0", "yo0"])
     dma("a", part(T.y, 0), part(T.yo, 0), ["yo0"], ["y0"])
+    act(T.hf[:], T.hv[:].indirect(T.ho[:]), ["hv0", "hv1", "ho"], ["hf"])
     cp(part(T.yo, 1), bank(1, 1), [], ["ps1", "yo1"])
     for k in range(4):
         dma("sa"[k // 2], T.osc[4 * k:4 * k + 4, :], sx[32 * k:32 * k + 4, :], qk, ["osc%d" % k])
-    dma("a", T.ot[:], T.hf[0:128:16, :], ["hf0", "hf1"], ["ot"])
+    dma("a", T.ot[:], T.hf[0:128:16, :], ["hf"], ["ot"])
     dma("s", part(T.y, 1), part(T.yo, 1), ["yo1"], ["y1"])
     g.wait_ge(T.sem.sent, sent[0])
     finish("s")

@@ -3,6 +3,11 @@ from concourse.mybir import dt, AluOpType as A, ActivationFunctionType as F
 C, CAP, ROUNDS, STEP = 320, 96, 3, [1, 2, 1]
 CUT = [0, 192, C]
 WCUT = [0, 176, C]
+TABLE = ("again0 wscan0 blocks0 both0 pick0 post0 again1 wscan1 blocks1 both1 pick1 post1 again2 again3 equal0 equal1 gap0 first0 first1 slots0 slots1 "
+         "gap1 enter0 gap6")
+PARSE = "b00a a00v b10a a10v f00a s00v n02v f10a s10v p00v p10v d00a d01a list d02a d03a"
+LAYER = ("g00v g02a g01v g03a g10v g11a g12a g13a q00v l00v a00v a01v q10v l10a a02v a03v s02a s00v s01v s03v a10v s10a x00v a11v s11a z00a "
+         "a12v a13v s12v s13v x10v z10a n05v")
 KS = [(0, 1, 2), (3, 4)]
 SEG = [CUT[1] // 4 + 1, C // 4 + 1]
 TAB, WIN = 260, 584
@@ -26,13 +31,12 @@ def _scratch():
                         ("gt", 4 * C, BF), ("qg", C, X4), ("sg", C, U8)]:
             s["%s%d" % (n, t)] = ("sbuf", [128, w], d)
     for d, names in [
-        (BF, "ut 512 vt 512 ones 516 z0 516 z1 516 dw 672 db 640 dsel 320 dd 312 bits 648 wscan 648 bscan 640 x1 20 g64 1280"),
+        (BF, "ut 512 vt 512 ones 516 z0 516 z1 516 dw 672 db 640 dsel 80 dd 408 bits 648 wscan 648 bscan 640 x1 20 g64 1280"),
         (X4, "uq 128 up 256 vq 128 wq 512 eq 512"), (U8, "usc 128 ups 256 vsc 128 wsc 512 esc 512"),
         (I32, "i_u 16 i_e 16 i_p 22 e16 16 j22 22"), (U16, "uo 16 jo 22 ofu 8 ho 20 ix 20 gl 80"),
-        (H16, "eqm 312 dscan 312 t2 320 tsel 320 dts 320"),
+        (H16, "eqm 408 dscan 408 t2 320 tsel 320 dts 320"),
         (F32, "k16 20 src_m 80 jf 8 j4 4 kp 1 kq 4 bk 1 wc0 1 fw 4 fa 4 tiny 4 pa 16 pc 16 pd 16 pw 16 po 16 pe 16 pf 16 pt 16 m0 16 sl 8 "
-              "cf 20 cx 20 ck 20 cl 20 hv 960 vv 20 wsel 80 al 320 be 320 tf 320 st 324 ssel 320 dss 320 y2 20 sh 20 lv 20 "
-              "hh 20 hf 320 yo 320"),
+              "cf 20 cx 20 ck 20 cl 20 hv 960 vv 32 wsel 80 al 320 be 320 tf 320 st 324 ssel 320 dss 320 y2 20 sh 20 lv 20 hh 20 hf 320 yo 320"),
     ]:
         w = names.split()
         for i in range(0, len(w), 2):
@@ -42,7 +46,7 @@ def _scratch():
 
 
 SCRATCH = _scratch()
-POOL = ["s%d" % i for i in range(130)]
+POOL = ["s%d" % i for i in range(128)]
 SEMAPHORES = POOL + ["sent"] + [n % t for n in ("ac%d", "aw%d_0", "aw%d_1") for t in range(ROUNDS)]
 
 
@@ -167,6 +171,9 @@ def rank_program(g, core, T, topo):
         g.remote_dma(out, src, T.sem[sem], T.sem.sent, pid, rid, topo.mask(core, peer))
         sent[0] += len(topo.engines(core, peer))
 
+    def scales(t):
+        send(t, T["lsc%d" % t][:], T["sx%d" % t][:], "ac%d" % t, [])
+
     def quant_x(t, h):
         qx, sx, k = T["qx%d" % t], T["sx%d" % t], "qx%d.%d" % (t, h)
         quant(part(qx, h), part(sx, h), part(tile_x(t), h, 4), keys("x", t, h), [k])
@@ -176,8 +183,8 @@ def rank_program(g, core, T, topo):
         arrives("lq%d" % t, "ac%d" % t, 3 * ne)
         arrives("lw%d.%d" % (t, h), "aw%d_%d" % (t, h), ne)
         send(t, part(T["lq%d" % t], h).bitcast(u8), part(qx, h).bitcast(u8), "ac%d" % t, [k])
-        if h:
-            send(t, T["lsc%d" % t][:], sx[:], "ac%d" % t, [k])
+        if h and t:
+            scales(t)
         for i in range(2):
             by_x(2 * h + i, T.up[:, 128 * i:128 * i + 128], T.ups[:, 128 * i:128 * i + 128], ["up%d" % i, "ups%d" % i], t, h)
 
@@ -195,189 +202,190 @@ def rank_program(g, core, T, topo):
     def fill(t):
         op("g", lambda e: e.affine_select(T["tm%d" % t][:, 0:TAB], T.ones[:, 0:TAB], [[0, TAB]], A.is_equal, NONE, 1, 0), ["ones"], ["tm%d" % t])
 
-    def words(t, h):
-        a, b, n = 2 * CUT[h], 2 * CUT[h + 1] + 8 * h, (WCUT[h + 1] - WCUT[h]) // 16
-        o, wd = 2 * WCUT[h], T["wd%d" % t][:, 16 * h:16 * h + n]
-        bit = ["bit%d" % (2 * h), "bit%d" % (2 * h + 1)]
-        return [
-            lambda: scan(T.wscan[:, a:b], T.dw[:, a:b], T.bits[:, a:b], T.wscan[:, a - 1:a] if h else 0.0, A.mult, A.add,
-                         ["dw0", "dw1", "bitp", "wscan0"][:3 + h] + bit, ["wscan%d" % h]),
-            lambda: tt(T.vv[:, 0:n], T.wscan[:, o + 31:o + 32 * n:32], T.wscan[:, o + 39:o + 32 * n + 8:32], A.add, ["wscan0", "wscan%d" % h], ["vv"]),
-            lambda: (ts(wd, T.vv[:, 0:n], T.fw[:, 0:1], 128.5, A.mult, A.add, ["vv", "fw"], ["wd%d.%d" % (t, h)]),
-                     send(t, T["lw%d" % t][:, 16 * h:16 * h + n], wd, "aw%d_%d" % (t, h), ["wd%d.%d" % (t, h)])),
-        ]
+    def listed(buf, h):
+        return buf[:, 16 * h:16 * h + (WCUT[h + 1] - WCUT[h]) // 16]
 
-    def table(t, h):
-        (o, e), n, k0 = seg(h), SEG[h], KS[h][0]
-        a, b = CUT[h] // 4, CUT[h + 1] // 4
-        blocks = ["bscan0", "bscan%d" % h]
+    def words(t):
+        def wscan(h):
+            a, b = 2 * CUT[h], 2 * CUT[h + 1] + 8 * h
+            scan(T.wscan[:, a:b], T.dw[:, a:b], T.bits[:, a:b], T.wscan[:, a - 1:a] if h else 0.0, A.mult, A.add,
+                 ["dw0", "dw1", "bit%d" % (2 * h), "bit%d" % (2 * h + 1), "bitp", "wscan0"][:4 + 2 * h], ["wscan%d" % h])
 
-        def equal():
-            act(T.eqm[:, o + b:e:n], T.wsel[:, a + 15:b:16], ["wsel%d" % h, "wc0"], ["wk%d" % h], func=F.Identity, scale=0.5, bias=T.wc0[:, 0:1])
-            for k in KS[h]:
-                ts(T.eqm[:, o + n * (k - k0):o + n * (k - k0) + b], T.bscan[:, 7:8 * b:8], T.kp[:, 0:1], T.wsel[:, 16 * k + 15:16 * k + 16],
-                   A.add, A.is_equal, blocks + ["wsel%d" % h, "kp"], ["eqm%d" % k])
-        return [
-            lambda: scan(part(T.bscan, h, 2), part(T.db, h, 2), part(T.bits, h, 2), 0.0, A.mult, A.add,
-                         ["db", "bit%d" % (2 * h), "bit%d" % (2 * h + 1)], ["bscan%d" % h]),
-            lambda: scan(T.wsel[:, a:b], T.bscan[:, 8 * a + 7:8 * b:8], T.dsel[:, a:b], -4 * LIFT, A.max, A.add, ["dsel", "bscan%d" % h], ["wsel%d" % h]),
-            equal,
-            lambda: scan(T.dscan[:, o:e], T.dd[:, o:e], T.eqm[:, o:e], 0.0, A.mult, A.max,
-                         ["dd", "wk%d" % h] + ["eqm%d" % k for k in KS[h]], ["dscan%d" % h]),
-            lambda: cp(T.ofu[:, k0:k0 + len(KS[h])], T.dscan[:, o + b:e:n], ["dscan%d" % h], ["ofu%d" % h]),
-        ]
+        def both(h):
+            a, b = 2 * WCUT[h], 2 * WCUT[h + 1]
+            tt(listed(T.vv, h), T.wscan[:, a + 31:b:32], T.wscan[:, a + 39:b + 8:32], A.add, ["wscan0", "wscan%d" % h], ["vv%d" % h])
 
-    def evac(t, b):
-        times("a", plane(t, b, 1), bank(4 + b), 64.0 if t else 1.0, [], ["ps%d" % (4 + b), "d%d.%d" % (t, b)])
+        def post(h):
+            wd, k = listed(T["wd%d" % t], h), "wd%d.%d" % (t, h)
+            ts(wd, listed(T.vv, h), T.fw[:, 0:1], 128.5, A.mult, A.add, ["vv%d" % h, "fw"], [k])
+            send(t, listed(T["lw%d" % t], h), wd, "aw%d_%d" % (t, h), [k])
+            if h and not t:
+                scales(0)
+        return dict(wscan=wscan, both=both, post=post)
 
-    def again(t, b):
+    def table(t):
+        def blocks(h):
+            scan(part(T.bscan, h, 2), part(T.db, h, 2), part(T.bits, h, 2), 0.0, A.mult, A.add,
+                 ["db", "bit%d" % (2 * h), "bit%d" % (2 * h + 1)], ["bscan%d" % h])
+
+        def pick(h):
+            a, b = CUT[h] // 4, CUT[h + 1] // 4
+            scan(T.wsel[:, a:b], T.bscan[:, 8 * a + 7:8 * b:8], T.dsel[:, a:b], -4 * LIFT, A.max, A.add, ["dsel", "bscan%d" % h], ["wsel%d" % h])
+
+        def equal(h):
+            (o, e), n, a, b = seg(h), SEG[h], CUT[h] // 4, CUT[h + 1] // 4
+            ts(T.eqm[:, o + b:e:n], T.wsel[:, a + 15:b:16], 0.5, T.wc0[:, 0:1], A.mult, A.add, ["wsel%d" % h, "wc0"], ["wk%d" % h])
+            for i, k in enumerate(KS[h]):
+                ts(T.eqm[:, o + n * i:o + n * i + b], T.bscan[:, 7:8 * b:8], T.kp[:, 0:1], T.wsel[:, 16 * k + 15:16 * k + 16],
+                   A.add, A.is_equal, ["bscan0", "bscan%d" % h, "wsel%d" % h, "kp"], ["eqm%d" % k])
+
+        def first(h):
+            o, e = seg(h)
+            scan(T.dscan[:, o:e], T.dd[:, o:e], T.eqm[:, o:e], 0.0, A.mult, A.max, ["ddz%d" % h, "wk%d" % h] + ["eqm%d" % k for k in KS[h]], ["dscan%d" % h])
+
+        def slots(h):
+            (o, e), n = seg(h), SEG[h]
+            cp(T.ofu[:, KS[h][0]:KS[h][-1] + 1], T.dscan[:, o + n - 1:e:n], ["dscan%d" % h], ["ofu%d" % h])
+
+        def enter(_):
+            cp(T["tm%d" % t][:].indirect(T.ofu[:, 0:5]), T.src_m[:], ["ofu0", "ofu1", "src_m"], ["tm%d" % t])
+        return dict(blocks=blocks, pick=pick, equal=equal, first=first, slots=slots, enter=enter)
+
+    def evac(t, b, q):
+        times(q, plane(t, b, 1), bank(4 + b), 64.0 if t else 1.0, [], ["ps%d" % (4 + b), "d%d.%d" % (t, b)])
+
+    def again(t, b, q):
         if t:
-            act(plane(t, b, 2), plane(t, b, 0), [keys("y", t, h)[b] for h in range(2)], ["yc%d.%d" % (t, b)])
+            times(q, plane(t, b, 2), plane(t, b, 0), 1.0, [keys("y", t, h)[b] for h in range(2)], ["yc%d.%d" % (t, b)])
 
     dma("a", T.ut[:], T.u[:], [], ["ut"])
     for h in range(2):
         dma("s", part(T.win0, h, 4), part(T.x, h, 4), [], keys("x", 0, h) + keys("y", 0, h))
-    dma("s", T.wq[:].bitcast(u8), T.wc[:], [], ["wq"])
-    dma("s", T.wsc[:], T.ws[:], [], ["wsc"])
+    dma("s", T.win0[:, 8 * C:12 * C], T.x[:], [], ["yc0.%d" % b for b in range(4)])
 
-    iota(T.i_p[:], [[0, 22]], 0, 1, ["i_p"])
     iota(T.i_e[:], [[1, 16]], 128, -1, ["i_e"])
+    iota(T.i_p[:], [[0, 22]], 0, 1, ["i_p"])
     iota(T.i_u[:], [[1, 2], [16, 8]], 0, 0, ["i_u"])
     iota(T.k16[:], [[16, 20]], 0, 0, ["k16"], True)
-    ms(T.ones[:], 1.0, ["ones"])
-    ms(T.tiny[:], -2.0 ** -120, ["tiny"])
-    ms(T.db[:], 2.0, ["db"])
-    ms(T.dd[:], 1.0, ["dd"])
-    op("g", lambda e: e.affine_select(T.z1[:], T.ones[:], [[-1, 516]], A.is_equal, 0.0, 3, 4), ["ones"], ["z1"])
-    fill(0)
     iota(T.src_m[:], [[4, 80]], 2 * C, 0, ["src_m"], True)
-    ts(T.j22[:], T.i_p[:], 15, None, A.bitwise_and, None, ["i_p"], ["j22"])
+    ms(T.ones[:], 1.0, ["ones"])
+    op("g", lambda e: e.affine_select(T.z1[:], T.ones[:], [[-1, 516]], A.is_equal, 0.0, 3, 4), ["ones"], ["z1"])
+    act(T.tm0[:, 0:TAB], T.ones[:, 0:TAB], ["ones"], ["tm0"], scale=NONE)
     ts(T.e16[:], T.i_e[:], 15, None, A.bitwise_and, None, ["i_e"], ["e16"])
-    ms(T.db[:, 0:640:8], 0.0, ["db"])
-    cp(T.jo[:], T.j22[:], ["j22"], ["jo"])
+    ms(T.tiny[:], -2.0 ** -120, ["tiny"])
+    ts(T.j22[:], T.i_p[:], 15, None, A.bitwise_and, None, ["i_p"], ["j22"])
     ts(T.po[:], T.e16[:], 3.5, 1.0, A.is_lt, A.add, ["e16"], ["po"])
     ts(T.pa[:], T.e16[:], 4.0, HOLD - 1, A.is_equal, A.mult, ["e16"], ["pa"])
+    cp(T.jo[:], T.j22[:], ["j22"], ["jo"])
     ts(T.pc[:], T.e16[:], 0.0, -2.0, A.is_equal, A.mult, ["e16"], ["pc"])
     ts(T.pe[:], T.e16[:], 0.0, LIFT, A.is_equal, A.mult, ["e16"], ["pe"])
-    ts(T.pf[:], T.e16[:], 15.0, -2 * LIFT, A.is_equal, A.mult, ["e16"], ["pf"])
+    act(T.dw[:, 1:672:2], T.po[:].indirect(T.jo[:, 0:21]), ["po", "jo"], ["dw1"])
     tt(T.pd[:], T.pa[:], T.pc[:], A.add, ["pa", "pc"], ["pd"])
+    ts(T.pf[:], T.e16[:], 15.0, -2 * LIFT, A.is_equal, A.mult, ["e16"], ["pf"])
     cp(T.jf[:], T.j22[:, 0:8], ["j22"], ["jf"])
+    tt(T.pw[:], T.pd[:], T.po[:], A.add, ["pd", "po"], ["pw"])
     tt(T.pt[:], T.pe[:], T.pf[:], A.add, ["pe", "pf"], ["pt"])
     cp(T.uo[:], T.i_u[:], ["i_u"], ["uo"])
-    tt(T.pw[:], T.pd[:], T.po[:], A.add, ["pd", "po"], ["pw"])
-    act(T.dw[:, 1:672:2], T.po[:].indirect(T.jo[:, 0:21]), ["po", "jo"], ["dw1"])
     act(T.dw[:, 0:672:2], T.pw[:].indirect(T.jo[:, 0:21]), ["pw", "jo"], ["dw0"])
-    act(T.dsel[:], T.pt[:].indirect(T.jo[:, 0:20]), ["pt", "jo"], ["dsel"])
     act(T.fa[:], T.jf[:, 0:4], ["jf"], ["fa"], func=F.Square, bias=-7.5)
+    ms(T.db[:], 2.0, ["db"])
+    ms(T.dd[:], 1.0, ["dd"])
     ts(T.m0[:], T.e16[:], 0.0, None, A.is_equal, None, ["e16"], ["m0"])
+    ms(T.db[:, 0:640:8], 0.0, ["db"])
     ts(T.j4[:], T.jf[:, 0:4], 4.0, TAB - 1.0, A.mult, A.add, ["jf"], ["j4"])
-    ts(T.kp[:], T.pt[:, 15:16], LIFT, LIFT, A.add, A.min, ["pt"], ["kp"])
-    ts(T.bits[:, 640:648], T.jf[:], 12.5, -2.0 ** 20, A.is_gt, A.mult, ["jf"], ["bitp"])
-    ts(T.sl[:, 0:5], T.k16[:, 0:5], 4.0, T.j4[:, 0:1], A.mult, A.add, ["k16", "j4"], ["sl"])
-    ts(T.cf[:], T.k16[:], T.jf[:, 0:1], None, A.add, None, ["k16", "jf"], ["cf"])
-    ts(T.bk[:], T.jf[:, 0:1], 14.5, LIFT, A.is_lt, A.mult, ["jf"], ["bk"])
 
     quant(T.uq[:], T.usc[:], T.ut[:], ["ut"], ["uq"])
-    ts(T.wc0[:], T.kp[:], -0.5, 128.5, A.mult, A.add, ["kp"], ["wc0"])
+    ts(T.sl[:, 0:5], T.k16[:, 0:5], 4.0, T.j4[:, 0:1], A.mult, A.add, ["k16", "j4"], ["sl"])
     for i in range(2):
         o = T.uo[:, 8 * i:8 * i + 8]
         act(T.ups[:, 128 * i:128 * i + 128], T.usc[:].indirect(o), ["uq", "uo"], ["ups%d" % i])
         cp(T.up[:, 128 * i:128 * i + 128].bitcast(u32), T.uq[:].bitcast(u32).indirect(o), ["uq", "uo"], ["up%d" % i])
-    for h in range(2):
-        for k in KS[h]:
-            o = seg(h)[0] + SEG[h] * (k - KS[h][0]) + 16 * k
-            act(T.dd[:, o:o + 16], T.m0[:], ["m0", "sl", "dd"], ["dd%d" % k], func=F.Identity, scale=T.sl[:, k:k + 1], bias=1.0)
+    act(T.dsel[:], T.pt[:].indirect(T.jo[:, 0:5]), ["pt", "jo"], ["dsel"])
     quant_x(0, 0)
     signs(0)
     ts(T.fw[:], T.fa[:], 16.0, 1.0, A.is_gt, A.add, ["fa"], ["fw"])
+    ts(T.kp[:], T.pt[:, 15:16], LIFT, LIFT, A.add, A.min, ["pt"], ["kp"])
     quant_e(1)
     quant_x(0, 1)
     signs(1)
+    for k in range(5):
+        h = int(k in KS[1])
+        o = seg(h)[0] + SEG[h] * (k - KS[h][0]) + 16 * k
+        act(T.dd[:, o:o + 16], T.m0[:], ["m0", "sl", "dd"], ["dd%d" % k], func=F.Identity, scale=T.sl[:, k:k + 1], bias=1.0)
+    ts(T.bits[:, 640:648], T.jf[:], 12.5, -2.0 ** 20, A.is_gt, A.mult, ["jf"], ["bitp"])
     ts(T.fw[:], T.fw[:], 0.25 / HOLD, None, A.mult, None, ["fw"], ["fw"])
-    for h in range(2):
-        ms(T.dd[:, seg(h)[0]:seg(h)[1]:SEG[h]], 0.0, ["dd"] + ["dd%d" % k for k in KS[h]])
+    ts(T.wc0[:], T.kp[:], -0.5, 128.5, A.mult, A.add, ["kp"], ["wc0"])
+    ts(T.cf[:], T.k16[:], T.jf[:, 0:1], None, A.add, None, ["k16", "jf"], ["cf"])
+    ts(T.bk[:], T.pt[:, 15:16], 0.0, BASE + LIFT + 576, A.max, A.subtract, ["pt"], ["bk"])
     quant_e(3)
+    ts(T.cx[:], T.cf[:], 1.5, None, A.subtract, None, ["cf"], ["cx"])
     act(T.z0[:, 0:514], T.z1[:, 1:515], ["z1"], ["z0"])
-    act(T.dss[:], T.dsel[:], ["dsel"], ["dss"])
-    act(T.dts[:], T.dsel[:], ["dsel"], ["dts"])
-    act(T.cx[:], T.cf[:], ["cf"], ["cx"], func=F.Identity, bias=574.5)
-    act(T.cl[:], T.cf[:], ["cf", "kp"], ["cl"], func=F.Identity, bias=T.kp[:, 0:1])
-    act(T.kq[:], T.k16[:, 0:4], ["k16", "kp"], ["kq"], func=F.Identity, scale=-1.0 / 64, bias=T.kp[:, 0:1])
-    once = [
-        lambda: quant_e(0),
-        lambda: quant_e(2),
-        lambda: ts(T.dss[:, 15:C:16], T.cf[:], BASE, T.bk[:, 0:1], A.subtract, A.subtract, ["cf", "bk"], ["dss"]),
-        lambda: ms(T.st[:, 0:1], BASE, ["st0"]),
-        lambda: ts(T.ck[:], T.cf[:], 576.0, T.pt[:, 15:16], A.add, A.add, ["cf", "pt"], ["ck"]),
-        lambda: None,
-        lambda: quant(T.vq[:], T.vsc[:], T.vt[:], ["vt"], ["vq"]),
-    ]
+    act(T.dss[:], T.pt[:].indirect(T.jo[:, 0:20]), ["pt", "jo"], ["dss"])
+    once = {
+        (0, 0): lambda: [ms(T.dd[:, seg(h)[0]:seg(h)[1]:SEG[h]], 0.0, ["ddz%d" % h] + ["dd%d" % k for k in KS[h]]) for h in range(2)],
+        (0, 1): lambda: quant_e(0),
+        (0, 6): lambda: quant_e(2),
+        (0, 2): lambda: [ms(T.st[:, 0:1], BASE, ["st0"]), cp(T.dts[:], T.dss[:], ["dss"], ["dts"]),
+                         ts(T.dss[:, 15:C:16], T.cf[:], T.bk[:, 0:1], None, A.add, None, ["cf", "bk"], ["dss", "dss15"])],
+        (0, 3): lambda: ts(T.ck[:], T.cf[:], BASE + 576 - LIFT, T.bk[:, 0:1], A.add, A.add, ["cf", "bk"], ["ck"]),
+        (1, 5): lambda: quant(T.vq[:], T.vsc[:], T.vt[:], ["vt"], ["vq"]),
+    }
 
-    def gap():
-        if once:
-            once.pop(0)()
+    def gap(t, i):
+        if (t, i) in once:
+            once[t, i]()
 
     for t in range(ROUNDS):
         lw, tm, gt, qg, sg = [T["%s%d" % (n, t)] for n in ("lw", "tm", "gt", "qg", "sg")]
         K = lambda n: "%s%d" % (n, t)
 
-        w0, w1, t0, t1 = words(t, 0), words(t, 1), table(t, 0), table(t, 1)
-        again(t, 0)
-        for step in [w0[0], t0[0], w0[1], t0[1], w0[2], w1[0], t1[0], w1[1], t1[1], w1[2], t0[2], t1[2], t0[3], t1[3], t0[4], t1[4], gap]:
-            step()
-        cp(tm[:].indirect(T.ofu[:, 0:5]), T.src_m[:], ["ofu0", "ofu1", "src_m"], [K("tm")])
+        steps = dict(words(t), **table(t))
+        steps.update(gap=lambda i: gap(t, i), again=lambda b: again(t, b, "a"))
+        for x in TABLE.split():
+            steps[x[:-1]](int(x[-1]))
         if t == 0:
-            dma("s", T.win0[:, 8 * C:12 * C], T.x[:], ["lw0.1"], ["yc0.%d" % b for b in range(4)])
+            dma("s", T.wq[:].bitcast(u8), T.wc[:], ["lw0.1"], ["wq"])
+            dma("s", T.wsc[:], T.ws[:], [], ["wsc"])
             dma("s", T.vt[:], T.v[:], [], ["vt"])
-        for b in range(1, 4):
-            again(t, b)
         if t + 1 < ROUNDS:
             fill(t + 1)
         if t == 1:
             iota(T.hv[:, 0:2 * C], [[1, 2 * C]], 0, 0, ["hv0"], True)
             iota(T.hv[:, 2 * C:3 * C], [[1, C]], 0, 0, ["hv1"], True)
-        gap()
         for b in range(4):
             mm(bank(4 + b), T.eq[:, 128 * b:128 * b + 128], T.esc[:, 128 * b:128 * b + 128], T[K("lq")][:], T[K("lsc")][:], ["eq%d" % b, K("lq")], ["ps%d" % (4 + b)])
 
-        look = [tm[:, 0:TAB].indirect(lw[:, 16 * h:16 * h + (WCUT[h + 1] - WCUT[h]) // 16]) for h in range(2)]
-        lk = [[K("tm"), "lw%d.%d" % (t, h)] for h in range(2)]
-        m = WCUT[1]
-        for h in range(2):
-            act(part(T.be, h, cut=WCUT), look[h], lk[h], ["be%d" % h], func=F.Identity, scale=-TINY, bias=B1)
-            ts(part(T.al, h, cut=WCUT), look[h], 0.0, A0, A.is_gt, A.max, lk[h], ["al%d" % h])
-        for h in range(2):
-            act(part(T.tf, h, cut=WCUT), look[h], lk[h], ["tf%d" % h], func=F.Relu)
-            scan(T.st[:, WCUT[h] + 1:WCUT[h + 1] + 1], part(T.al, h, cut=WCUT), part(T.be, h, cut=WCUT), T.st[:, m:m + 1] if h else BASE,
-                 A.mult, A.mult, ["al%d" % h, "be%d" % h, "st1"][:2 + h], ["st%d" % (h + 1)])
-            if h == 0:
-                gap()
-                gap()
-        for h in range(2):
-            scan(part(T.ssel, h, cut=WCUT), part(T.st, h, cut=WCUT), part(T.dss, h, cut=WCUT), 0.0, A.max, A.add,
-                 ["dss", "st%d" % h, "st%d" % (h + 1)], ["ssel%d" % h])
-        evac(t, 0)
-        evac(t, 1)
-        gap()
+        look = [tm[:, 0:TAB].indirect(listed(lw, h)) for h in range(2)]
+        lk, m = [[K("tm"), "lw%d.%d" % (t, h)] for h in range(2)], WCUT[1]
+        steps = dict(
+            d=lambda h, b, q: evac(t, b, q), n=lambda h, b, q: gap(t, b),
+            b=lambda h, b, q: act(part(T.be, h, cut=WCUT), look[h], lk[h], ["be%d" % h], func=F.Identity, scale=-TINY, bias=B1),
+            a=lambda h, b, q: ts(part(T.al, h, cut=WCUT), look[h], 0.0, A0, A.is_gt, A.max, lk[h], ["al%d" % h]),
+            f=lambda h, b, q: act(part(T.tf, h, cut=WCUT), look[h], lk[h], ["tf%d" % h], func=F.Relu),
+            s=lambda h, b, q: scan(T.st[:, WCUT[h] + 1:WCUT[h + 1] + 1], part(T.al, h, cut=WCUT), part(T.be, h, cut=WCUT), T.st[:, m:m + 1] if h else BASE,
+                                   A.mult, A.mult, ["al%d" % h, "be%d" % h, "st1"][:2 + h], ["st%d" % (h + 1)]),
+            p=lambda h, b, q: scan(part(T.ssel, h, cut=WCUT), part(T.st, h, cut=WCUT), part(T.dss, h, cut=WCUT), 0.0, A.max, A.add,
+                                   ["dss15", "st%d" % h, "st%d" % (h + 1)], ["ssel%d" % h]))
+        ahead, behind = [o.split() for o in PARSE.split("list")]
+        for x in ahead:
+            steps[x[0]](int(x[1]), int(x[2]), x[3])
+        gap(t, 3)
         ll, sk = T.ssel[:, 15:C:16], ["ssel0", "ssel1"]
         tt(T.x1[:], ll, T.cx[:], A.subtract, sk + ["cx"], ["x1"])
-        ts(T.sh[:], ll, CAP - 0.5, float(C), A.is_lt, A.mult, sk, ["sh"])
+        ts(T.sh[:], ll, CAP - 576.5, float(C), A.is_lt, A.mult, sk, ["sh"])
+        tt(T.ix[:], ll, T.x1[:], A.subtract, sk + ["x1"], ["ix"])
         tt(T.y2[:], ll, T.x1[:], A.subtract, sk + ["x1"], ["y2"])
-        tt(T.lv[:], T.sh[:], T.cl[:], A.add, ["sh", "cl"], ["lv"])
-        ts(T.ix[:], T.y2[:], 576.0, None, A.subtract, None, ["y2"], ["ix"])
-        act(T.t2[:, 0:C // 2], T.tf[:].indirect(T.ix[:, 0:10]), ["tf0", "tf1", "ix"], ["t2a"])
-        evac(t, 2)
-        evac(t, 3)
+        act(T.t2[:, 0:128], T.tf[:].indirect(T.ix[:, 0:8]), ["tf0", "tf1", "ix"], ["t2a"], func=F.Identity, bias=LIFT)
+        for x in behind:
+            steps[x[0]](int(x[1]), int(x[2]), x[3])
+        tt(T.lv[:], T.sh[:], T.cf[:], A.add, ["sh", "cf"], ["lv"])
+        ts(T.t2[:, 128:C], T.tf[:].indirect(T.ix[:, 8:20]), LIFT, None, A.add, None, ["tf0", "tf1", "ix"], ["t2b"])
         tt(T.dts[:, 15:C:16], T.ck[:], T.y2[:], A.subtract, ["ck", "y2"], ["dts"])
-        cp(T.t2[:, C // 2:C], T.tf[:].indirect(T.ix[:, 10:20]), ["tf0", "tf1", "ix"], ["t2b"])
-        gap()
         scan(T.tsel[:], T.t2[:], T.dts[:], 0.0, A.max, A.add, ["dts", "t2a", "t2b"], ["tsel"])
-        tt(T.hh[:], T.tsel[:, 15:C:16], T.lv[:], A.max, ["tsel", "lv"], ["hh"])
-        if t:
-            ts(T.ho[:], T.hh[:], T.kp[:, 0:1], None, A.subtract, None, ["hh", "kp"], ["ho"])
-        else:
+        tt(T.ho[:] if t else T.hh[:], T.tsel[:, 15:C:16], T.lv[:], A.max, ["tsel", "lv"], ["ho"])
+        if t == 0:
             for b in (0, 2, 1, 3):
-                ts(T.gl[:, 20 * b:20 * b + 20], T.hh[:], T.kq[:, b:b + 1], 4.0, A.subtract, A.mult, ["hh", "kq"], ["gl%d" % b])
+                ts(T.gl[:, 20 * b:20 * b + 20], T.hh[:], 4.0, float(b), A.mult, A.add, ["ho"], ["gl%d" % b])
 
         def gather(h, b, q):
             lo, hi = CUT[h] // 16, CUT[h + 1] // 16
@@ -401,34 +409,10 @@ def rank_program(g, core, T, topo):
 
         def scale(h, b, q):
             times(q, part(T["xt%d" % (t + 1)], h, 4, b), plane(t + 1, b, 0, h), 2.0 ** -6, [keys("y", t + 1, h)[b]], [keys("x", t + 1, h)[b]])
-        for h, b, q in [(0, 0, "v"), (0, 2, "a"), (0, 1, "v"), (0, 3, "a"), (1, 0, "a"), (1, 1, "a"), (1, 2, "a"), (1, 3, "a")]:
-            gather(h, b, q)
-        layer(0)
-        lift(0, "v")
-        add(0, 0)
-        scale(0, 0, "a")
-        add(0, 1)
-        layer(1)
-        lift(1, "a")
-        add(0, 2)
-        scale(0, 2, "a")
-        add(0, 3)
-        scale(0, 1, "v")
-        scale(0, 3, "v")
-        add(1, 0)
-        scale(1, 0, "a")
-        quant_x(t + 1, 0)
-        add(1, 1)
-        scale(1, 1, "a")
-        if t + 1 < ROUNDS:
-            signs(0)
-        add(1, 2)
-        add(1, 3)
-        scale(1, 2, "v")
-        scale(1, 3, "v")
-        quant_x(t + 1, 1)
-        if t + 1 < ROUNDS:
-            signs(1)
+        steps = dict(g=gather, s=scale, n=lambda h, b, q: gap(t, b), a=lambda h, b, q: add(h, b), q=lambda h, b, q: layer(h), l=lambda h, b, q: lift(h, q),
+                     x=lambda h, b, q: quant_x(t + 1, h), z=lambda h, b, q: t + 1 < ROUNDS and signs(h))
+        for x in LAYER.split():
+            steps[x[0]](int(x[1]), int(x[2]), x[3])
 
     qx, sx = T["qx%d" % ROUNDS], T["sx%d" % ROUNDS]
     qk = ["qx%d.%d" % (ROUNDS, h) for h in range(2)]
@@ -437,11 +421,12 @@ def rank_program(g, core, T, topo):
         dma("s", part(T.oc, h, 4), part(qx, h).bitcast(u8), [qk[h]], ["oc%d" % h])
     act(part(T.yo, 0), bank(0, 0), [], ["ps0", "yo0"])
     dma("a", part(T.y, 0), part(T.yo, 0), ["yo0"], ["y0"])
-    act(T.hf[:], T.hv[:].indirect(T.ho[:]), ["hv0", "hv1", "ho"], ["hf"])
+    cp(T.hf[:, 0:C // 2], T.hv[:].indirect(T.ho[:, 0:10]), ["hv0", "hv1", "ho"], ["hf0"])
+    act(T.hf[:, C // 2:C], T.hv[:].indirect(T.ho[:, 10:20]), ["hv0", "hv1", "ho"], ["hf1"])
     cp(part(T.yo, 1), bank(1, 1), [], ["ps1", "yo1"])
     for k in range(4):
         dma("sa"[k // 2], T.osc[4 * k:4 * k + 4, :], sx[32 * k:32 * k + 4, :], qk, ["osc%d" % k])
-    dma("a", T.ot[:], T.hf[0:128:16, :], ["hf"], ["ot"])
+    dma("a", T.ot[:], T.hf[0:128:16, :], ["hf0", "hf1"], ["ot"])
     dma("s", part(T.y, 1), part(T.yo, 1), ["yo1"], ["y1"])
     g.wait_ge(T.sem.sent, sent[0])
     finish("s")

@@ -3,11 +3,12 @@ from concourse.mybir import dt, AluOpType as A, ActivationFunctionType as F
 C, CAP, ROUNDS, STEP = 320, 96, 3, [1, 2, 1]
 CUT = [0, 192, C]
 WCUT = [0, 176, C]
-TABLE = ("again0 wscan0 blocks0 both0 pick0 post0 again1 wscan1 blocks1 both1 pick1 post1 again2 again3 equal0 equal1 gap0 first0 first1 slots0 slots1 "
-         "gap1 enter0 gap6")
-PARSE = "b00a a00v b10a a10v f00a s00v n02v f10a s10v p00v p10v d00a d01a list d02a d03a"
-LAYER = ("g00v g02a g01v g03a g10v g11a g12a g13a q00v l00v a00v a01v q10v l10a a02v a03v s02a s00v s01v s03v a10v s10a x00v a11v s11a z00a "
-         "a12v a13v s12v s13v x10v z10a n05v")
+ORDER = ("u00p u01p u02p u03p k00v k01a k10v p00v k11a k12a n02v k02a p10v n03v h00v h10v h01v d00a h02v d01a h11v h04v h12v h14v h05v h06v "
+         "h17v h15v h07a h08v h16v h18v h09v d02a h19v j02v j00v j01v j11v d03a g02a j03v g03a g00v g11a g01v j13v j12v j10v g10a "
+         "q00v g13a l00v g12v a00v q10v a01v l10a a02v a03v s01v s02v s00a a10v s03a a11v s10a a12v x00v a13v s12v s11a Z00a s13v x10v Z10a n05v "
+         "Y02a W00v Y01a B00v O00v W10v B10v Y03a I00v P00v O10v G00v I10v E01v E00v P10v N00v N10v E14v E13v E02v F00v F01v F14v Y00a F13v F02v "
+         "G06v T00v G01v")
+END = 640
 KS = [(0, 1, 2), (3, 4)]
 SEG = [CUT[1] // 4 + 1, C // 4 + 1]
 TAB, WIN = 260, 584
@@ -33,7 +34,7 @@ def _scratch():
     for d, names in [
         (BF, "ut 512 vt 512 ones 516 z0 516 z1 516 dw 672 db 640 dsel 80 dd 408 bits 648 wscan 648 bscan 640 x1 20 g64 1280"),
         (X4, "uq 128 up 256 vq 128 wq 512 eq 512"), (U8, "usc 128 ups 256 vsc 128 wsc 512 esc 512"),
-        (I32, "i_u 16 i_e 16 i_p 22 e16 16 j22 22"), (U16, "uo 16 jo 22 ofu 8 ho 20 ix 20 gl 80"),
+        (I32, "i_u 16 i_e 16 i_p 22 e16 16 j22 22"), (U16, "uo 16 jo 22 ofu 648 ho 20 ix 20 gl 80"),
         (H16, "eqm 408 dscan 408 t2 320 tsel 320 dts 320"),
         (F32, "k16 20 src_m 80 jf 8 j4 4 kp 1 kq 4 bk 1 wc0 1 fw 4 fa 4 tiny 4 pa 16 pc 16 pd 16 pw 16 po 16 pe 16 pf 16 pt 16 m0 16 sl 8 "
               "cf 20 cx 20 ck 20 cl 20 hv 960 vv 32 wsel 80 al 320 be 320 tf 320 st 324 ssel 320 dss 320 y2 20 sh 20 lv 20 hh 20 hf 320 yo 320"),
@@ -205,58 +206,130 @@ def rank_program(g, core, T, topo):
     def listed(buf, h):
         return buf[:, 16 * h:16 * h + (WCUT[h + 1] - WCUT[h]) // 16]
 
-    def words(t):
-        def wscan(h):
-            a, b = 2 * CUT[h], 2 * CUT[h + 1] + 8 * h
-            scan(T.wscan[:, a:b], T.dw[:, a:b], T.bits[:, a:b], T.wscan[:, a - 1:a] if h else 0.0, A.mult, A.add,
-                 ["dw0", "dw1", "bit%d" % (2 * h), "bit%d" % (2 * h + 1), "bitp", "wscan0"][:4 + 2 * h], ["wscan%d" % h])
+    def wscan(t, h, b, q):
+        lo, hi = 2 * CUT[h], 2 * CUT[h + 1] + 8 * h
+        scan(T.wscan[:, lo:hi], T.dw[:, lo:hi], T.bits[:, lo:hi], T.wscan[:, lo - 1:lo] if h else 0.0, A.mult, A.add,
+             ["dw0", "dw1", "bit%d" % (2 * h), "bit%d" % (2 * h + 1), "bitp", "wscan0"][:4 + 2 * h], ["wscan%d" % h])
 
-        def both(h):
-            a, b = 2 * WCUT[h], 2 * WCUT[h + 1]
-            tt(listed(T.vv, h), T.wscan[:, a + 31:b:32], T.wscan[:, a + 39:b + 8:32], A.add, ["wscan0", "wscan%d" % h], ["vv%d" % h])
+    def both(t, h, b, q):
+        lo, hi = 2 * WCUT[h], 2 * WCUT[h + 1]
+        tt(listed(T.vv, h), T.wscan[:, lo + 31:hi:32], T.wscan[:, lo + 39:hi + 8:32], A.add, ["wscan0", "wscan%d" % h], ["vv%d" % h])
 
-        def post(h):
-            wd, k = listed(T["wd%d" % t], h), "wd%d.%d" % (t, h)
-            ts(wd, listed(T.vv, h), T.fw[:, 0:1], 128.5, A.mult, A.add, ["vv%d" % h, "fw"], [k])
-            send(t, listed(T["lw%d" % t], h), wd, "aw%d_%d" % (t, h), [k])
-            if h and not t:
-                scales(0)
-        return dict(wscan=wscan, both=both, post=post)
+    def post(t, h, b, q):
+        wd, k = listed(T["wd%d" % t], h), "wd%d.%d" % (t, h)
+        ts(wd, listed(T.vv, h), T.fw[:, 0:1], 128.5, A.mult, A.add, ["vv%d" % h, "fw"], [k])
+        send(t, listed(T["lw%d" % t], h), wd, "aw%d_%d" % (t, h), [k])
+        if h and t == 0:
+            scales(0)
+            dma("s", T.wq[:].bitcast(u8), T.wc[:], ["lw0.1"], ["wq"])
+            dma("s", T.wsc[:], T.ws[:], [], ["wsc"])
+            dma("s", T.vt[:], T.v[:], [], ["vt"])
+        if h and t + 1 < ROUNDS:
+            fill(t + 1)
+        if h and t == 1:
+            iota(T.hv[:, 0:2 * C], [[1, 2 * C]], 0, 0, ["hv0"], True)
+            iota(T.hv[:, 2 * C:3 * C], [[1, C]], 0, 0, ["hv1"], True)
 
-    def table(t):
-        def blocks(h):
-            scan(part(T.bscan, h, 2), part(T.db, h, 2), part(T.bits, h, 2), 0.0, A.mult, A.add,
-                 ["db", "bit%d" % (2 * h), "bit%d" % (2 * h + 1)], ["bscan%d" % h])
+    def blocks(t, h, b, q):
+        scan(part(T.bscan, h, 2), part(T.db, h, 2), part(T.bits, h, 2), 0.0, A.mult, A.add,
+             ["db", "bit%d" % (2 * h), "bit%d" % (2 * h + 1)], ["bscan%d" % h])
 
-        def pick(h):
-            a, b = CUT[h] // 4, CUT[h + 1] // 4
-            scan(T.wsel[:, a:b], T.bscan[:, 8 * a + 7:8 * b:8], T.dsel[:, a:b], -4 * LIFT, A.max, A.add, ["dsel", "bscan%d" % h], ["wsel%d" % h])
+    def pick(t, h, b, q):
+        lo, hi = CUT[h] // 4, CUT[h + 1] // 4
+        scan(T.wsel[:, lo:hi], T.bscan[:, 8 * lo + 7:8 * hi:8], T.dsel[:, lo:hi], -4 * LIFT, A.max, A.add, ["dsel", "bscan%d" % h], ["wsel%d" % h])
 
-        def equal(h):
-            (o, e), n, a, b = seg(h), SEG[h], CUT[h] // 4, CUT[h + 1] // 4
-            ts(T.eqm[:, o + b:e:n], T.wsel[:, a + 15:b:16], 0.5, T.wc0[:, 0:1], A.mult, A.add, ["wsel%d" % h, "wc0"], ["wk%d" % h])
-            for i, k in enumerate(KS[h]):
-                ts(T.eqm[:, o + n * i:o + n * i + b], T.bscan[:, 7:8 * b:8], T.kp[:, 0:1], T.wsel[:, 16 * k + 15:16 * k + 16],
-                   A.add, A.is_equal, ["bscan0", "bscan%d" % h, "wsel%d" % h, "kp"], ["eqm%d" % k])
+    def entry(t, h, b, q):
+        (o, e), lo, hi = seg(h), CUT[h] // 4, CUT[h + 1] // 4
+        ts(T.eqm[:, o + hi:e:SEG[h]], T.wsel[:, lo + 15:hi:16], 0.5, T.wc0[:, 0:1], A.mult, A.add, ["wsel%d" % h, "wc0"], ["wk%d" % h])
 
-        def first(h):
-            o, e = seg(h)
-            scan(T.dscan[:, o:e], T.dd[:, o:e], T.eqm[:, o:e], 0.0, A.mult, A.max, ["ddz%d" % h, "wk%d" % h] + ["eqm%d" % k for k in KS[h]], ["dscan%d" % h])
+    def equal(t, h, k, q):
+        o, hi = seg(h)[0] + SEG[h] * (k - KS[h][0]), CUT[h + 1] // 4
+        ts(T.eqm[:, o:o + hi], T.bscan[:, 7:8 * hi:8], T.kp[:, 0:1], T.wsel[:, 16 * k + 15:16 * k + 16],
+           A.add, A.is_equal, ["bscan0", "bscan%d" % h, "wsel%d" % h, "kp"], ["eqm%d" % k])
 
-        def slots(h):
-            (o, e), n = seg(h), SEG[h]
-            cp(T.ofu[:, KS[h][0]:KS[h][-1] + 1], T.dscan[:, o + n - 1:e:n], ["dscan%d" % h], ["ofu%d" % h])
+    def first(t, h, k, q):
+        o, n = seg(h)[0] + SEG[h] * (k - KS[h][0]), SEG[h]
+        scan(T.ofu[:, END + k - 8 * (n - 1):END + k + 1:8], T.dd[:, o:o + n], T.eqm[:, o:o + n], 0.0, A.mult, A.max,
+             ["ddz%d" % h, "wk%d" % h, "eqm%d" % k], ["ofu%d" % k])
 
-        def enter(_):
-            cp(T["tm%d" % t][:].indirect(T.ofu[:, 0:5]), T.src_m[:], ["ofu0", "ofu1", "src_m"], ["tm%d" % t])
-        return dict(blocks=blocks, pick=pick, equal=equal, first=first, slots=slots, enter=enter)
+    def enter(t, h, b, q):
+        cp(T["tm%d" % t][:].indirect(T.ofu[:, END:END + 5]), T.src_m[:], ["ofu%d" % k for k in range(5)] + ["src_m"], ["tm%d" % t])
 
-    def evac(t, b, q):
+    def again(t, h, b, q):
+        if t:
+            times(q, plane(t, b, 2), plane(t, b, 0), 1.0, [keys("y", t, i)[b] for i in range(2)], ["yc%d.%d" % (t, b)])
+
+    def unpack(t, h, b, q):
+        mm(bank(4 + b), T.eq[:, 128 * b:128 * b + 128], T.esc[:, 128 * b:128 * b + 128], T["lq%d" % t][:], T["lsc%d" % t][:], ["eq%d" % b, "lq%d" % t], ["ps%d" % (4 + b)])
+
+    def evac(t, h, b, q):
         times(q, plane(t, b, 1), bank(4 + b), 64.0 if t else 1.0, [], ["ps%d" % (4 + b), "d%d.%d" % (t, b)])
 
-    def again(t, b, q):
+    def look(t, h, b, q):
+        src, r = T["tm%d" % t][:, 0:TAB].indirect(listed(T["lw%d" % t], h)), ["tm%d" % t, "lw%d.%d" % (t, h)]
+        if b == 0:
+            ts(part(T.al, h, cut=WCUT), src, 0.0, A0, A.is_gt, A.max, r, ["al%d" % h])
+        elif b == 1:
+            act(part(T.be, h, cut=WCUT), src, r, ["be%d" % h], func=F.Identity, scale=-TINY, bias=B1)
+        else:
+            act(part(T.tf, h, cut=WCUT), src, r, ["tf%d" % h], func=F.Relu)
+
+    def parse(t, h, b, q):
+        m = WCUT[1]
+        scan(T.st[:, WCUT[h] + 1:WCUT[h + 1] + 1], part(T.al, h, cut=WCUT), part(T.be, h, cut=WCUT), T.st[:, m:m + 1] if h else BASE,
+             A.mult, A.mult, ["al%d" % h, "be%d" % h, "st1"][:2 + h], ["st%d" % (h + 1)])
+
+    def lists(t, h, b, q):
+        k = slice(CUT[h] // 16, CUT[h + 1] // 16)
+        ll, n = T.ssel[:, CUT[h] + 15:CUT[h + 1]:16], lambda *a: ["%s%d" % (x, h) for x in a]
+        if b == 0:
+            scan(part(T.ssel, h), part(T.st, h), part(T.dss, h), 0.0, A.max, A.add, ["dss15", "st0", "st1", "st2"], n("ssel"))
+        elif b == 1:
+            tt(T.x1[:, k], ll, T.cx[:, k], A.subtract, n("ssel") + ["cx"], n("x1"))
+        elif b == 2:
+            ts(T.sh[:, k], ll, CAP - 576.5, float(C), A.is_lt, A.mult, n("ssel"), n("sh"))
+        elif b == 4:
+            tt(T.ix[:, k], ll, T.x1[:, k], A.subtract, n("ssel", "x1"), n("ix"))
+        elif b == 5:
+            tt(T.dts[:, CUT[h] + 15:CUT[h + 1]:16], T.ck[:, k], T.ix[:, k], A.subtract, n("ix") + ["ck", "dts"], n("dts"))
+        elif b == 6:
+            tt(T.lv[:, k], T.sh[:, k], T.cf[:, k], A.add, n("sh") + ["cf"], n("lv"))
+        elif b == 7 and q == "a":
+            act(part(T.t2, h), T.tf[:].indirect(T.ix[:, k]), ["tf0", "tf1"] + n("ix"), n("t2"), func=F.Identity, bias=LIFT)
+        elif b == 7:
+            ts(part(T.t2, h), T.tf[:].indirect(T.ix[:, k]), LIFT, None, A.add, None, ["tf0", "tf1"] + n("ix"), n("t2"))
+        elif b == 8:
+            scan(part(T.tsel, h), part(T.t2, h), part(T.dts, h), 0.0, A.max, A.add, n("dts", "t2"), n("tsel"))
+        else:
+            tt((T.ho if t else T.hh)[:, k], T.tsel[:, CUT[h] + 15:CUT[h + 1]:16], T.lv[:, k], A.max, n("tsel", "lv"), n("ho"))
+
+    def spread(t, h, b, q):
+        lo, hi = CUT[h] // 16, CUT[h + 1] // 16
+        if t == 0:
+            ts(T.gl[:, 20 * b + lo:20 * b + hi], T.hh[:, lo:hi], 4.0, float(b), A.mult, A.add, ["ho%d" % h], ["gl%d.%d" % (h, b)])
+
+    def gather(t, h, b, q):
+        lo, hi, out = CUT[h] // 16, CUT[h + 1] // 16, part(T["gt%d" % t], h, 4, b)
+        src = lambda i: [keys("y", t, 0)[i], keys("y", t, 1)[i], "d%d.%d" % (t, i), "yc%d.%d" % (t, i)]
         if t:
-            times(q, plane(t, b, 2), plane(t, b, 0), 1.0, [keys("y", t, h)[b] for h in range(2)], ["yc%d.%d" % (t, b)])
+            times(q, out, T["win%d" % t][:, 3 * C * b:3 * C * (b + 1)].indirect(T.ho[:, lo:hi]), 2.0 ** -6, src(b) + ["ho%d" % h], [keys("g", t, h)[b]])
+        else:
+            times(q, out, T.win0[:].indirect(T.gl[:, 20 * b + lo:20 * b + hi]), 1.0, sum(map(src, range(4)), ["gl%d.%d" % (h, b)]), [keys("g", t, h)[b]])
+
+    def layer(t, h, b, q):
+        qg, sg = part(T["qg%d" % t], h), part(T["sg%d" % t], h)
+        quant(qg, sg, part(T["gt%d" % t], h, 4), keys("g", t, h), ["qg%d.%d" % (t, h)])
+        for i in range(4):
+            mm(bank(4 * h + i, h), T.wq[:, 128 * i:128 * i + 128], T.wsc[:, 128 * i:128 * i + 128], qg, sg, ["wq", "wsc", "qg%d.%d" % (t, h)], ["ps%d" % (4 * h + i)])
+
+    def lift(t, h, b, q):
+        times(q, part(T.g64, h, 4), part(T["gt%d" % t], h, 4), 64.0, keys("g", t, h), ["g64.%d" % h])
+
+    def add(t, h, b, q):
+        tt(plane(t + 1, b, 0, h), bank(4 * h + b, h), part(T.g64, h, 4, b), A.add, ["g64.%d" % h], ["ps%d" % (4 * h + b), keys("y", t + 1, h)[b]])
+
+    def scale(t, h, b, q):
+        times(q, part(T["xt%d" % (t + 1)], h, 4, b), plane(t + 1, b, 0, h), 2.0 ** -6, [keys("y", t + 1, h)[b]], [keys("x", t + 1, h)[b]])
 
     dma("a", T.ut[:], T.u[:], [], ["ut"])
     for h in range(2):
@@ -320,13 +393,14 @@ def rank_program(g, core, T, topo):
     quant_e(3)
     ts(T.cx[:], T.cf[:], 1.5, None, A.subtract, None, ["cf"], ["cx"])
     act(T.z0[:, 0:514], T.z1[:, 1:515], ["z1"], ["z0"])
-    act(T.dss[:], T.pt[:].indirect(T.jo[:, 0:20]), ["pt", "jo"], ["dss"])
+    act(T.dts[:], T.pt[:].indirect(T.jo[:, 0:20]), ["pt", "jo"], ["dts"])
+    act(T.dss[:], T.dts[:], ["dts"], ["dss"])
+    act(T.dss[:, 15:C:16], T.cf[:], ["cf", "bk"], ["dss", "dss15"], func=F.Identity, bias=T.bk[:, 0:1])
     once = {
         (0, 0): lambda: [ms(T.dd[:, seg(h)[0]:seg(h)[1]:SEG[h]], 0.0, ["ddz%d" % h] + ["dd%d" % k for k in KS[h]]) for h in range(2)],
         (0, 1): lambda: quant_e(0),
         (0, 6): lambda: quant_e(2),
-        (0, 2): lambda: [ms(T.st[:, 0:1], BASE, ["st0"]), cp(T.dts[:], T.dss[:], ["dss"], ["dts"]),
-                         ts(T.dss[:, 15:C:16], T.cf[:], T.bk[:, 0:1], None, A.add, None, ["cf", "bk"], ["dss", "dss15"])],
+        (0, 2): lambda: ms(T.st[:, 0:1], BASE, ["st0"]),
         (0, 3): lambda: ts(T.ck[:], T.cf[:], BASE + 576 - LIFT, T.bk[:, 0:1], A.add, A.add, ["cf", "bk"], ["ck"]),
         (1, 5): lambda: quant(T.vq[:], T.vsc[:], T.vt[:], ["vt"], ["vq"]),
     }
@@ -335,84 +409,16 @@ def rank_program(g, core, T, topo):
         if (t, i) in once:
             once[t, i]()
 
-    for t in range(ROUNDS):
-        lw, tm, gt, qg, sg = [T["%s%d" % (n, t)] for n in ("lw", "tm", "gt", "qg", "sg")]
-        K = lambda n: "%s%d" % (n, t)
-
-        steps = dict(words(t), **table(t))
-        steps.update(gap=lambda i: gap(t, i), again=lambda b: again(t, b, "a"))
-        for x in TABLE.split():
-            steps[x[:-1]](int(x[-1]))
-        if t == 0:
-            dma("s", T.wq[:].bitcast(u8), T.wc[:], ["lw0.1"], ["wq"])
-            dma("s", T.wsc[:], T.ws[:], [], ["wsc"])
-            dma("s", T.vt[:], T.v[:], [], ["vt"])
-        if t + 1 < ROUNDS:
-            fill(t + 1)
-        if t == 1:
-            iota(T.hv[:, 0:2 * C], [[1, 2 * C]], 0, 0, ["hv0"], True)
-            iota(T.hv[:, 2 * C:3 * C], [[1, C]], 0, 0, ["hv1"], True)
-        for b in range(4):
-            mm(bank(4 + b), T.eq[:, 128 * b:128 * b + 128], T.esc[:, 128 * b:128 * b + 128], T[K("lq")][:], T[K("lsc")][:], ["eq%d" % b, K("lq")], ["ps%d" % (4 + b)])
-
-        look = [tm[:, 0:TAB].indirect(listed(lw, h)) for h in range(2)]
-        lk, m = [[K("tm"), "lw%d.%d" % (t, h)] for h in range(2)], WCUT[1]
-        steps = dict(
-            d=lambda h, b, q: evac(t, b, q), n=lambda h, b, q: gap(t, b),
-            b=lambda h, b, q: act(part(T.be, h, cut=WCUT), look[h], lk[h], ["be%d" % h], func=F.Identity, scale=-TINY, bias=B1),
-            a=lambda h, b, q: ts(part(T.al, h, cut=WCUT), look[h], 0.0, A0, A.is_gt, A.max, lk[h], ["al%d" % h]),
-            f=lambda h, b, q: act(part(T.tf, h, cut=WCUT), look[h], lk[h], ["tf%d" % h], func=F.Relu),
-            s=lambda h, b, q: scan(T.st[:, WCUT[h] + 1:WCUT[h + 1] + 1], part(T.al, h, cut=WCUT), part(T.be, h, cut=WCUT), T.st[:, m:m + 1] if h else BASE,
-                                   A.mult, A.mult, ["al%d" % h, "be%d" % h, "st1"][:2 + h], ["st%d" % (h + 1)]),
-            p=lambda h, b, q: scan(part(T.ssel, h, cut=WCUT), part(T.st, h, cut=WCUT), part(T.dss, h, cut=WCUT), 0.0, A.max, A.add,
-                                   ["dss15", "st%d" % h, "st%d" % (h + 1)], ["ssel%d" % h]))
-        ahead, behind = [o.split() for o in PARSE.split("list")]
-        for x in ahead:
-            steps[x[0]](int(x[1]), int(x[2]), x[3])
-        gap(t, 3)
-        ll, sk = T.ssel[:, 15:C:16], ["ssel0", "ssel1"]
-        tt(T.x1[:], ll, T.cx[:], A.subtract, sk + ["cx"], ["x1"])
-        ts(T.sh[:], ll, CAP - 576.5, float(C), A.is_lt, A.mult, sk, ["sh"])
-        tt(T.ix[:], ll, T.x1[:], A.subtract, sk + ["x1"], ["ix"])
-        tt(T.y2[:], ll, T.x1[:], A.subtract, sk + ["x1"], ["y2"])
-        act(T.t2[:, 0:128], T.tf[:].indirect(T.ix[:, 0:8]), ["tf0", "tf1", "ix"], ["t2a"], func=F.Identity, bias=LIFT)
-        for x in behind:
-            steps[x[0]](int(x[1]), int(x[2]), x[3])
-        tt(T.lv[:], T.sh[:], T.cf[:], A.add, ["sh", "cf"], ["lv"])
-        ts(T.t2[:, 128:C], T.tf[:].indirect(T.ix[:, 8:20]), LIFT, None, A.add, None, ["tf0", "tf1", "ix"], ["t2b"])
-        tt(T.dts[:, 15:C:16], T.ck[:], T.y2[:], A.subtract, ["ck", "y2"], ["dts"])
-        scan(T.tsel[:], T.t2[:], T.dts[:], 0.0, A.max, A.add, ["dts", "t2a", "t2b"], ["tsel"])
-        tt(T.ho[:] if t else T.hh[:], T.tsel[:, 15:C:16], T.lv[:], A.max, ["tsel", "lv"], ["ho"])
-        if t == 0:
-            for b in (0, 2, 1, 3):
-                ts(T.gl[:, 20 * b:20 * b + 20], T.hh[:], 4.0, float(b), A.mult, A.add, ["ho"], ["gl%d" % b])
-
-        def gather(h, b, q):
-            lo, hi = CUT[h] // 16, CUT[h + 1] // 16
-            src = lambda i: [keys("y", t, 0)[i], keys("y", t, 1)[i], "d%d.%d" % (t, i), "yc%d.%d" % (t, i)]
-            if t:
-                times(q, part(gt, h, 4, b), T[K("win")][:, 3 * C * b:3 * C * (b + 1)].indirect(T.ho[:, lo:hi]), 2.0 ** -6, src(b) + ["ho"], [keys("g", t, h)[b]])
-            else:
-                times(q, part(gt, h, 4, b), T.win0[:].indirect(T.gl[:, 20 * b + lo:20 * b + hi]), 1.0, sum(map(src, range(4)), ["gl%d" % b]), [keys("g", t, h)[b]])
-
-        def layer(h):
-            quant(part(qg, h), part(sg, h), part(gt, h, 4), keys("g", t, h), ["qg%d.%d" % (t, h)])
-            for b in range(4):
-                mm(bank(4 * h + b, h), T.wq[:, 128 * b:128 * b + 128], T.wsc[:, 128 * b:128 * b + 128], part(qg, h), part(sg, h),
-                   ["wq", "wsc", "qg%d.%d" % (t, h)], ["ps%d" % (4 * h + b)])
-
-        def lift(h, q):
-            times(q, part(T.g64, h, 4), part(gt, h, 4), 64.0, keys("g", t, h), ["g64.%d" % h])
-
-        def add(h, b):
-            tt(plane(t + 1, b, 0, h), bank(4 * h + b, h), part(T.g64, h, 4, b), A.add, ["g64.%d" % h], ["ps%d" % (4 * h + b), keys("y", t + 1, h)[b]])
-
-        def scale(h, b, q):
-            times(q, part(T["xt%d" % (t + 1)], h, 4, b), plane(t + 1, b, 0, h), 2.0 ** -6, [keys("y", t + 1, h)[b]], [keys("x", t + 1, h)[b]])
-        steps = dict(g=gather, s=scale, n=lambda h, b, q: gap(t, b), a=lambda h, b, q: add(h, b), q=lambda h, b, q: layer(h), l=lambda h, b, q: lift(h, q),
-                     x=lambda h, b, q: quant_x(t + 1, h), z=lambda h, b, q: t + 1 < ROUNDS and signs(h))
-        for x in LAYER.split():
-            steps[x[0]](int(x[1]), int(x[2]), x[3])
+    now = dict(u=unpack, d=evac, k=look, p=parse, h=lists, j=spread, g=gather, q=layer, l=lift, a=add, s=scale,
+               x=lambda t, h, b, q: quant_x(t + 1, h), n=lambda t, h, b, q: gap(t, b))
+    ahead = dict(Z=lambda t, h, b, q: t and signs(h), W=wscan, O=both, P=post, B=blocks, I=pick, N=entry, E=equal, F=first, T=enter, Y=again,
+                 G=lambda t, h, b, q: gap(t, b))
+    for t in range(-1, ROUNDS):
+        for x in ORDER.split():
+            if x[0] in now and t >= 0:
+                now[x[0]](t, int(x[1]), int(x[2]), x[3])
+            elif x[0] in ahead and t + 1 < ROUNDS:
+                ahead[x[0]](t + 1, int(x[1]), int(x[2]), x[3])
 
     qx, sx = T["qx%d" % ROUNDS], T["sx%d" % ROUNDS]
     qk = ["qx%d.%d" % (ROUNDS, h) for h in range(2)]
@@ -421,8 +427,8 @@ def rank_program(g, core, T, topo):
         dma("s", part(T.oc, h, 4), part(qx, h).bitcast(u8), [qk[h]], ["oc%d" % h])
     act(part(T.yo, 0), bank(0, 0), [], ["ps0", "yo0"])
     dma("a", part(T.y, 0), part(T.yo, 0), ["yo0"], ["y0"])
-    cp(T.hf[:, 0:C // 2], T.hv[:].indirect(T.ho[:, 0:10]), ["hv0", "hv1", "ho"], ["hf0"])
-    act(T.hf[:, C // 2:C], T.hv[:].indirect(T.ho[:, 10:20]), ["hv0", "hv1", "ho"], ["hf1"])
+    cp(T.hf[:, 0:C // 2], T.hv[:].indirect(T.ho[:, 0:10]), ["hv0", "hv1", "ho0"], ["hf0"])
+    act(T.hf[:, C // 2:C], T.hv[:].indirect(T.ho[:, 10:20]), ["hv0", "hv1", "ho0", "ho1"], ["hf1"])
     cp(part(T.yo, 1), bank(1, 1), [], ["ps1", "yo1"])
     for k in range(4):
         dma("sa"[k // 2], T.osc[4 * k:4 * k + 4, :], sx[32 * k:32 * k + 4, :], qk, ["osc%d" % k])

@@ -1,12 +1,12 @@
+from concourse.bass import DstId, RemoteDMATransfer
 from concourse.mybir import dt, AluOpType as A, ActivationFunctionType as F
 
 C, CAP, ROUNDS, STEP = 320, 96, 3, [1, 2, 1]
 CUT = [0, 192, C]
-WCUT = [0, 176, C]
-ORDER = ("u00p u01p u02p u03p k00v k01a k10v p00v k11a k12a n02v k02a p10v n03v h00v h10v h01v d00a h02v d01a h11v h04v h12v h14v h05v h06v "
-         "h17v h15v h07a h08v h16v h18v h09v d02a h19v j02v j00v j01v j11v d03a g02a j03v g03a g00v g11a g01v j13v j12v j10v g10a "
-         "q00v g13a l00v g12v a00v q10v a01v l10a a02v a03v s01v s02v s00a a10v s03a a11v s10a a12v x00v a13v s12v s11a Z00a s13v x10v Z10a n05v "
-         "Y02a W00v Y01a B00v O00v W10v B10v Y03a I00v P00v O10v G00v I10v E01v E00v P10v N00v N10v E14v E13v E02v F00v F01v F14v Y00a F13v F02v "
+ORDER = ("u01p u02p u00p u03p n02v k00v n03v k01a k10v p00v k11a h00v p10v k02a h01v h02v h10v h04v d11v h11v k12a d01v d02a h05v h14v h07a d00v "
+         "h06v h08v h12v h15v h17a h09v h16v d10v j02v j01v h18v d03a j00v g02a j03v g03a g01v h19v g00v j11v g11a j10v j12v g10a "
+         "q00v j13v l00v g12v a00v g13a l10a q10v a01v a02v s00a a03v s01v a10v s02v s03a a11v a12v s10a x00v a13v s11a Z00a s12v s13v x10v "
+         "Y00v n05v Z10a W00v B00v W10v B10v Y03a I00v P10v I10v Y02a N00a E02v E00v E01v N10a E14v E13v F02v Y01a F01v F00v F14v F13v "
          "G06v T00v G01v")
 END = 640
 KS = [(0, 1, 2), (3, 4)]
@@ -28,7 +28,7 @@ def _scratch():
         for n, w, d in [("xt", 4 * C, BF), ("win", 12 * C, BF), ("qx", C, X4), ("sx", C, U8)]:
             s["%s%d" % (n, t)] = ("sbuf", [128, w], d)
     for t in range(ROUNDS):
-        for n, w, d in [("lq", C, X4), ("lsc", C, U8), ("wd", 32, U16), ("lw", 32, U16), ("tm", WIN, F32),
+        for n, w, d in [("lq", C, X4), ("lsc", C, U8), ("wd", 20, U16), ("we", 20, U16), ("lw", 20, U16), ("tm", WIN, F32),
                         ("gt", 4 * C, BF), ("qg", C, X4), ("sg", C, U8)]:
             s["%s%d" % (n, t)] = ("sbuf", [128, w], d)
     for d, names in [
@@ -36,7 +36,7 @@ def _scratch():
         (X4, "uq 128 up 256 vq 128 wq 512 eq 512"), (U8, "usc 128 ups 256 vsc 128 wsc 512 esc 512"),
         (I32, "i_u 16 i_e 16 i_p 22 e16 16 j22 22"), (U16, "uo 16 jo 22 ofu 648 ho 20 ix 20 gl 80"),
         (H16, "eqm 408 dscan 408 t2 320 tsel 320 dts 320"),
-        (F32, "k16 20 src_m 80 jf 8 j4 4 kp 1 kq 4 bk 1 wc0 1 fw 4 fa 4 tiny 4 pa 16 pc 16 pd 16 pw 16 po 16 pe 16 pf 16 pt 16 m0 16 sl 8 "
+        (F32, "k16 20 src_m 80 jf 8 j4 4 kp 1 bk 1 wc0 1 fw 2 tiny 4 pa 16 pc 16 pd 16 pw 16 po 16 pe 16 pf 16 pt 16 m0 16 sl 8 "
               "cf 20 cx 20 ck 20 cl 20 hv 960 vv 32 wsel 80 al 320 be 320 tf 320 st 324 ssel 320 dss 320 y2 20 sh 20 lv 20 hh 20 hf 320 yo 320"),
     ]:
         w = names.split()
@@ -48,7 +48,7 @@ def _scratch():
 
 SCRATCH = _scratch()
 POOL = ["s%d" % i for i in range(128)]
-SEMAPHORES = POOL + ["sent"] + [n % t for n in ("ac%d", "aw%d_0", "aw%d_1") for t in range(ROUNDS)]
+SEMAPHORES = POOL + ["sent"] + [n % t for n in ("ac%d", "aw%d") for t in range(ROUNDS)]
 
 
 def _sequencer(g, T):
@@ -169,24 +169,31 @@ def rank_program(g, core, T, topo):
         peer = T.cores[rank ^ STEP[t]]
         rid, pid = topo.addr(peer)[0:2]
         need("g", r, [])
-        g.remote_dma(out, src, T.sem[sem], T.sem.sent, pid, rid, topo.mask(core, peer))
+        if isinstance(src, list):
+            g.remote_dma_fused([RemoteDMATransfer(dst_ids=[DstId(rid=rid, pnc=pid)], dma_engine_mask=topo.mask(core, peer), remote_sem=T.sem[sem],
+                                                  srcs=src, dsts=[out], alu_op=2)], local_sem=T.sem.sent)
+        else:
+            g.remote_dma(out, src, T.sem[sem], T.sem.sent, pid, rid, topo.mask(core, peer))
         sent[0] += len(topo.engines(core, peer))
 
     def scales(t):
         send(t, T["lsc%d" % t][:], T["sx%d" % t][:], "ac%d" % t, [])
 
-    def quant_x(t, h):
+    def quant_x(t, h, rows=(0, 1)):
         qx, sx, k = T["qx%d" % t], T["sx%d" % t], "qx%d.%d" % (t, h)
         quant(part(qx, h), part(sx, h), part(tile_x(t), h, 4), keys("x", t, h), [k])
         if t == ROUNDS:
             return
         ne = len(topo.engines(core, T.cores[rank ^ STEP[t]]))
         arrives("lq%d" % t, "ac%d" % t, 3 * ne)
-        arrives("lw%d.%d" % (t, h), "aw%d_%d" % (t, h), ne)
+        arrives("lw%d" % t, "aw%d" % t, ne)
         send(t, part(T["lq%d" % t], h).bitcast(u8), part(qx, h).bitcast(u8), "ac%d" % t, [k])
         if h and t:
             scales(t)
-        for i in range(2):
+        symbols(t, h, rows)
+
+    def symbols(t, h, rows):
+        for i in rows:
             by_x(2 * h + i, T.up[:, 128 * i:128 * i + 128], T.ups[:, 128 * i:128 * i + 128], ["up%d" % i, "ups%d" % i], t, h)
 
     def signs(h):
@@ -203,30 +210,24 @@ def rank_program(g, core, T, topo):
     def fill(t):
         op("g", lambda e: e.affine_select(T["tm%d" % t][:, 0:TAB], T.ones[:, 0:TAB], [[0, TAB]], A.is_equal, NONE, 1, 0), ["ones"], ["tm%d" % t])
 
-    def listed(buf, h):
-        return buf[:, 16 * h:16 * h + (WCUT[h + 1] - WCUT[h]) // 16]
-
     def wscan(t, h, b, q):
         lo, hi = 2 * CUT[h], 2 * CUT[h + 1] + 8 * h
         scan(T.wscan[:, lo:hi], T.dw[:, lo:hi], T.bits[:, lo:hi], T.wscan[:, lo - 1:lo] if h else 0.0, A.mult, A.add,
              ["dw0", "dw1", "bit%d" % (2 * h), "bit%d" % (2 * h + 1), "bitp", "wscan0"][:4 + 2 * h], ["wscan%d" % h])
 
-    def both(t, h, b, q):
-        lo, hi = 2 * WCUT[h], 2 * WCUT[h + 1]
-        tt(listed(T.vv, h), T.wscan[:, lo + 31:hi:32], T.wscan[:, lo + 39:hi + 8:32], A.add, ["wscan0", "wscan%d" % h], ["vv%d" % h])
-
     def post(t, h, b, q):
-        wd, k = listed(T["wd%d" % t], h), "wd%d.%d" % (t, h)
-        ts(wd, listed(T.vv, h), T.fw[:, 0:1], 128.5, A.mult, A.add, ["vv%d" % h, "fw"], [k])
-        send(t, listed(T["lw%d" % t], h), wd, "aw%d_%d" % (t, h), [k])
-        if h and t == 0:
+        wd, k = [T["w%s%d" % (n, t)][:] for n in "de"], ["wd%d.%d" % (t, i) for i in range(2)]
+        for i in range(2):
+            ts(wd[i], T.wscan[:, 31 + 8 * i:2 * C + 8 * i:32], 257 * HOLD, T.fw[:, i:i + 1], A.add, A.mult, ["wscan0", "wscan1", "fw%d" % i], [k[i]])
+        send(t, T["lw%d" % t][:], wd, "aw%d" % t, k)
+        if t == 0:
             scales(0)
-            dma("s", T.wq[:].bitcast(u8), T.wc[:], ["lw0.1"], ["wq"])
+            dma("s", T.wq[:].bitcast(u8), T.wc[:], ["lw0"], ["wq"])
             dma("s", T.wsc[:], T.ws[:], [], ["wsc"])
             dma("s", T.vt[:], T.v[:], [], ["vt"])
-        if h and t + 1 < ROUNDS:
+        if t + 1 < ROUNDS:
             fill(t + 1)
-        if h and t == 1:
+        if t == 1:
             iota(T.hv[:, 0:2 * C], [[1, 2 * C]], 0, 0, ["hv0"], True)
             iota(T.hv[:, 2 * C:3 * C], [[1, C]], 0, 0, ["hv1"], True)
 
@@ -240,7 +241,11 @@ def rank_program(g, core, T, topo):
 
     def entry(t, h, b, q):
         (o, e), lo, hi = seg(h), CUT[h] // 4, CUT[h + 1] // 4
-        ts(T.eqm[:, o + hi:e:SEG[h]], T.wsel[:, lo + 15:hi:16], 0.5, T.wc0[:, 0:1], A.mult, A.add, ["wsel%d" % h, "wc0"], ["wk%d" % h])
+        out, src, r = T.eqm[:, o + hi:e:SEG[h]], T.wsel[:, lo + 15:hi:16], ["wsel%d" % h, "wc0"]
+        if t and q == "a":
+            act(out, src, r, ["wk%d" % h], func=F.Identity, scale=0.5, bias=T.wc0[:, 0:1])
+        else:
+            ts(out, src, 0.5, T.wc0[:, 0:1], A.mult, A.add, r, ["wk%d" % h])
 
     def equal(t, h, k, q):
         o, hi = seg(h)[0] + SEG[h] * (k - KS[h][0]), CUT[h + 1] // 4
@@ -250,7 +255,7 @@ def rank_program(g, core, T, topo):
     def first(t, h, k, q):
         o, n = seg(h)[0] + SEG[h] * (k - KS[h][0]), SEG[h]
         scan(T.ofu[:, END + k - 8 * (n - 1):END + k + 1:8], T.dd[:, o:o + n], T.eqm[:, o:o + n], 0.0, A.mult, A.max,
-             ["ddz%d" % h, "wk%d" % h, "eqm%d" % k], ["ofu%d" % k])
+             ["dd%d" % k, "wk%d" % h, "eqm%d" % k], ["ofu%d" % k])
 
     def enter(t, h, b, q):
         cp(T["tm%d" % t][:].indirect(T.ofu[:, END:END + 5]), T.src_m[:], ["ofu%d" % k for k in range(5)] + ["src_m"], ["tm%d" % t])
@@ -263,27 +268,31 @@ def rank_program(g, core, T, topo):
         mm(bank(4 + b), T.eq[:, 128 * b:128 * b + 128], T.esc[:, 128 * b:128 * b + 128], T["lq%d" % t][:], T["lsc%d" % t][:], ["eq%d" % b, "lq%d" % t], ["ps%d" % (4 + b)])
 
     def evac(t, h, b, q):
-        times(q, plane(t, b, 1), bank(4 + b), 64.0 if t else 1.0, [], ["ps%d" % (4 + b), "d%d.%d" % (t, b)])
+        k, c, o = keys("d", t, 0)[b], 64.0 if t else 1.0, 512 * (4 + b)
+        if q == "a":
+            times(q, plane(t, b, 1), bank(4 + b), c, [], ["ps%d" % (4 + b), k, keys("d", t, 1)[b]])
+        else:
+            times(q, plane(t, b, 1, h), T.ps[:, o + CUT[h]:o + CUT[h + 1]], c, ["ps%d" % (4 + b)], [keys("d", t, h)[b]])
 
     def look(t, h, b, q):
-        src, r = T["tm%d" % t][:, 0:TAB].indirect(listed(T["lw%d" % t], h)), ["tm%d" % t, "lw%d.%d" % (t, h)]
+        src, r = T["tm%d" % t][:, 0:TAB].indirect(T["lw%d" % t][:, CUT[h] // 16:CUT[h + 1] // 16]), ["tm%d" % t, "lw%d" % t]
         if b == 0:
-            ts(part(T.al, h, cut=WCUT), src, 0.0, A0, A.is_gt, A.max, r, ["al%d" % h])
+            ts(part(T.al, h), src, 0.0, A0, A.is_gt, A.max, r, ["al%d" % h])
         elif b == 1:
-            act(part(T.be, h, cut=WCUT), src, r, ["be%d" % h], func=F.Identity, scale=-TINY, bias=B1)
+            act(part(T.be, h), src, r, ["be%d" % h], func=F.Identity, scale=-TINY, bias=B1)
         else:
-            act(part(T.tf, h, cut=WCUT), src, r, ["tf%d" % h], func=F.Relu)
+            act(part(T.tf, h), src, r, ["tf%d" % h], func=F.Relu)
 
     def parse(t, h, b, q):
-        m = WCUT[1]
-        scan(T.st[:, WCUT[h] + 1:WCUT[h + 1] + 1], part(T.al, h, cut=WCUT), part(T.be, h, cut=WCUT), T.st[:, m:m + 1] if h else BASE,
+        m = CUT[1]
+        scan(T.st[:, CUT[h] + 1:CUT[h + 1] + 1], part(T.al, h), part(T.be, h), T.st[:, m:m + 1] if h else BASE,
              A.mult, A.mult, ["al%d" % h, "be%d" % h, "st1"][:2 + h], ["st%d" % (h + 1)])
 
     def lists(t, h, b, q):
         k = slice(CUT[h] // 16, CUT[h + 1] // 16)
         ll, n = T.ssel[:, CUT[h] + 15:CUT[h + 1]:16], lambda *a: ["%s%d" % (x, h) for x in a]
         if b == 0:
-            scan(part(T.ssel, h), part(T.st, h), part(T.dss, h), 0.0, A.max, A.add, ["dss15", "st0", "st1", "st2"], n("ssel"))
+            scan(part(T.ssel, h), part(T.st, h), part(T.dss, h), 0.0, A.max, A.add, ["dss15", "st%d" % h, "st%d" % (h + 1)], n("ssel"))
         elif b == 1:
             tt(T.x1[:, k], ll, T.cx[:, k], A.subtract, n("ssel") + ["cx"], n("x1"))
         elif b == 2:
@@ -295,9 +304,9 @@ def rank_program(g, core, T, topo):
         elif b == 6:
             tt(T.lv[:, k], T.sh[:, k], T.cf[:, k], A.add, n("sh") + ["cf"], n("lv"))
         elif b == 7 and q == "a":
-            act(part(T.t2, h), T.tf[:].indirect(T.ix[:, k]), ["tf0", "tf1"] + n("ix"), n("t2"), func=F.Identity, bias=LIFT)
+            act(part(T.t2, h), T.tf[:, 0:CUT[h + 1]].indirect(T.ix[:, k]), ["tf0"] + n("tf", "ix"), n("t2"), func=F.Identity, bias=LIFT)
         elif b == 7:
-            ts(part(T.t2, h), T.tf[:].indirect(T.ix[:, k]), LIFT, None, A.add, None, ["tf0", "tf1"] + n("ix"), n("t2"))
+            ts(part(T.t2, h), T.tf[:, 0:CUT[h + 1]].indirect(T.ix[:, k]), LIFT, None, A.add, None, ["tf0"] + n("tf", "ix"), n("t2"))
         elif b == 8:
             scan(part(T.tsel, h), part(T.t2, h), part(T.dts, h), 0.0, A.max, A.add, n("dts", "t2"), n("tsel"))
         else:
@@ -310,7 +319,7 @@ def rank_program(g, core, T, topo):
 
     def gather(t, h, b, q):
         lo, hi, out = CUT[h] // 16, CUT[h + 1] // 16, part(T["gt%d" % t], h, 4, b)
-        src = lambda i: [keys("y", t, 0)[i], keys("y", t, 1)[i], "d%d.%d" % (t, i), "yc%d.%d" % (t, i)]
+        src = lambda i: [keys(n, t, j)[i] for n in "yd" for j in range(2)] + ["yc%d.%d" % (t, i)]
         if t:
             times(q, out, T["win%d" % t][:, 3 * C * b:3 * C * (b + 1)].indirect(T.ho[:, lo:hi]), 2.0 ** -6, src(b) + ["ho%d" % h], [keys("g", t, h)[b]])
         else:
@@ -331,7 +340,7 @@ def rank_program(g, core, T, topo):
     def scale(t, h, b, q):
         times(q, part(T["xt%d" % (t + 1)], h, 4, b), plane(t + 1, b, 0, h), 2.0 ** -6, [keys("y", t + 1, h)[b]], [keys("x", t + 1, h)[b]])
 
-    dma("a", T.ut[:], T.u[:], [], ["ut"])
+    dma("s", T.ut[:], T.u[:], [], ["ut"])
     for h in range(2):
         dma("s", part(T.win0, h, 4), part(T.x, h, 4), [], keys("x", 0, h) + keys("y", 0, h))
     dma("s", T.win0[:, 8 * C:12 * C], T.x[:], [], ["yc0.%d" % b for b in range(4)])
@@ -360,7 +369,6 @@ def rank_program(g, core, T, topo):
     tt(T.pt[:], T.pe[:], T.pf[:], A.add, ["pe", "pf"], ["pt"])
     cp(T.uo[:], T.i_u[:], ["i_u"], ["uo"])
     act(T.dw[:, 0:672:2], T.pw[:].indirect(T.jo[:, 0:21]), ["pw", "jo"], ["dw0"])
-    act(T.fa[:], T.jf[:, 0:4], ["jf"], ["fa"], func=F.Square, bias=-7.5)
     ms(T.db[:], 2.0, ["db"])
     ms(T.dd[:], 1.0, ["dd"])
     ts(T.m0[:], T.e16[:], 0.0, None, A.is_equal, None, ["e16"], ["m0"])
@@ -373,20 +381,22 @@ def rank_program(g, core, T, topo):
         o = T.uo[:, 8 * i:8 * i + 8]
         act(T.ups[:, 128 * i:128 * i + 128], T.usc[:].indirect(o), ["uq", "uo"], ["ups%d" % i])
         cp(T.up[:, 128 * i:128 * i + 128].bitcast(u32), T.uq[:].bitcast(u32).indirect(o), ["uq", "uo"], ["up%d" % i])
+        if i == 0:
+            quant_x(0, 0, [0])
+    symbols(0, 0, [1])
     act(T.dsel[:], T.pt[:].indirect(T.jo[:, 0:5]), ["pt", "jo"], ["dsel"])
-    quant_x(0, 0)
     signs(0)
-    ts(T.fw[:], T.fa[:], 16.0, 1.0, A.is_gt, A.add, ["fa"], ["fw"])
-    ts(T.kp[:], T.pt[:, 15:16], LIFT, LIFT, A.add, A.min, ["pt"], ["kp"])
-    quant_e(1)
     quant_x(0, 1)
     signs(1)
+    ts(T.fw[:, 0:1], T.jf[:, 0:1], 7.5, 0.5 / HOLD, A.is_lt, A.mult, ["jf"], ["fw0"])
+    ts(T.kp[:], T.pt[:, 15:16], LIFT, LIFT, A.add, A.min, ["pt"], ["kp"])
+    quant_e(1)
     for k in range(5):
         h = int(k in KS[1])
         o = seg(h)[0] + SEG[h] * (k - KS[h][0]) + 16 * k
         act(T.dd[:, o:o + 16], T.m0[:], ["m0", "sl", "dd"], ["dd%d" % k], func=F.Identity, scale=T.sl[:, k:k + 1], bias=1.0)
     ts(T.bits[:, 640:648], T.jf[:], 12.5, -2.0 ** 20, A.is_gt, A.mult, ["jf"], ["bitp"])
-    ts(T.fw[:], T.fw[:], 0.25 / HOLD, None, A.mult, None, ["fw"], ["fw"])
+    ts(T.fw[:, 1:2], T.jf[:, 0:1], 7.5, 0.5 / HOLD, A.is_gt, A.mult, ["jf"], ["fw1"])
     ts(T.wc0[:], T.kp[:], -0.5, 128.5, A.mult, A.add, ["kp"], ["wc0"])
     ts(T.cf[:], T.k16[:], T.jf[:, 0:1], None, A.add, None, ["k16", "jf"], ["cf"])
     ts(T.bk[:], T.pt[:, 15:16], 0.0, BASE + LIFT + 576, A.max, A.subtract, ["pt"], ["bk"])
@@ -397,7 +407,6 @@ def rank_program(g, core, T, topo):
     act(T.dss[:], T.dts[:], ["dts"], ["dss"])
     act(T.dss[:, 15:C:16], T.cf[:], ["cf", "bk"], ["dss", "dss15"], func=F.Identity, bias=T.bk[:, 0:1])
     once = {
-        (0, 0): lambda: [ms(T.dd[:, seg(h)[0]:seg(h)[1]:SEG[h]], 0.0, ["ddz%d" % h] + ["dd%d" % k for k in KS[h]]) for h in range(2)],
         (0, 1): lambda: quant_e(0),
         (0, 6): lambda: quant_e(2),
         (0, 2): lambda: ms(T.st[:, 0:1], BASE, ["st0"]),
@@ -411,7 +420,7 @@ def rank_program(g, core, T, topo):
 
     now = dict(u=unpack, d=evac, k=look, p=parse, h=lists, j=spread, g=gather, q=layer, l=lift, a=add, s=scale,
                x=lambda t, h, b, q: quant_x(t + 1, h), n=lambda t, h, b, q: gap(t, b))
-    ahead = dict(Z=lambda t, h, b, q: t and signs(h), W=wscan, O=both, P=post, B=blocks, I=pick, N=entry, E=equal, F=first, T=enter, Y=again,
+    ahead = dict(Z=lambda t, h, b, q: t and signs(h), W=wscan, P=post, B=blocks, I=pick, N=entry, E=equal, F=first, T=enter, Y=again,
                  G=lambda t, h, b, q: gap(t, b))
     for t in range(-1, ROUNDS):
         for x in ORDER.split():

from concourse.bass import DstId, RemoteDMATransfer
from concourse.mybir import dt, AluOpType as A, ActivationFunctionType as F

C, CAP, ROUNDS, STEP = 320, 96, 3, [1, 2, 1]
CUT = [0, 192, C]
ORDER = ("u01p u02p u00p u03p n02v k00v n03v k01a k10v p00v k11a h00v p10v k02a h01v h02v h10v h04v d11v h11v k12a d01v d02a h05v h14v h07a d00v "
         "h06v h08v h12v h15v h17a h09v h16v d10v j02v j01v h18v d03a j00v g02a j03v g03a g01v h19v g00v j11v g11a j10v j12v g10a "
         "q00v j13v l00v g12v a00v g13a l10a q10v a01v a02v s00a a03v s01v a10v s02v s03a a11v a12v s10a x00v a13v s11a Z00a s12v s13v x10v "
         "Y00v n05v Z10a W00v B00v W10v B10v Y03a I00v P10v I10v Y02a N00a E02v E00v E01v N10a E14v E13v F02v Y01a F01v F00v F14v F13v "
         "G06v T00v G01v")
END = 640
KS = [(0, 1, 2), (3, 4)]
SEG = [CUT[1] // 4 + 1, C // 4 + 1]
TAB, WIN = 260, 584
HOLD, LIFT = 1024.0, 1024.0
BASE = 14212656.0
A0 = 0.75 + 9 * 2.0 ** -24
B0 = (11184811 - 9) * 2.0 ** -23
B1 = 1.0 - 2.0 ** -24
TINY = 2.0 ** -40
NONE = (B1 - B0) / TINY
X4, U8, U16, I32, F32, BF, H16 = "float8_e4m3fn_x4", "uint8", "uint16", "int32", "float32", "bfloat16", "float16"


def _scratch():
    s = {}
    for t in range(ROUNDS + 1):
        for n, w, d in [("xt", 4 * C, BF), ("win", 12 * C, BF), ("qx", C, X4), ("sx", C, U8)]:
            s["%s%d" % (n, t)] = ("sbuf", [128, w], d)
    for t in range(ROUNDS):
        for n, w, d in [("lq", C, X4), ("lsc", C, U8), ("wd", 20, U16), ("we", 20, U16), ("lw", 20, U16), ("tm", WIN, F32),
                        ("gt", 4 * C, BF), ("qg", C, X4), ("sg", C, U8)]:
            s["%s%d" % (n, t)] = ("sbuf", [128, w], d)
    for d, names in [
        (BF, "ut 512 vt 512 ones 516 z0 516 z1 516 dw 672 db 640 dsel 80 dd 408 bits 648 wscan 648 bscan 640 x1 20 g64 1280"),
        (X4, "uq 128 up 256 vq 128 wq 512 eq 512"), (U8, "usc 128 ups 256 vsc 128 wsc 512 esc 512"),
        (I32, "i_u 16 i_e 16 i_p 22 e16 16 j22 22"), (U16, "uo 16 jo 22 ofu 648 ho 20 ix 20 gl 80"),
        (H16, "eqm 408 dscan 408 t2 320 tsel 320 dts 320"),
        (F32, "k16 20 src_m 80 jf 8 j4 4 kp 1 bk 1 wc0 1 fw 2 tiny 4 pa 16 pc 16 pd 16 pw 16 po 16 pe 16 pf 16 pt 16 m0 16 sl 8 "
              "cf 20 cx 20 ck 20 cl 20 hv 960 vv 32 wsel 80 al 320 be 320 tf 320 st 324 ssel 320 dss 320 y2 20 sh 20 lv 20 hh 20 hf 320 yo 320"),
    ]:
        w = names.split()
        for i in range(0, len(w), 2):
            s[w[i]] = ("sbuf", [128, int(w[i + 1])], d)
    s["ps"] = ("psum", [128, 4096], F32)
    return s


SCRATCH = _scratch()
POOL = ["s%d" % i for i in range(128)]
SEMAPHORES = POOL + ["sent"] + [n % t for n in ("ac%d", "aw%d") for t in range(ROUNDS)]


def _sequencer(g, T):
    Q = {"g": g, "v": g.vector, "a": g.scalar, "p": g.tensor, "s": g.sync}
    know = {q: {} for q in Q}
    count, waited, writer, readers = {}, {}, {}, {}

    def wait(q, tok):
        sem, val, clock = tok
        if know[q].get(sem, 0) >= val:
            return
        Q[q].wait_ge(T.sem[sem], val)
        waited[sem] = max(waited.get(sem, 0), val)
        for k, x in list(clock.items()) + [(sem, val)]:
            if know[q].get(k, 0) < x:
                know[q][k] = x

    def need(q, r, w):
        deps = [writer[k] for k in r + w if k in writer]
        for k in w:
            deps += readers.get(k, [])
        for tok in sorted(deps, key=lambda x: -sum(x[2].values())):
            wait(q, tok)

    def op(q, fn, r=(), w=(), n=1):
        r, w = list(r), list(w)
        need(q, r, w)
        sem = [s for s in POOL if know[q].get(s, 0) == count.get(s, 0)][0]
        fn(Q[q]).then_inc(T.sem[sem], n)
        count[sem] = count.get(sem, 0) + n
        tok = (sem, count[sem], dict(know[q]))
        for k in r:
            readers.setdefault(k, []).append(tok)
        for k in w:
            writer[k], readers[k] = tok, []
        return tok

    def arrives(key, sem, val):
        writer[key] = (sem, val, {})

    def finish(q):
        for s in POOL:
            if count.get(s, 0) > waited.get(s, 0):
                wait(q, (s, count[s], {}))
    return op, need, arrives, finish


def rank_program(g, core, T, topo):
    rank = T.rank_of(core)
    if rank is None:
        return
    op, need, arrives, finish = _sequencer(g, T)
    u8, u32 = dt.uint8, dt.uint32

    def ts(out, in0, s1, s2, o0, o1, r, w):
        if o1 is None:
            return op("v", lambda e: e.tensor_scalar(out, in0, s1, None, o0), r, w)
        return op("v", lambda e: e.tensor_scalar(out, in0, s1, s2, o0, o1), r, w)

    def tt(out, a, b, o, r, w):
        return op("v", lambda e: e.tensor_tensor(out, a, b, o), r, w)

    def cp(out, a, r, w):
        return op("v", lambda e: e.tensor_copy(out, a), r, w)

    def ms(out, c, w):
        return op("v", lambda e: e.memset(out, c), (), w)

    def scan(out, d0, d1, init, o0, o1, r, w):
        return op("v", lambda e: e.tensor_tensor_scan(out, d0, d1, init, o0, o1), r, w)

    def act(out, a, r, w, func=F.Copy, **kw):
        return op("a", lambda e: e.activation(out, a, func, **kw), r, w)

    def times(q, out, a, c, r, w):
        return act(out, a, r, w, scale=c) if q == "a" else ts(out, a, c, None, A.mult, None, r, w)

    def quant(q, s, a, r, w):
        return op("v", lambda e: e.quantize_mx(q, s, a), r, w)

    def mm(out, lq, ls, rq, rs, r, w):
        return op("p", lambda e: e.matmul_mx(out, lq, ls, rq, rs, True, True), r, w)

    def dma(q, out, a, r, w):
        return op(q, lambda e: e.dma_start(out, a), r, w, 16)

    def iota(out, pat, base, cm, w, flt=False):
        if flt:
            return op("g", lambda e: e.iota(out, pat, base, cm, allow_small_or_imprecise_dtypes=True), (), w)
        return op("g", lambda e: e.iota(out, pat, base, cm), (), w)

    def bank(k, h=None):
        return T.ps[:, 512 * k:512 * k + (C if h is None else CUT[h + 1] - CUT[h])]

    def part(buf, h, w=1, b=None, cut=CUT):
        return buf[:, w * cut[h]:w * cut[h + 1]] if b is None else buf[:, w * cut[h] + b:w * cut[h + 1]:w]

    def plane(t, b, third, h=None):
        lo, hi = (0, C) if h is None else CUT[h:h + 2]
        if t == 0:
            return T.win0[:, 4 * (C * third + lo) + b:4 * (C * third + hi):4]
        o = 3 * C * b + C * third
        return T["win%d" % t][:, o + lo:o + hi]

    def tile_x(t):
        return T["xt%d" % t] if t else T.win0

    def keys(n, t, h):
        return ["%s%d.%d.%d" % (n, t, h, b) for b in range(4)]

    def seg(h):
        o = h * len(KS[0]) * SEG[0]
        return o, o + len(KS[h]) * SEG[h]

    sent = [0]

    def send(t, out, src, sem, r):
        peer = T.cores[rank ^ STEP[t]]
        rid, pid = topo.addr(peer)[0:2]
        need("g", r, [])
        if isinstance(src, list):
            g.remote_dma_fused([RemoteDMATransfer(dst_ids=[DstId(rid=rid, pnc=pid)], dma_engine_mask=topo.mask(core, peer), remote_sem=T.sem[sem],
                                                  srcs=src, dsts=[out], alu_op=2)], local_sem=T.sem.sent)
        else:
            g.remote_dma(out, src, T.sem[sem], T.sem.sent, pid, rid, topo.mask(core, peer))
        sent[0] += len(topo.engines(core, peer))

    def scales(t):
        send(t, T["lsc%d" % t][:], T["sx%d" % t][:], "ac%d" % t, [])

    def quant_x(t, h, rows=(0, 1)):
        qx, sx, k = T["qx%d" % t], T["sx%d" % t], "qx%d.%d" % (t, h)
        quant(part(qx, h), part(sx, h), part(tile_x(t), h, 4), keys("x", t, h), [k])
        if t == ROUNDS:
            return
        ne = len(topo.engines(core, T.cores[rank ^ STEP[t]]))
        arrives("lq%d" % t, "ac%d" % t, 3 * ne)
        arrives("lw%d" % t, "aw%d" % t, ne)
        send(t, part(T["lq%d" % t], h).bitcast(u8), part(qx, h).bitcast(u8), "ac%d" % t, [k])
        if h and t:
            scales(t)
        symbols(t, h, rows)

    def symbols(t, h, rows):
        for i in rows:
            by_x(2 * h + i, T.up[:, 128 * i:128 * i + 128], T.ups[:, 128 * i:128 * i + 128], ["up%d" % i, "ups%d" % i], t, h)

    def signs(h):
        for i in range(2):
            act(part(T.bits, h, 2, i), bank(2 * h + i, h), ["tiny"], ["ps%d" % (2 * h + i), "bit%d" % (2 * h + i)], func=F.Sign, bias=T.tiny[:, 0:1])

    def quant_e(b):
        o = 2 - b // 2 * 2
        quant(T.eq[:, 128 * b:128 * b + 128], T.esc[:, 128 * b:128 * b + 128], T["z%d" % (b % 2)][:, o:o + 512], ["z%d" % (b % 2)], ["eq%d" % b])

    def by_x(k, q, sc, ks, t, h):
        mm(bank(k, h), q, sc, part(T["qx%d" % t], h), part(T["sx%d" % t], h), ks + ["qx%d.%d" % (t, h)], ["ps%d" % k])

    def fill(t):
        op("g", lambda e: e.affine_select(T["tm%d" % t][:, 0:TAB], T.ones[:, 0:TAB], [[0, TAB]], A.is_equal, NONE, 1, 0), ["ones"], ["tm%d" % t])

    def wscan(t, h, b, q):
        lo, hi = 2 * CUT[h], 2 * CUT[h + 1] + 8 * h
        scan(T.wscan[:, lo:hi], T.dw[:, lo:hi], T.bits[:, lo:hi], T.wscan[:, lo - 1:lo] if h else 0.0, A.mult, A.add,
             ["dw0", "dw1", "bit%d" % (2 * h), "bit%d" % (2 * h + 1), "bitp", "wscan0"][:4 + 2 * h], ["wscan%d" % h])

    def post(t, h, b, q):
        wd, k = [T["w%s%d" % (n, t)][:] for n in "de"], ["wd%d.%d" % (t, i) for i in range(2)]
        for i in range(2):
            ts(wd[i], T.wscan[:, 31 + 8 * i:2 * C + 8 * i:32], 257 * HOLD, T.fw[:, i:i + 1], A.add, A.mult, ["wscan0", "wscan1", "fw%d" % i], [k[i]])
        send(t, T["lw%d" % t][:], wd, "aw%d" % t, k)
        if t == 0:
            scales(0)
            dma("s", T.wq[:].bitcast(u8), T.wc[:], ["lw0"], ["wq"])
            dma("s", T.wsc[:], T.ws[:], [], ["wsc"])
            dma("s", T.vt[:], T.v[:], [], ["vt"])
        if t + 1 < ROUNDS:
            fill(t + 1)
        if t == 1:
            iota(T.hv[:, 0:2 * C], [[1, 2 * C]], 0, 0, ["hv0"], True)
            iota(T.hv[:, 2 * C:3 * C], [[1, C]], 0, 0, ["hv1"], True)

    def blocks(t, h, b, q):
        scan(part(T.bscan, h, 2), part(T.db, h, 2), part(T.bits, h, 2), 0.0, A.mult, A.add,
             ["db", "bit%d" % (2 * h), "bit%d" % (2 * h + 1)], ["bscan%d" % h])

    def pick(t, h, b, q):
        lo, hi = CUT[h] // 4, CUT[h + 1] // 4
        scan(T.wsel[:, lo:hi], T.bscan[:, 8 * lo + 7:8 * hi:8], T.dsel[:, lo:hi], -4 * LIFT, A.max, A.add, ["dsel", "bscan%d" % h], ["wsel%d" % h])

    def entry(t, h, b, q):
        (o, e), lo, hi = seg(h), CUT[h] // 4, CUT[h + 1] // 4
        out, src, r = T.eqm[:, o + hi:e:SEG[h]], T.wsel[:, lo + 15:hi:16], ["wsel%d" % h, "wc0"]
        if t and q == "a":
            act(out, src, r, ["wk%d" % h], func=F.Identity, scale=0.5, bias=T.wc0[:, 0:1])
        else:
            ts(out, src, 0.5, T.wc0[:, 0:1], A.mult, A.add, r, ["wk%d" % h])

    def equal(t, h, k, q):
        o, hi = seg(h)[0] + SEG[h] * (k - KS[h][0]), CUT[h + 1] // 4
        ts(T.eqm[:, o:o + hi], T.bscan[:, 7:8 * hi:8], T.kp[:, 0:1], T.wsel[:, 16 * k + 15:16 * k + 16],
           A.add, A.is_equal, ["bscan0", "bscan%d" % h, "wsel%d" % h, "kp"], ["eqm%d" % k])

    def first(t, h, k, q):
        o, n = seg(h)[0] + SEG[h] * (k - KS[h][0]), SEG[h]
        scan(T.ofu[:, END + k - 8 * (n - 1):END + k + 1:8], T.dd[:, o:o + n], T.eqm[:, o:o + n], 0.0, A.mult, A.max,
             ["dd%d" % k, "wk%d" % h, "eqm%d" % k], ["ofu%d" % k])

    def enter(t, h, b, q):
        cp(T["tm%d" % t][:].indirect(T.ofu[:, END:END + 5]), T.src_m[:], ["ofu%d" % k for k in range(5)] + ["src_m"], ["tm%d" % t])

    def again(t, h, b, q):
        if t:
            times(q, plane(t, b, 2), plane(t, b, 0), 1.0, [keys("y", t, i)[b] for i in range(2)], ["yc%d.%d" % (t, b)])

    def unpack(t, h, b, q):
        mm(bank(4 + b), T.eq[:, 128 * b:128 * b + 128], T.esc[:, 128 * b:128 * b + 128], T["lq%d" % t][:], T["lsc%d" % t][:], ["eq%d" % b, "lq%d" % t], ["ps%d" % (4 + b)])

    def evac(t, h, b, q):
        k, c, o = keys("d", t, 0)[b], 64.0 if t else 1.0, 512 * (4 + b)
        if q == "a":
            times(q, plane(t, b, 1), bank(4 + b), c, [], ["ps%d" % (4 + b), k, keys("d", t, 1)[b]])
        else:
            times(q, plane(t, b, 1, h), T.ps[:, o + CUT[h]:o + CUT[h + 1]], c, ["ps%d" % (4 + b)], [keys("d", t, h)[b]])

    def look(t, h, b, q):
        src, r = T["tm%d" % t][:, 0:TAB].indirect(T["lw%d" % t][:, CUT[h] // 16:CUT[h + 1] // 16]), ["tm%d" % t, "lw%d" % t]
        if b == 0:
            ts(part(T.al, h), src, 0.0, A0, A.is_gt, A.max, r, ["al%d" % h])
        elif b == 1:
            act(part(T.be, h), src, r, ["be%d" % h], func=F.Identity, scale=-TINY, bias=B1)
        else:
            act(part(T.tf, h), src, r, ["tf%d" % h], func=F.Relu)

    def parse(t, h, b, q):
        m = CUT[1]
        scan(T.st[:, CUT[h] + 1:CUT[h + 1] + 1], part(T.al, h), part(T.be, h), T.st[:, m:m + 1] if h else BASE,
             A.mult, A.mult, ["al%d" % h, "be%d" % h, "st1"][:2 + h], ["st%d" % (h + 1)])

    def lists(t, h, b, q):
        k = slice(CUT[h] // 16, CUT[h + 1] // 16)
        ll, n = T.ssel[:, CUT[h] + 15:CUT[h + 1]:16], lambda *a: ["%s%d" % (x, h) for x in a]
        if b == 0:
            scan(part(T.ssel, h), part(T.st, h), part(T.dss, h), 0.0, A.max, A.add, ["dss15", "st%d" % h, "st%d" % (h + 1)], n("ssel"))
        elif b == 1:
            tt(T.x1[:, k], ll, T.cx[:, k], A.subtract, n("ssel") + ["cx"], n("x1"))
        elif b == 2:
            ts(T.sh[:, k], ll, CAP - 576.5, float(C), A.is_lt, A.mult, n("ssel"), n("sh"))
        elif b == 4:
            tt(T.ix[:, k], ll, T.x1[:, k], A.subtract, n("ssel", "x1"), n("ix"))
        elif b == 5:
            tt(T.dts[:, CUT[h] + 15:CUT[h + 1]:16], T.ck[:, k], T.ix[:, k], A.subtract, n("ix") + ["ck", "dts"], n("dts"))
        elif b == 6:
            tt(T.lv[:, k], T.sh[:, k], T.cf[:, k], A.add, n("sh") + ["cf"], n("lv"))
        elif b == 7 and q == "a":
            act(part(T.t2, h), T.tf[:, 0:CUT[h + 1]].indirect(T.ix[:, k]), ["tf0"] + n("tf", "ix"), n("t2"), func=F.Identity, bias=LIFT)
        elif b == 7:
            ts(part(T.t2, h), T.tf[:, 0:CUT[h + 1]].indirect(T.ix[:, k]), LIFT, None, A.add, None, ["tf0"] + n("tf", "ix"), n("t2"))
        elif b == 8:
            scan(part(T.tsel, h), part(T.t2, h), part(T.dts, h), 0.0, A.max, A.add, n("dts", "t2"), n("tsel"))
        else:
            tt((T.ho if t else T.hh)[:, k], T.tsel[:, CUT[h] + 15:CUT[h + 1]:16], T.lv[:, k], A.max, n("tsel", "lv"), n("ho"))

    def spread(t, h, b, q):
        lo, hi = CUT[h] // 16, CUT[h + 1] // 16
        if t == 0:
            ts(T.gl[:, 20 * b + lo:20 * b + hi], T.hh[:, lo:hi], 4.0, float(b), A.mult, A.add, ["ho%d" % h], ["gl%d.%d" % (h, b)])

    def gather(t, h, b, q):
        lo, hi, out = CUT[h] // 16, CUT[h + 1] // 16, part(T["gt%d" % t], h, 4, b)
        src = lambda i: [keys(n, t, j)[i] for n in "yd" for j in range(2)] + ["yc%d.%d" % (t, i)]
        if t:
            times(q, out, T["win%d" % t][:, 3 * C * b:3 * C * (b + 1)].indirect(T.ho[:, lo:hi]), 2.0 ** -6, src(b) + ["ho%d" % h], [keys("g", t, h)[b]])
        else:
            times(q, out, T.win0[:].indirect(T.gl[:, 20 * b + lo:20 * b + hi]), 1.0, sum(map(src, range(4)), ["gl%d.%d" % (h, b)]), [keys("g", t, h)[b]])

    def layer(t, h, b, q):
        qg, sg = part(T["qg%d" % t], h), part(T["sg%d" % t], h)
        quant(qg, sg, part(T["gt%d" % t], h, 4), keys("g", t, h), ["qg%d.%d" % (t, h)])
        for i in range(4):
            mm(bank(4 * h + i, h), T.wq[:, 128 * i:128 * i + 128], T.wsc[:, 128 * i:128 * i + 128], qg, sg, ["wq", "wsc", "qg%d.%d" % (t, h)], ["ps%d" % (4 * h + i)])

    def lift(t, h, b, q):
        times(q, part(T.g64, h, 4), part(T["gt%d" % t], h, 4), 64.0, keys("g", t, h), ["g64.%d" % h])

    def add(t, h, b, q):
        tt(plane(t + 1, b, 0, h), bank(4 * h + b, h), part(T.g64, h, 4, b), A.add, ["g64.%d" % h], ["ps%d" % (4 * h + b), keys("y", t + 1, h)[b]])

    def scale(t, h, b, q):
        times(q, part(T["xt%d" % (t + 1)], h, 4, b), plane(t + 1, b, 0, h), 2.0 ** -6, [keys("y", t + 1, h)[b]], [keys("x", t + 1, h)[b]])

    dma("s", T.ut[:], T.u[:], [], ["ut"])
    for h in range(2):
        dma("s", part(T.win0, h, 4), part(T.x, h, 4), [], keys("x", 0, h) + keys("y", 0, h))
    dma("s", T.win0[:, 8 * C:12 * C], T.x[:], [], ["yc0.%d" % b for b in range(4)])

    iota(T.i_e[:], [[1, 16]], 128, -1, ["i_e"])
    iota(T.i_p[:], [[0, 22]], 0, 1, ["i_p"])
    iota(T.i_u[:], [[1, 2], [16, 8]], 0, 0, ["i_u"])
    iota(T.k16[:], [[16, 20]], 0, 0, ["k16"], True)
    iota(T.src_m[:], [[4, 80]], 2 * C, 0, ["src_m"], True)
    ms(T.ones[:], 1.0, ["ones"])
    op("g", lambda e: e.affine_select(T.z1[:], T.ones[:], [[-1, 516]], A.is_equal, 0.0, 3, 4), ["ones"], ["z1"])
    act(T.tm0[:, 0:TAB], T.ones[:, 0:TAB], ["ones"], ["tm0"], scale=NONE)
    ts(T.e16[:], T.i_e[:], 15, None, A.bitwise_and, None, ["i_e"], ["e16"])
    ms(T.tiny[:], -2.0 ** -120, ["tiny"])
    ts(T.j22[:], T.i_p[:], 15, None, A.bitwise_and, None, ["i_p"], ["j22"])
    ts(T.po[:], T.e16[:], 3.5, 1.0, A.is_lt, A.add, ["e16"], ["po"])
    ts(T.pa[:], T.e16[:], 4.0, HOLD - 1, A.is_equal, A.mult, ["e16"], ["pa"])
    cp(T.jo[:], T.j22[:], ["j22"], ["jo"])
    ts(T.pc[:], T.e16[:], 0.0, -2.0, A.is_equal, A.mult, ["e16"], ["pc"])
    ts(T.pe[:], T.e16[:], 0.0, LIFT, A.is_equal, A.mult, ["e16"], ["pe"])
    act(T.dw[:, 1:672:2], T.po[:].indirect(T.jo[:, 0:21]), ["po", "jo"], ["dw1"])
    tt(T.pd[:], T.pa[:], T.pc[:], A.add, ["pa", "pc"], ["pd"])
    ts(T.pf[:], T.e16[:], 15.0, -2 * LIFT, A.is_equal, A.mult, ["e16"], ["pf"])
    cp(T.jf[:], T.j22[:, 0:8], ["j22"], ["jf"])
    tt(T.pw[:], T.pd[:], T.po[:], A.add, ["pd", "po"], ["pw"])
    tt(T.pt[:], T.pe[:], T.pf[:], A.add, ["pe", "pf"], ["pt"])
    cp(T.uo[:], T.i_u[:], ["i_u"], ["uo"])
    act(T.dw[:, 0:672:2], T.pw[:].indirect(T.jo[:, 0:21]), ["pw", "jo"], ["dw0"])
    ms(T.db[:], 2.0, ["db"])
    ms(T.dd[:], 1.0, ["dd"])
    ts(T.m0[:], T.e16[:], 0.0, None, A.is_equal, None, ["e16"], ["m0"])
    ms(T.db[:, 0:640:8], 0.0, ["db"])
    ts(T.j4[:], T.jf[:, 0:4], 4.0, TAB - 1.0, A.mult, A.add, ["jf"], ["j4"])

    quant(T.uq[:], T.usc[:], T.ut[:], ["ut"], ["uq"])
    ts(T.sl[:, 0:5], T.k16[:, 0:5], 4.0, T.j4[:, 0:1], A.mult, A.add, ["k16", "j4"], ["sl"])
    for i in range(2):
        o = T.uo[:, 8 * i:8 * i + 8]
        act(T.ups[:, 128 * i:128 * i + 128], T.usc[:].indirect(o), ["uq", "uo"], ["ups%d" % i])
        cp(T.up[:, 128 * i:128 * i + 128].bitcast(u32), T.uq[:].bitcast(u32).indirect(o), ["uq", "uo"], ["up%d" % i])
        if i == 0:
            quant_x(0, 0, [0])
    symbols(0, 0, [1])
    act(T.dsel[:], T.pt[:].indirect(T.jo[:, 0:5]), ["pt", "jo"], ["dsel"])
    signs(0)
    quant_x(0, 1)
    signs(1)
    ts(T.fw[:, 0:1], T.jf[:, 0:1], 7.5, 0.5 / HOLD, A.is_lt, A.mult, ["jf"], ["fw0"])
    ts(T.kp[:], T.pt[:, 15:16], LIFT, LIFT, A.add, A.min, ["pt"], ["kp"])
    quant_e(1)
    for k in range(5):
        h = int(k in KS[1])
        o = seg(h)[0] + SEG[h] * (k - KS[h][0]) + 16 * k
        act(T.dd[:, o:o + 16], T.m0[:], ["m0", "sl", "dd"], ["dd%d" % k], func=F.Identity, scale=T.sl[:, k:k + 1], bias=1.0)
    ts(T.bits[:, 640:648], T.jf[:], 12.5, -2.0 ** 20, A.is_gt, A.mult, ["jf"], ["bitp"])
    ts(T.fw[:, 1:2], T.jf[:, 0:1], 7.5, 0.5 / HOLD, A.is_gt, A.mult, ["jf"], ["fw1"])
    ts(T.wc0[:], T.kp[:], -0.5, 128.5, A.mult, A.add, ["kp"], ["wc0"])
    ts(T.cf[:], T.k16[:], T.jf[:, 0:1], None, A.add, None, ["k16", "jf"], ["cf"])
    ts(T.bk[:], T.pt[:, 15:16], 0.0, BASE + LIFT + 576, A.max, A.subtract, ["pt"], ["bk"])
    quant_e(3)
    ts(T.cx[:], T.cf[:], 1.5, None, A.subtract, None, ["cf"], ["cx"])
    act(T.z0[:, 0:514], T.z1[:, 1:515], ["z1"], ["z0"])
    act(T.dts[:], T.pt[:].indirect(T.jo[:, 0:20]), ["pt", "jo"], ["dts"])
    act(T.dss[:], T.dts[:], ["dts"], ["dss"])
    act(T.dss[:, 15:C:16], T.cf[:], ["cf", "bk"], ["dss", "dss15"], func=F.Identity, bias=T.bk[:, 0:1])
    once = {
        (0, 1): lambda: quant_e(0),
        (0, 6): lambda: quant_e(2),
        (0, 2): lambda: ms(T.st[:, 0:1], BASE, ["st0"]),
        (0, 3): lambda: ts(T.ck[:], T.cf[:], BASE + 576 - LIFT, T.bk[:, 0:1], A.add, A.add, ["cf", "bk"], ["ck"]),
        (1, 5): lambda: quant(T.vq[:], T.vsc[:], T.vt[:], ["vt"], ["vq"]),
    }

    def gap(t, i):
        if (t, i) in once:
            once[t, i]()

    now = dict(u=unpack, d=evac, k=look, p=parse, h=lists, j=spread, g=gather, q=layer, l=lift, a=add, s=scale,
               x=lambda t, h, b, q: quant_x(t + 1, h), n=lambda t, h, b, q: gap(t, b))
    ahead = dict(Z=lambda t, h, b, q: t and signs(h), W=wscan, P=post, B=blocks, I=pick, N=entry, E=equal, F=first, T=enter, Y=again,
                 G=lambda t, h, b, q: gap(t, b))
    for t in range(-1, ROUNDS):
        for x in ORDER.split():
            if x[0] in now and t >= 0:
                now[x[0]](t, int(x[1]), int(x[2]), x[3])
            elif x[0] in ahead and t + 1 < ROUNDS:
                ahead[x[0]](t + 1, int(x[1]), int(x[2]), x[3])

    qx, sx = T["qx%d" % ROUNDS], T["sx%d" % ROUNDS]
    qk = ["qx%d.%d" % (ROUNDS, h) for h in range(2)]
    for h in range(2):
        by_x(h, T.vq[:], T.vsc[:], ["vq"], ROUNDS, h)
        dma("s", part(T.oc, h, 4), part(qx, h).bitcast(u8), [qk[h]], ["oc%d" % h])
    act(part(T.yo, 0), bank(0, 0), [], ["ps0", "yo0"])
    dma("a", part(T.y, 0), part(T.yo, 0), ["yo0"], ["y0"])
    cp(T.hf[:, 0:C // 2], T.hv[:].indirect(T.ho[:, 0:10]), ["hv0", "hv1", "ho0"], ["hf0"])
    act(T.hf[:, C // 2:C], T.hv[:].indirect(T.ho[:, 10:20]), ["hv0", "hv1", "ho0", "ho1"], ["hf1"])
    cp(part(T.yo, 1), bank(1, 1), [], ["ps1", "yo1"])
    for k in range(4):
        dma("sa"[k // 2], T.osc[4 * k:4 * k + 4, :], sx[32 * k:32 * k + 4, :], qk, ["osc%d" % k])
    dma("a", T.ot[:], T.hf[0:128:16, :], ["hf0", "hf1"], ["ot"])
    dma("s", part(T.y, 1), part(T.yo, 1), ["yo1"], ["y1"])
    g.wait_ge(T.sem.sent, sent[0])
    finish("s")
